import numpy as np
import ml_dtypes


def mxq(x, axis, fmt="e4m3"):
    dtype, down = {"e4m3": (ml_dtypes.float8_e4m3fn, 7), "e5m2": (ml_dtypes.float8_e5m2, 14)}[fmt]
    v = np.moveaxis(np.asarray(x, np.float32).astype(ml_dtypes.bfloat16).astype(np.float64), axis, -1)
    blocks = v.reshape(v.shape[:-1] + (-1, 32))
    amax = np.abs(blocks).max(-1, keepdims=True)
    byte = np.maximum(np.where(amax > 0, np.frexp(amax)[1] - 1 + 127, 0) - down, 1)
    scale = np.exp2(byte - 127.0)
    codes = (blocks / scale).astype(np.float32).astype(dtype).astype(np.float64)
    return np.moveaxis((codes * scale).reshape(v.shape), -1, axis)


WIDE = False


def mx_kscale(k):
    if not WIDE:
        return np.ones(k)
    levels = np.array([10, -10, 5, -5, 0])
    if k % 512:
        return np.exp2(np.random.permutation(np.resize(levels, k // 32))).repeat(32)
    a = np.empty((k // 512, 16))
    for p in range(k // 512):
        a[p, :8] = np.random.permutation(np.resize(levels, 8))
        for g in range(8):
            far = levels[np.abs(levels - a[p, g]) >= 10]
            a[p, g + 8] = far[np.random.randint(len(far))]
    return np.exp2(a.ravel()).repeat(32)


BF16 = ml_dtypes.bfloat16


def bf(x):
    return np.asarray(x, np.float32).astype(BF16)


def f64(x):
    return np.asarray(x).astype(np.float64)


E2M1 = np.array([0.0, 0.5, 1.0, 1.5, 2.0, 3.0, 4.0, 6.0, -0.0, -0.5, -1.0, -1.5, -2.0, -3.0, -4.0, -6.0])


def pack_weight(w, fmt):
    k, n = w.shape
    w = f64(bf(w)).reshape(k // 32, 32, n)
    amax = np.abs(w).max(1)
    if fmt == "e4m3":
        byte = np.frexp(amax)[1] - 1 + 127 - 7
    else:
        mant, ex = np.frexp(amax / 6.0)
        byte = np.where(mant > 0.5, ex, ex - 1) + 127
    byte = np.clip(np.where(amax > 0, byte, 1), 1, 254)
    scaled = (w * np.exp2(127.0 - byte)[:, None, :]).reshape(k, n).astype(np.float32)
    by_word = np.ascontiguousarray(scaled.reshape(k // 512, 128, 4, n).transpose(0, 1, 3, 2))
    if fmt == "e4m3":
        words = by_word.astype(ml_dtypes.float8_e4m3fn).view(np.uint8)
    else:
        c = by_word.astype(ml_dtypes.float4_e2m1fn).view(np.uint8) & 0xF
        words = c[..., 0::2] | (c[..., 1::2] << 4)
    return np.ascontiguousarray(words), np.ascontiguousarray(byte.astype(np.uint8).reshape(k // 512, 16, n))


def unpack_weight(words, scales, fmt):
    g, p, n, _ = words.shape
    if fmt == "e4m3":
        vals = np.ascontiguousarray(words).view(ml_dtypes.float8_e4m3fn).astype(np.float64)
    else:
        nib = np.empty((g, p, n, 4), np.uint8)
        nib[..., 0::2] = words & 0xF
        nib[..., 1::2] = words >> 4
        vals = E2M1[nib]
    vals = vals * np.repeat(np.exp2(scales.astype(np.float64) - 127.0), 8, axis=1)[..., None]
    return vals.transpose(0, 1, 3, 2).reshape(g * 512, n)
def pack4(w):
    words, scales = pack_weight(w, "e2m1")
    return words.reshape(words.shape[0], 128, -1), scales


def unpack4(words, scales):
    return unpack_weight(words.reshape(words.shape[0], 128, -1, 2), scales, "e2m1")


M, N, D, F, C = 1024, 2048, 1024, 512, 512

SPREAD = 0.7
JITTER = 0.3


def setup_inputs():
    s = mx_kscale(D)
    u = mx_kscale(F)
    t = mx_kscale(N)
    a_words, a_scales = pack4(np.random.standard_normal((D, M)) * s[:, None])
    b_words, b_scales = pack4(SPREAD * np.random.standard_normal((D, N)) / np.sqrt(D) / s[:, None])
    return {"a_words": a_words, "a_scales": a_scales,
            "b_words": b_words, "b_scales": b_scales,
            "gamma": bf(np.exp(JITTER * np.random.standard_normal(N)) / np.sqrt(N) * t),
            "rho": bf(np.exp(JITTER * np.random.standard_normal(M))),
            "x": bf(np.random.standard_normal((N, F)) * u / t[:, None]),
            "w": bf(np.random.standard_normal((F, C)) / np.sqrt(F) / u[:, None])}


def reference(a_words, a_scales, b_words, b_scales, gamma, rho, x, w):
    gram = unpack4(a_words, a_scales).T @ unpack4(b_words, b_scales)
    weights = np.exp(gram) * f64(gamma)
    v = mxq(f64(x), 1, "e4m3") @ mxq(f64(w), 0, "e4m3")
    avg = mxq(weights, 1, "e4m3") @ mxq(v, 0, "e4m3")
    return avg * f64(rho)[:, None]

@@ -1,0 +1,435 @@
+import math
+from contextlib import ExitStack
+
+import concourse.mybir as mybir
+from concourse.masks import make_identity
+
+M, N, D, F, C = 1024, 2048, 1024, 512, 512
+PLAN = [
+    ("T", 0,),
+    ("rho",),
+    ("arr", 0,),
+    ("G", 0, 0,),
+    ("qx", 0,),
+    ("arr", 1,),
+    ("G", 0, 1,),
+    ("G", 0, 2,),
+    ("G", 0, 3,),
+    ("wi",),
+    ("G", 1, 0,),
+    ("G", 1, 1,),
+    ("il", 0, 0,),
+    ("G", 1, 2,),
+    ("G", 1, 3,),
+    ("arr", 2,),
+    ("T", 1,),
+    ("arr", 3,),
+    ("T", 2,),
+    ("wq",),
+    ("il", 1, 0,),
+    ("il", 0, 1,),
+    ("qx", 1,),
+    ("V", 0, 0,),
+    ("G", 2, 0,),
+    ("il", 1, 1,),
+    ("G", 2, 1,),
+    ("V", 1, 0,),
+    ("V", 1, 1,),
+    ("qe", 1,),
+    ("G", 3, 0,),
+    ("V", 0, 1,),
+    ("G", 2, 2,),
+    ("qx", 2,),
+    ("G", 2, 3,),
+    ("V", 0, 2,),
+    ("V", 1, 2,),
+    ("V", 0, 3,),
+    ("T", 3,),
+    ("G", 4, 0,),
+    ("qe", 0,),
+    ("G", 3, 1,),
+    ("qv", 0,),
+    ("il", 2, 0,),
+    ("G", 3, 2,),
+    ("qx", 3,),
+    ("V", 1, 3,),
+    ("G", 3, 3,),
+    ("V", 2, 0,),
+    ("qv", 1,),
+    ("G", 4, 1,),
+    ("V", 2, 1,),
+    ("V", 3, 0,),
+    ("G", 4, 2,),
+    ("il", 3, 0,),
+    ("G", 4, 3,),
+    ("O", 0, 2, 0,),
+    ("V", 2, 2,),
+    ("O", 0, 3, 0,),
+    ("V", 3, 1,),
+    ("il", 2, 1,),
+    ("G", 5, 0,),
+    ("V", 3, 2,),
+    ("il", 4, 0,),
+    ("O", 0, 2, 1,),
+    ("O", 0, 0, 0,),
+    ("G", 6, 0,),
+    ("V", 2, 3,),
+    ("G", 5, 1,),
+    ("O", 0, 1, 0,),
+    ("il", 3, 1,),
+    ("O", 0, 0, 1,),
+    ("G", 7, 0,),
+    ("G", 5, 2,),
+    ("G", 5, 3,),
+    ("qv", 2,),
+    ("il", 4, 1,),
+    ("qe", 2,),
+    ("V", 3, 3,),
+    ("il", 5, 0,),
+    ("G", 6, 1,),
+    ("il", 5, 1,),
+    ("qv", 3,),
+    ("G", 6, 2,),
+    ("O", 0, 3, 1,),
+    ("G", 6, 3,),
+    ("O", 0, 0, 2,),
+    ("O", 0, 3, 2,),
+    ("O", 0, 1, 1,),
+    ("G", 7, 1,),
+    ("G", 7, 2,),
+    ("G", 7, 3,),
+    ("O", 0, 2, 2,),
+    ("qe", 3,),
+    ("O", 0, 0, 3,),
+    ("qe", 5,),
+    ("qe", 4,),
+    ("O", 0, 3, 3,),
+    ("O", 0, 1, 2,),
+    ("O", 0, 2, 3,),
+    ("il", 6, 0,),
+    ("il", 6, 1,),
+    ("O", 1, 0, 0,),
+    ("F", 0, 0, False,),
+    ("O", 1, 1, 0,),
+    ("O", 0, 1, 3,),
+    ("O", 1, 1, 1,),
+    ("O", 1, 3, 0,),
+    ("il", 7, 0,),
+    ("qe", 6,),
+    ("O", 1, 0, 1,),
+    ("F", 0, 3, False,),
+    ("O", 1, 0, 2,),
+    ("il", 7, 1,),
+    ("O", 1, 2, 0,),
+    ("O", 1, 1, 2,),
+    ("O", 1, 3, 1,),
+    ("qe", 7,),
+    ("O", 1, 0, 3,),
+    ("O", 1, 1, 3,),
+    ("F", 0, 2, False,),
+    ("O", 1, 3, 2,),
+    ("O", 1, 3, 3,),
+    ("F", 0, 1, False,),
+    ("O", 1, 2, 1,),
+    ("F", 1, 0, True,),
+    ("O", 1, 2, 2,),
+    ("F", 1, 1, False,),
+    ("F", 1, 3, False,),
+    ("O", 1, 2, 3,),
+    ("F", 1, 2, True,),
+]
+FLOPS = 2 * (M * N * D + N * F * C + M * N * C)
+
+F32 = mybir.dt.float32
+BF16 = mybir.dt.bfloat16
+I32 = mybir.dt.int32
+U32 = mybir.dt.uint32
+U8 = mybir.dt.uint8
+E4M3 = mybir.dt.float8_e4m3fn_x4
+E2M1 = mybir.dt.float4_e2m1fn_x4
+ALU = mybir.AluOpType
+ACT = mybir.ActivationFunctionType
+
+P = 128
+JG = N // 512
+HALF = 512
+DG = D // 512
+
+
+def tile_balanced_nonlocal_means_s12_kernel(
+    tc, a_words, a_scales, b_words, b_scales, gamma, rho, x, w, out
+):
+    nc = tc.nc
+    with ExitStack() as ctx:
+        keep = ctx.enter_context(tc.tile_pool(name="keep", bufs=1))
+        work = ctx.enter_context(tc.tile_pool(name="work", bufs=3))
+        psum = ctx.enter_context(tc.psum_pool(name="psum", bufs=4))
+        ctx.enter_context(tc.manual_schedule())
+
+        def kept(name, shape, dtype):
+            return keep.tile(shape, dtype, name=name, tag=name, align_bytes=64)
+
+        a_codes = [kept("a_codes%d" % h, [P, DG, 1024], U8) for h in range(2)]
+        a_plane = kept("a_plane", [P, DG, M], U8)
+        b_plane_raw = kept("b_plane_raw", [P, DG, N], U8)
+        b_raw = [kept("b_raw%d" % g, [P, DG, 1024], U8) for g in range(JG)]
+        b_codes = [kept("b_codes%d" % g, [P, DG, 1024], U8) for g in range(JG)]
+        b_plane = [kept("b_plane%d" % g, [P, DG, 512], U8) for g in range(JG)]
+        x_raw = [kept("x_raw%d" % g, [P, 4, F], BF16) for g in range(JG)]
+        w_raw = kept("w_raw", [P, 4, C], BF16)
+        w_grp = kept("w_grp", [P, C, 4], BF16)
+        w_codes = kept("w_codes", [P, C], U32)
+        w_plane = kept("w_plane", [P, C], U8)
+        x_codes = [kept("x_codes%d" % g, [P, 512], U32) for g in range(JG)]
+        x_plane = [kept("x_plane%d" % g, [P, 512], U8) for g in range(JG)]
+        v_codes = [kept("v_codes%d" % g, [P, C], U32) for g in range(JG)]
+        v_plane = [kept("v_plane%d" % g, [P, C], U8) for g in range(JG)]
+        e_codes = [kept("e_codes%d" % s, [P, HALF], U32) for s in range(2 * JG)]
+        e_plane = [kept("e_plane%d" % s, [P, HALF], U8) for s in range(2 * JG)]
+        g_row = kept("g_row", [JG, 512], BF16)
+        vec_rows = kept("vec_rows", [P, 4, P], BF16)
+        rho_rows = kept("rho_rows", [P, P], BF16)
+        id_bf = kept("id_bf", [P, P], BF16)
+        id_f = kept("id_f", [P, P], F32)
+        dummy = kept("dummy", [P, 1], F32)
+        gam = kept("gam", [P, 4, JG], F32)
+        mant = kept("mant", [P, 4, JG], I32)
+        expo = kept("expo", [P, 4, JG], I32)
+        expo_ln = kept("expo_ln", [P, 4, JG], F32)
+        mant_ln = kept("mant_ln", [P, 4, JG], F32)
+        ln_gam = kept("ln_gam", [P, 4, JG], F32)
+        sgn2 = kept("sgn2", [P, JG, 4], F32)
+        sgn = kept("sgn", [P, JG, 4], F32)
+        rho_col = kept("rho_col", [P, M // P], F32)
+
+        def load_b(queue, g):
+            queue.dma_start(
+                out=b_raw[g][:].bitcast(I32),
+                in_=b_words.rearrange("d p n -> p d n")[:, :, g * 1024 : (g + 1) * 1024].bitcast(I32),
+            )
+
+        def load_a(queue, h):
+            queue.dma_start(
+                out=a_codes[h][:].bitcast(I32),
+                in_=a_words.rearrange("d p n -> p d n")[:, :, h * 1024 : (h + 1) * 1024].bitcast(I32),
+            )
+
+        def load_x(g):
+            nc.sync.dma_start(out=x_raw[g][:], in_=x.rearrange("(g m b) f -> g m b f", g=JG, b=4)[g])
+
+        nc.sync.dma_start(out=g_row[:], in_=gamma.rearrange("(g n) -> g n", g=JG))
+        make_identity(nc, id_bf[:])
+        nc.vector.memset(a_plane[:].bitcast(I32), 0)
+        nc.vector.memset(b_plane_raw[:].bitcast(I32), 0)
+        nc.vector.memset(dummy[:], 1.0)
+        nc.vector.memset(vec_rows[:], 0.0)
+        nc.vector.memset(rho_rows[:], 0.0)
+        nc.gpsimd.dma_start(out=rho_rows[0:8, :], in_=rho.rearrange("(i p) -> i p", p=P))
+
+        def load_plane(plane, rows, q):
+            nc.sync.dma_start(
+                out=plane[32 * q : 32 * q + 4, :, :].bitcast(I32),
+                in_=rows[:, 4 * q : 4 * q + 4, :].rearrange("d r n -> r d n").bitcast(I32),
+            )
+
+        for q in range(3):
+            load_plane(a_plane, a_scales, q)
+        load_x(0)
+        load_b(nc.sync, 0)
+        load_a(nc.sync, 0)
+        load_plane(a_plane, a_scales, 3)
+        for q in range(4):
+            load_plane(b_plane_raw, b_scales, q)
+        nc.sync.dma_start(out=w_raw[:], in_=w.rearrange("(p j) c -> p j c", j=4))
+        load_b(nc.sync, 1)
+        load_b(nc.sync, 2)
+        load_x(1)
+        load_b(nc.sync, 3)
+        load_x(2)
+        load_x(3)
+        load_a(nc.sync, 1)
+
+        nc.scalar.activation(out=mant_ln[:, 0, 0:1], in_=dummy[:], func=ACT.Ln)
+        nc.vector.tensor_copy(out=id_f[:], in_=id_bf[:])
+
+        def arrange_b(g):
+            for d in range(DG):
+                nc.vector.tensor_copy(
+                    out=b_codes[g][:, d, :].bitcast(I32).rearrange("p (t s w) -> p t s w", t=4, w=2),
+                    in_=b_raw[g][:, d, :].bitcast(I32).rearrange("p (s t w) -> p t s w", t=4, w=2),
+                )
+            nc.vector.tensor_copy(
+                out=b_plane[g][:].bitcast(I32).rearrange("p d (t s) -> p d t s", t=4),
+                in_=b_plane_raw[:, :, g * 512 : (g + 1) * 512].bitcast(I32).rearrange("p d (s t) -> p d t s", t=4),
+            )
+
+        x_grp = {}
+        e_bf = {}
+        e_grp = {}
+        v_grp = {}
+        o_bank = {}
+
+        def turn_x(g):
+            grp = work.tile([P, 512, 4], BF16, name="x_grp", tag="x_grp", bufs=4, align_bytes=64)
+            x_grp[g] = grp
+            words = grp[:].rearrange("p c j -> p (c j)").bitcast(F32)
+            banks = []
+            for k in range(2):
+                bank = psum.tile([P, 4, P], F32, name="xt", tag="m", bufs=4)
+                banks.append(bank)
+                for bl in range(2):
+                    for u in range(2):
+                        nc.tensor.transpose(
+                            bank[:, 2 * bl + u, :], x_raw[g][:, 2 * k + bl, :].bitcast(F32)[:, u::2], id_f[:]
+                        )
+            for k in range(2):
+                nc.scalar.copy(
+                    out=words.rearrange("p (t s e) -> p t s e", t=4, e=8)[:, :, :, 4 * k : 4 * k + 4],
+                    in_=banks[k][:].rearrange("p e (s t) -> p t s e", t=4),
+                )
+
+        def quant_x(g):
+            nc.vector.quantize_mx(
+                out=x_codes[g][:].bitcast(E4M3), scales=x_plane[g][:], in_=x_grp[g][:].rearrange("p c j -> p (c j)")
+            )
+
+        def weigh(s, t):
+            h, g = divmod(s, JG)
+            bank = psum.tile([P, HALF], F32, name="gram", tag="m", bufs=4)
+            for d in range(DG):
+                nc.tensor.matmul_mx(
+                    out=bank[:],
+                    lhsT=b_codes[g][:, d, 256 * t : 256 * (t + 1)].bitcast(E2M1),
+                    lhsT_scale=b_plane[g][:, d, P * t : P * (t + 1)],
+                    rhs=a_codes[h][:, d, :].bitcast(E2M1),
+                    rhs_scale=a_plane[:, d, HALF * h : HALF * (h + 1)],
+                    start=(d == 0),
+                    stop=(d == DG - 1),
+                )
+            if t == 0:
+                e_bf[s] = work.tile([P, 4, HALF], BF16, name="e_bf", tag="e_bf", bufs=8, align_bytes=64)
+            nc.scalar.activation(out=e_bf[s][:, t, :], in_=bank[:], func=ACT.Exp, bias=ln_gam[:, t, g : g + 1])
+
+        def interleave(s, part):
+            if part == 0:
+                e_grp[s] = work.tile([P, HALF, 4], BF16, name="e_grp", tag="e_grp", bufs=4, align_bytes=64)
+            cols = slice(part * 256, (part + 1) * 256)
+            nc.vector.tensor_copy(
+                out=e_grp[s][:, cols, :].rearrange("p (c i) t -> p c t i", i=4),
+                in_=e_bf[s][:, :, cols].rearrange("p t (c i) -> p c t i", i=4),
+            )
+
+        def quant_e(s):
+            nc.vector.quantize_mx(
+                out=e_codes[s][:].bitcast(E4M3), scales=e_plane[s][:], in_=e_grp[s][:].rearrange("p c t -> p (c t)")
+            )
+
+        def project(g, cq):
+            bank = psum.tile([P, 4, P], F32, name="val", tag="m", bufs=4)
+            cols = slice(P * cq, P * (cq + 1))
+            for t in range(4):
+                nc.tensor.matmul_mx(
+                    out=bank[:, t, :],
+                    lhsT=x_codes[g][:, P * t : P * (t + 1)].bitcast(E4M3),
+                    lhsT_scale=x_plane[g][:, P * t : P * (t + 1)],
+                    rhs=w_codes[:, cols].bitcast(E4M3),
+                    rhs_scale=w_plane[:, cols],
+                    start=True,
+                    stop=True,
+                )
+            if cq == 0:
+                v_grp[g] = work.tile([P, C, 4], BF16, name="v_grp", tag="v_grp", bufs=4, align_bytes=64)
+            nc.vector.tensor_tensor(
+                out=v_grp[g][:, cols, :],
+                in0=bank[:].rearrange("p t c -> p c t"),
+                in1=sgn[:, g : g + 1, :].to_broadcast([P, P, 4]),
+                op=ALU.mult,
+            )
+
+        def quant_v(g):
+            nc.vector.quantize_mx(
+                out=v_codes[g][:].bitcast(E4M3), scales=v_plane[g][:], in_=v_grp[g][:].rearrange("p c t -> p (c t)")
+            )
+
+        def average(h, i, g):
+            if g == 0:
+                o_bank[h, i] = psum.tile([P, C], F32, name="avg", tag=("o", "m")[h], bufs=4)
+            s = h * JG + g
+            nc.tensor.matmul_mx(
+                out=o_bank[h, i][:],
+                lhsT=e_codes[s][:, P * i : P * (i + 1)].bitcast(E4M3),
+                lhsT_scale=e_plane[s][:, P * i : P * (i + 1)],
+                rhs=v_codes[g][:].bitcast(E4M3),
+                rhs_scale=v_plane[g][:],
+                start=(g == 0),
+                stop=(g == JG - 1),
+            )
+
+        def finish(h, i, on_vector):
+            k = 4 * h + i
+            res = work.tile([P, C], F32, name="res", tag="res", bufs=4)
+            if on_vector:
+                nc.vector.tensor_scalar_mul(out=res[:], in0=o_bank[h, i][:], scalar1=rho_col[:, k : k + 1])
+            else:
+                nc.scalar.activation(out=res[:], in_=o_bank[h, i][:], func=ACT.Copy, scale=rho_col[:, k : k + 1])
+            nc.sync.dma_start(out=out[P * k : P * (k + 1), :], in_=res[:])
+
+        nc.vector.tensor_copy(
+            out=vec_rows[0:JG, :, :].rearrange("g t (s b) -> g t s b", b=4),
+            in_=g_row[:].rearrange("g (s t b) -> g t s b", t=4, b=4),
+        )
+        vec_t = psum.tile([P, 4, P], BF16, name="vec_t", tag="m", bufs=4)
+        for t in range(4):
+            nc.tensor.transpose(vec_t[:, t, :], vec_rows[:, t, :], id_bf[:])
+        nc.vector.tensor_copy(out=gam[:], in_=vec_t[:, :, 0:JG])
+        bits = gam[:].bitcast(I32)
+        nc.vector.tensor_scalar(
+            out=mant[:], in0=bits, scalar1=0x007FFFFF, scalar2=0x3F800000, op0=ALU.bitwise_and, op1=ALU.bitwise_or
+        )
+        nc.vector.tensor_scalar(
+            out=expo[:], in0=bits, scalar1=23, scalar2=0xFF, op0=ALU.logical_shift_right, op1=ALU.bitwise_and
+        )
+        nc.scalar.activation(out=mant_ln[:], in_=mant[:].bitcast(F32), func=ACT.Ln)
+        nc.scalar.activation(out=dummy[:], in_=dummy[:], func=ACT.Exp)
+        nc.vector.tensor_scalar(
+            out=expo_ln[:], in0=expo[:], scalar1=-127.0, scalar2=math.log(2.0), op0=ALU.add, op1=ALU.mult
+        )
+        nc.vector.tensor_scalar(
+            out=sgn2[:], in0=gam[:].rearrange("p t g -> p g t"), scalar1=0.0, scalar2=2.0, op0=ALU.is_ge, op1=ALU.mult
+        )
+        nc.vector.tensor_tensor(out=ln_gam[:], in0=mant_ln[:], in1=expo_ln[:], op=ALU.add)
+        nc.vector.tensor_scalar_add(out=sgn[:], in0=sgn2[:], scalar1=-1.0)
+
+
+        def weights_w():
+            nc.vector.tensor_copy(
+                out=w_grp[:].rearrange("p (c i) j -> p c j i", i=4), in_=w_raw[:].rearrange("p j (c i) -> p c j i", i=4)
+            )
+
+        def quant_w():
+            nc.vector.quantize_mx(
+                out=w_codes[:].bitcast(E4M3), scales=w_plane[:], in_=w_grp[:].rearrange("p c j -> p (c j)")
+            )
+
+        def rho_turn():
+            rho_t = psum.tile([P, P], BF16, name="rho_t", tag="m", bufs=4)
+            nc.tensor.transpose(rho_t[:], rho_rows[:], id_bf[:])
+            nc.vector.tensor_copy(out=rho_col[:], in_=rho_t[:, 0:8])
+
+        do = {
+            "G": weigh,
+            "T": turn_x,
+            "V": project,
+            "O": average,
+            "F": finish,
+            "arr": arrange_b,
+            "il": interleave,
+            "qe": quant_e,
+            "qx": quant_x,
+            "qv": quant_v,
+            "wi": weights_w,
+            "wq": quant_w,
+            "rho": rho_turn,
+        }
+        for step in PLAN:
+            do[step[0]](*step[1:])

@@ -5,139 +5,6 @@ import concourse.mybir as mybir
 from concourse.masks import make_identity
 
 M, N, D, F, C = 1024, 2048, 1024, 512, 512
-PLAN = [
-    ("T", 0,),
-    ("rho",),
-    ("arr", 0,),
-    ("G", 0, 0,),
-    ("qx", 0,),
-    ("arr", 1,),
-    ("G", 0, 1,),
-    ("G", 0, 2,),
-    ("G", 0, 3,),
-    ("wi",),
-    ("G", 1, 0,),
-    ("G", 1, 1,),
-    ("il", 0, 0,),
-    ("G", 1, 2,),
-    ("G", 1, 3,),
-    ("arr", 2,),
-    ("T", 1,),
-    ("arr", 3,),
-    ("T", 2,),
-    ("wq",),
-    ("il", 1, 0,),
-    ("il", 0, 1,),
-    ("qx", 1,),
-    ("V", 0, 0,),
-    ("G", 2, 0,),
-    ("il", 1, 1,),
-    ("G", 2, 1,),
-    ("V", 1, 0,),
-    ("V", 1, 1,),
-    ("qe", 1,),
-    ("G", 3, 0,),
-    ("V", 0, 1,),
-    ("G", 2, 2,),
-    ("qx", 2,),
-    ("G", 2, 3,),
-    ("V", 0, 2,),
-    ("V", 1, 2,),
-    ("V", 0, 3,),
-    ("T", 3,),
-    ("G", 4, 0,),
-    ("qe", 0,),
-    ("G", 3, 1,),
-    ("qv", 0,),
-    ("il", 2, 0,),
-    ("G", 3, 2,),
-    ("qx", 3,),
-    ("V", 1, 3,),
-    ("G", 3, 3,),
-    ("V", 2, 0,),
-    ("qv", 1,),
-    ("G", 4, 1,),
-    ("V", 2, 1,),
-    ("V", 3, 0,),
-    ("G", 4, 2,),
-    ("il", 3, 0,),
-    ("G", 4, 3,),
-    ("O", 0, 2, 0,),
-    ("V", 2, 2,),
-    ("O", 0, 3, 0,),
-    ("V", 3, 1,),
-    ("il", 2, 1,),
-    ("G", 5, 0,),
-    ("V", 3, 2,),
-    ("il", 4, 0,),
-    ("O", 0, 2, 1,),
-    ("O", 0, 0, 0,),
-    ("G", 6, 0,),
-    ("V", 2, 3,),
-    ("G", 5, 1,),
-    ("O", 0, 1, 0,),
-    ("il", 3, 1,),
-    ("O", 0, 0, 1,),
-    ("G", 7, 0,),
-    ("G", 5, 2,),
-    ("G", 5, 3,),
-    ("qv", 2,),
-    ("il", 4, 1,),
-    ("qe", 2,),
-    ("V", 3, 3,),
-    ("il", 5, 0,),
-    ("G", 6, 1,),
-    ("il", 5, 1,),
-    ("qv", 3,),
-    ("G", 6, 2,),
-    ("O", 0, 3, 1,),
-    ("G", 6, 3,),
-    ("O", 0, 0, 2,),
-    ("O", 0, 3, 2,),
-    ("O", 0, 1, 1,),
-    ("G", 7, 1,),
-    ("G", 7, 2,),
-    ("G", 7, 3,),
-    ("O", 0, 2, 2,),
-    ("qe", 3,),
-    ("O", 0, 0, 3,),
-    ("qe", 5,),
-    ("qe", 4,),
-    ("O", 0, 3, 3,),
-    ("O", 0, 1, 2,),
-    ("O", 0, 2, 3,),
-    ("il", 6, 0,),
-    ("il", 6, 1,),
-    ("O", 1, 0, 0,),
-    ("F", 0, 0, False,),
-    ("O", 1, 1, 0,),
-    ("O", 0, 1, 3,),
-    ("O", 1, 1, 1,),
-    ("O", 1, 3, 0,),
-    ("il", 7, 0,),
-    ("qe", 6,),
-    ("O", 1, 0, 1,),
-    ("F", 0, 3, False,),
-    ("O", 1, 0, 2,),
-    ("il", 7, 1,),
-    ("O", 1, 2, 0,),
-    ("O", 1, 1, 2,),
-    ("O", 1, 3, 1,),
-    ("qe", 7,),
-    ("O", 1, 0, 3,),
-    ("O", 1, 1, 3,),
-    ("F", 0, 2, False,),
-    ("O", 1, 3, 2,),
-    ("O", 1, 3, 3,),
-    ("F", 0, 1, False,),
-    ("O", 1, 2, 1,),
-    ("F", 1, 0, True,),
-    ("O", 1, 2, 2,),
-    ("F", 1, 1, False,),
-    ("F", 1, 3, False,),
-    ("O", 1, 2, 3,),
-    ("F", 1, 2, True,),
-]
 FLOPS = 2 * (M * N * D + N * F * C + M * N * C)
 
 F32 = mybir.dt.float32
@@ -151,9 +18,11 @@ ALU = mybir.AluOpType
 ACT = mybir.ActivationFunctionType
 
 P = 128
-JG = N // 512
+GROUPS = N // 512
 HALF = 512
-DG = D // 512
+DEPTH = D // 512
+TILES = HALF // P
+STEPS = 2 * GROUPS
 
 
 def tile_balanced_nonlocal_means_s12_kernel(
@@ -162,171 +31,174 @@ def tile_balanced_nonlocal_means_s12_kernel(
     nc = tc.nc
     with ExitStack() as ctx:
         keep = ctx.enter_context(tc.tile_pool(name="keep", bufs=1))
-        work = ctx.enter_context(tc.tile_pool(name="work", bufs=3))
+        work = ctx.enter_context(tc.tile_pool(name="work", bufs=4))
         psum = ctx.enter_context(tc.psum_pool(name="psum", bufs=4))
         ctx.enter_context(tc.manual_schedule())
 
         def kept(name, shape, dtype):
             return keep.tile(shape, dtype, name=name, tag=name, align_bytes=64)
 
-        a_codes = [kept("a_codes%d" % h, [P, DG, 1024], U8) for h in range(2)]
-        a_plane = kept("a_plane", [P, DG, M], U8)
-        b_plane_raw = kept("b_plane_raw", [P, DG, N], U8)
-        b_raw = [kept("b_raw%d" % g, [P, DG, 1024], U8) for g in range(JG)]
-        b_codes = [kept("b_codes%d" % g, [P, DG, 1024], U8) for g in range(JG)]
-        b_plane = [kept("b_plane%d" % g, [P, DG, 512], U8) for g in range(JG)]
-        x_raw = [kept("x_raw%d" % g, [P, 4, F], BF16) for g in range(JG)]
+        a_codes = [kept("a_codes%d" % h, [P, DEPTH, 2 * HALF], U8) for h in range(2)]
+        a_plane = [kept("a_plane%d" % h, [P, DEPTH, HALF], U8) for h in range(2)]
+        b_raw = [kept("b_raw%d" % g, [P, DEPTH, 1024], U8) for g in range(GROUPS)]
+        b_rows_first = kept("b_rows_first", [P, DEPTH, 512], U8)
+        b_rows_rest = kept("b_rows_rest", [P, DEPTH, N - 512], U8)
+        b_codes = [kept("b_codes%d" % g, [P, DEPTH, 1024], U8) for g in range(GROUPS)]
+        b_plane = [kept("b_plane%d" % g, [P, DEPTH, 512], U8) for g in range(GROUPS)]
+        x_raw = [kept("x_raw%d" % g, [P, 4, F], BF16) for g in range(GROUPS)]
+        x_sorted = [kept("x_sorted%d" % g, [P, 4, F], BF16) for g in range(GROUPS)]
+        x_grp = [kept("x_grp%d" % g, [P, 512, 4], BF16) for g in range(GROUPS)]
+        x_codes = [kept("x_codes%d" % g, [P, 512], U32) for g in range(GROUPS)]
+        x_plane = [kept("x_plane%d" % g, [P, 512], U8) for g in range(GROUPS)]
         w_raw = kept("w_raw", [P, 4, C], BF16)
         w_grp = kept("w_grp", [P, C, 4], BF16)
         w_codes = kept("w_codes", [P, C], U32)
         w_plane = kept("w_plane", [P, C], U8)
-        x_codes = [kept("x_codes%d" % g, [P, 512], U32) for g in range(JG)]
-        x_plane = [kept("x_plane%d" % g, [P, 512], U8) for g in range(JG)]
-        v_codes = [kept("v_codes%d" % g, [P, C], U32) for g in range(JG)]
-        v_plane = [kept("v_plane%d" % g, [P, C], U8) for g in range(JG)]
-        e_codes = [kept("e_codes%d" % s, [P, HALF], U32) for s in range(2 * JG)]
-        e_plane = [kept("e_plane%d" % s, [P, HALF], U8) for s in range(2 * JG)]
-        g_row = kept("g_row", [JG, 512], BF16)
-        vec_rows = kept("vec_rows", [P, 4, P], BF16)
-        rho_rows = kept("rho_rows", [P, P], BF16)
-        id_bf = kept("id_bf", [P, P], BF16)
-        id_f = kept("id_f", [P, P], F32)
-        dummy = kept("dummy", [P, 1], F32)
-        gam = kept("gam", [P, 4, JG], F32)
-        mant = kept("mant", [P, 4, JG], I32)
-        expo = kept("expo", [P, 4, JG], I32)
-        expo_ln = kept("expo_ln", [P, 4, JG], F32)
-        mant_ln = kept("mant_ln", [P, 4, JG], F32)
-        ln_gam = kept("ln_gam", [P, 4, JG], F32)
-        sgn2 = kept("sgn2", [P, JG, 4], F32)
-        sgn = kept("sgn", [P, JG, 4], F32)
+        v_grp = [kept("v_grp%d" % g, [P, C, 4], BF16) for g in range(GROUPS)]
+        v_codes = [kept("v_codes%d" % g, [P, C], U32) for g in range(GROUPS)]
+        v_plane = [kept("v_plane%d" % g, [P, C], U8) for g in range(GROUPS)]
+        e_bf = [kept("e_bf%d" % s, [P, 4, HALF], BF16) for s in range(STEPS)]
+        e_grp = [kept("e_grp%d" % s, [P, HALF, 4], BF16) for s in range(STEPS)]
+        e_codes = [kept("e_codes%d" % s, [P, HALF], U32) for s in range(STEPS)]
+        e_plane = [kept("e_plane%d" % s, [P, HALF], U8) for s in range(STEPS)]
+        gam_raw = kept("gam_raw", [P, 512], BF16)
+        rho_raw = kept("rho_raw", [P, 256], BF16)
+        gam_x = kept("gam_x", [P, GROUPS, 4], BF16)
+        gam_rows = kept("gam_rows", [P, 512], F32)
+        gam_t = kept("gam_t", [P, 512], F32)
+        rho_t = kept("rho_t", [P, 256], BF16)
         rho_col = kept("rho_col", [P, M // P], F32)
+        mant = kept("mant", [P, 16], I32)
+        expo = kept("expo", [P, 16], I32)
+        expo_ln = kept("expo_ln", [P, 16], F32)
+        mant_ln = kept("mant_ln", [P, 16], F32)
+        ln_gam = kept("ln_gam", [P, 16], F32)
+        twice_pos = kept("twice_pos", [P, 16], F32)
+        sign = kept("sign", [P, 16], F32)
+        ident = kept("ident", [P, P], F32)
 
-        def load_b(queue, g):
+        def load_codes(queue, tile, words, first):
             queue.dma_start(
-                out=b_raw[g][:].bitcast(I32),
-                in_=b_words.rearrange("d p n -> p d n")[:, :, g * 1024 : (g + 1) * 1024].bitcast(I32),
+                out=tile[:].bitcast(I32),
+                in_=words.rearrange("d p n -> p d n")[:, :, first : first + 1024].bitcast(I32),
             )
 
-        def load_a(queue, h):
-            queue.dma_start(
-                out=a_codes[h][:].bitcast(I32),
-                in_=a_words.rearrange("d p n -> p d n")[:, :, h * 1024 : (h + 1) * 1024].bitcast(I32),
-            )
+        def load_rows(plane, rows, first, last):
+            for q in range(4):
+                nc.sync.dma_start(
+                    out=plane[32 * q : 32 * q + 4, :, :].bitcast(I32),
+                    in_=rows[:, 4 * q : 4 * q + 4, first:last].rearrange("d r n -> r d n").bitcast(I32),
+                )
 
         def load_x(g):
-            nc.sync.dma_start(out=x_raw[g][:], in_=x.rearrange("(g m b) f -> g m b f", g=JG, b=4)[g])
+            nc.sync.dma_start(out=x_raw[g][:], in_=x.rearrange("(g m b) f -> g m b f", g=GROUPS, b=4)[g])
 
-        nc.sync.dma_start(out=g_row[:], in_=gamma.rearrange("(g n) -> g n", g=JG))
-        make_identity(nc, id_bf[:])
-        nc.vector.memset(a_plane[:].bitcast(I32), 0)
-        nc.vector.memset(b_plane_raw[:].bitcast(I32), 0)
-        nc.vector.memset(dummy[:], 1.0)
-        nc.vector.memset(vec_rows[:], 0.0)
-        nc.vector.memset(rho_rows[:], 0.0)
-        nc.gpsimd.dma_start(out=rho_rows[0:8, :], in_=rho.rearrange("(i p) -> i p", p=P))
+        nc.vector.memset(gam_raw[:], 0.0)
+        nc.vector.memset(b_rows_first[:].bitcast(I32), 0)
+        nc.vector.memset(a_plane[0][:].bitcast(I32), 0)
+        nc.vector.memset(b_rows_rest[:].bitcast(I32), 0)
+        nc.vector.memset(a_plane[1][:].bitcast(I32), 0)
+        nc.vector.memset(rho_raw[:], 0.0)
 
-        def load_plane(plane, rows, q):
-            nc.sync.dma_start(
-                out=plane[32 * q : 32 * q + 4, :, :].bitcast(I32),
-                in_=rows[:, 4 * q : 4 * q + 4, :].rearrange("d r n -> r d n").bitcast(I32),
-            )
+        load_codes(nc.gpsimd, a_codes[0], a_words, 0)
+        make_identity(nc, ident[:])
+        nc.gpsimd.dma_start(out=w_raw[:], in_=w.rearrange("(p j) c -> p j c", j=4))
 
-        for q in range(3):
-            load_plane(a_plane, a_scales, q)
+        load_codes(nc.sync, b_raw[0], b_words, 0)
+        nc.sync.dma_start(
+            out=gam_raw[0:P:32, :].rearrange("q (g n) -> q g n", g=GROUPS),
+            in_=gamma.rearrange("(g q n) -> q g n", g=GROUPS, q=4),
+        )
+        load_rows(b_rows_first, b_scales, 0, 512)
+        load_rows(a_plane[0], a_scales, 0, HALF)
+        load_rows(b_rows_rest, b_scales, 512, N)
+        load_codes(nc.sync, b_raw[1], b_words, 1024)
+        nc.sync.dma_start(out=gam_x[:], in_=gamma.rearrange("(g m b) -> m g b", g=GROUPS, b=4))
         load_x(0)
-        load_b(nc.sync, 0)
-        load_a(nc.sync, 0)
-        load_plane(a_plane, a_scales, 3)
-        for q in range(4):
-            load_plane(b_plane_raw, b_scales, q)
-        nc.sync.dma_start(out=w_raw[:], in_=w.rearrange("(p j) c -> p j c", j=4))
-        load_b(nc.sync, 1)
-        load_b(nc.sync, 2)
         load_x(1)
-        load_b(nc.sync, 3)
+        load_codes(nc.sync, b_raw[2], b_words, 2048)
+        load_codes(nc.sync, b_raw[3], b_words, 3072)
         load_x(2)
         load_x(3)
-        load_a(nc.sync, 1)
-
-        nc.scalar.activation(out=mant_ln[:, 0, 0:1], in_=dummy[:], func=ACT.Ln)
-        nc.vector.tensor_copy(out=id_f[:], in_=id_bf[:])
+        load_codes(nc.sync, a_codes[1], a_words, 1024)
+        load_rows(a_plane[1], a_scales, HALF, M)
+        nc.sync.dma_start(
+            out=rho_raw[0:P:32, :].rearrange("q (k c) -> q k c", c=32),
+            in_=rho.rearrange("(k q c) -> q k c", q=4, c=32),
+        )
 
         def arrange_b(g):
-            for d in range(DG):
-                nc.vector.tensor_copy(
-                    out=b_codes[g][:, d, :].bitcast(I32).rearrange("p (t s w) -> p t s w", t=4, w=2),
-                    in_=b_raw[g][:, d, :].bitcast(I32).rearrange("p (s t w) -> p t s w", t=4, w=2),
-                )
             nc.vector.tensor_copy(
-                out=b_plane[g][:].bitcast(I32).rearrange("p d (t s) -> p d t s", t=4),
-                in_=b_plane_raw[:, :, g * 512 : (g + 1) * 512].bitcast(I32).rearrange("p d (s t) -> p d t s", t=4),
+                out=b_codes[g][:].bitcast(I32).rearrange("p d (t q w) -> p d t q w", t=4, w=4),
+                in_=b_raw[g][:].bitcast(I32).rearrange("p d (q t w) -> p d t q w", t=4, w=4),
+            )
+            rows = b_rows_first[:] if g == 0 else b_rows_rest[:, :, (g - 1) * 512 : g * 512]
+            nc.vector.tensor_copy(
+                out=b_plane[g][:].bitcast(I32).rearrange("p d (t q w) -> p d t q w", t=4, w=2),
+                in_=rows.bitcast(I32).rearrange("p d (q t w) -> p d t q w", t=4, w=2),
             )
 
-        x_grp = {}
-        e_bf = {}
-        e_grp = {}
-        v_grp = {}
-        o_bank = {}
-
-        def turn_x(g):
-            grp = work.tile([P, 512, 4], BF16, name="x_grp", tag="x_grp", bufs=4, align_bytes=64)
-            x_grp[g] = grp
-            words = grp[:].rearrange("p c j -> p (c j)").bitcast(F32)
-            banks = []
-            for k in range(2):
-                bank = psum.tile([P, 4, P], F32, name="xt", tag="m", bufs=4)
-                banks.append(bank)
-                for bl in range(2):
-                    for u in range(2):
-                        nc.tensor.transpose(
-                            bank[:, 2 * bl + u, :], x_raw[g][:, 2 * k + bl, :].bitcast(F32)[:, u::2], id_f[:]
-                        )
-            for k in range(2):
-                nc.scalar.copy(
-                    out=words.rearrange("p (t s e) -> p t s e", t=4, e=8)[:, :, :, 4 * k : 4 * k + 4],
-                    in_=banks[k][:].rearrange("p e (s t) -> p t s e", t=4),
+        def sort_x(g):
+            for row in range(4):
+                nc.vector.tensor_scalar_mul(
+                    out=x_sorted[g][:, row, :].rearrange("m (u p e) -> m u p e", u=2, e=2),
+                    in0=x_raw[g][:, row, :].rearrange("m (p u e) -> m u p e", u=2, e=2),
+                    scalar1=sign[:, 4 * g + row : 4 * g + row + 1],
                 )
 
-        def quant_x(g):
+        x_banks = {}
+
+        def turn_x(g):
+            for k in range(2):
+                bank = psum.tile([P, 4, P], F32, name="x_t", tag="side")
+                x_banks[g, k] = bank
+                for row in range(2):
+                    for u in range(2):
+                        nc.tensor.transpose(
+                            bank[:, 2 * row + u, :], x_sorted[g][:, 2 * k + row, :].bitcast(F32)[:, P * u : P * (u + 1)], ident[:]
+                        )
+
+        def take_x(g, copy):
+            words = x_grp[g][:].rearrange("p c j -> p (c j)").bitcast(F32)
+            for k in range(2):
+                copy(
+                    out=words.rearrange("p (t q r e) -> p t q r e", t=4, r=2, e=8)[:, :, :, :, 4 * k : 4 * k + 4],
+                    in_=x_banks[g, k][:].rearrange("p e (q t r) -> p t q r e", t=4, r=2),
+                )
+
+        def quantize(codes, plane, grouped, first=0, last=512):
             nc.vector.quantize_mx(
-                out=x_codes[g][:].bitcast(E4M3), scales=x_plane[g][:], in_=x_grp[g][:].rearrange("p c j -> p (c j)")
+                out=codes[:, first:last].bitcast(E4M3),
+                scales=plane[:, first:last],
+                in_=grouped[:, first:last, :].rearrange("p c t -> p (c t)"),
+            )
+
+        def interleave(grouped, rows, first=0, last=512):
+            nc.vector.tensor_copy(
+                out=grouped[:, first:last, :].rearrange("p (c i) t -> p c t i", i=4),
+                in_=rows[:, :, first:last].rearrange("p t (c i) -> p c t i", i=4),
             )
 
         def weigh(s, t):
-            h, g = divmod(s, JG)
-            bank = psum.tile([P, HALF], F32, name="gram", tag="m", bufs=4)
-            for d in range(DG):
+            h, g = divmod(s, GROUPS)
+            bank = psum.tile([P, HALF], F32, name="gram", tag="gram")
+            for d in range(DEPTH):
                 nc.tensor.matmul_mx(
                     out=bank[:],
                     lhsT=b_codes[g][:, d, 256 * t : 256 * (t + 1)].bitcast(E2M1),
                     lhsT_scale=b_plane[g][:, d, P * t : P * (t + 1)],
                     rhs=a_codes[h][:, d, :].bitcast(E2M1),
-                    rhs_scale=a_plane[:, d, HALF * h : HALF * (h + 1)],
+                    rhs_scale=a_plane[h][:, d, :],
                     start=(d == 0),
-                    stop=(d == DG - 1),
+                    stop=(d == DEPTH - 1),
                 )
-            if t == 0:
-                e_bf[s] = work.tile([P, 4, HALF], BF16, name="e_bf", tag="e_bf", bufs=8, align_bytes=64)
-            nc.scalar.activation(out=e_bf[s][:, t, :], in_=bank[:], func=ACT.Exp, bias=ln_gam[:, t, g : g + 1])
-
-        def interleave(s, part):
-            if part == 0:
-                e_grp[s] = work.tile([P, HALF, 4], BF16, name="e_grp", tag="e_grp", bufs=4, align_bytes=64)
-            cols = slice(part * 256, (part + 1) * 256)
-            nc.vector.tensor_copy(
-                out=e_grp[s][:, cols, :].rearrange("p (c i) t -> p c t i", i=4),
-                in_=e_bf[s][:, :, cols].rearrange("p t (c i) -> p c t i", i=4),
+            nc.scalar.activation(
+                out=e_bf[s][:, t, :], in_=bank[:], func=ACT.Exp, bias=ln_gam[:, 4 * g + t : 4 * g + t + 1]
             )
 
-        def quant_e(s):
-            nc.vector.quantize_mx(
-                out=e_codes[s][:].bitcast(E4M3), scales=e_plane[s][:], in_=e_grp[s][:].rearrange("p c t -> p (c t)")
-            )
-
-        def project(g, cq):
-            bank = psum.tile([P, 4, P], F32, name="val", tag="m", bufs=4)
-            cols = slice(P * cq, P * (cq + 1))
+        def project(g, quarter):
+            bank = psum.tile([P, 4, P], F32, name="val", tag="side")
+            cols = slice(P * quarter, P * (quarter + 1))
             for t in range(4):
                 nc.tensor.matmul_mx(
                     out=bank[:, t, :],
@@ -337,52 +209,42 @@ def tile_balanced_nonlocal_means_s12_kernel(
                     start=True,
                     stop=True,
                 )
-            if cq == 0:
-                v_grp[g] = work.tile([P, C, 4], BF16, name="v_grp", tag="v_grp", bufs=4, align_bytes=64)
-            nc.vector.tensor_tensor(
-                out=v_grp[g][:, cols, :],
-                in0=bank[:].rearrange("p t c -> p c t"),
-                in1=sgn[:, g : g + 1, :].to_broadcast([P, P, 4]),
-                op=ALU.mult,
-            )
+            copy = nc.scalar.copy if quarter % 2 == 0 else nc.vector.tensor_copy
+            copy(out=v_grp[g][:, cols, :], in_=bank[:].rearrange("p t c -> p c t"))
 
-        def quant_v(g):
-            nc.vector.quantize_mx(
-                out=v_codes[g][:].bitcast(E4M3), scales=v_plane[g][:], in_=v_grp[g][:].rearrange("p c t -> p (c t)")
-            )
+        o_bank = {}
 
-        def average(h, i, g):
+        def average(k, g, first=0, last=C):
+            h, i = divmod(k, TILES)
             if g == 0:
-                o_bank[h, i] = psum.tile([P, C], F32, name="avg", tag=("o", "m")[h], bufs=4)
-            s = h * JG + g
+                tag = "gram" if h == 1 and first == 0 else "side"
+                o_bank[k, first] = psum.tile([P, last - first], F32, name="avg", tag=tag)
+            s = h * GROUPS + g
             nc.tensor.matmul_mx(
-                out=o_bank[h, i][:],
+                out=o_bank[k, first][:],
                 lhsT=e_codes[s][:, P * i : P * (i + 1)].bitcast(E4M3),
                 lhsT_scale=e_plane[s][:, P * i : P * (i + 1)],
-                rhs=v_codes[g][:].bitcast(E4M3),
-                rhs_scale=v_plane[g][:],
+                rhs=v_codes[g][:, first:last].bitcast(E4M3),
+                rhs_scale=v_plane[g][:, first:last],
                 start=(g == 0),
-                stop=(g == JG - 1),
+                stop=(g == GROUPS - 1),
             )
 
-        def finish(h, i, on_vector):
-            k = 4 * h + i
-            res = work.tile([P, C], F32, name="res", tag="res", bufs=4)
+        def finish(k, on_vector, first=0, last=C):
+            res = work.tile([P, last - first], F32, name="res", tag="res", bufs=9)
             if on_vector:
-                nc.vector.tensor_scalar_mul(out=res[:], in0=o_bank[h, i][:], scalar1=rho_col[:, k : k + 1])
+                nc.vector.tensor_scalar_mul(out=res[:], in0=o_bank[k, first][:], scalar1=rho_col[:, k : k + 1])
             else:
-                nc.scalar.activation(out=res[:], in_=o_bank[h, i][:], func=ACT.Copy, scale=rho_col[:, k : k + 1])
-            nc.sync.dma_start(out=out[P * k : P * (k + 1), :], in_=res[:])
+                nc.scalar.activation(out=res[:], in_=o_bank[k, first][:], func=ACT.Copy, scale=rho_col[:, k : k + 1])
+            nc.sync.dma_start(out=out[P * k : P * (k + 1), first:last], in_=res[:])
 
         nc.vector.tensor_copy(
-            out=vec_rows[0:JG, :, :].rearrange("g t (s b) -> g t s b", b=4),
-            in_=g_row[:].rearrange("g (s t b) -> g t s b", t=4, b=4),
+            out=gam_rows[:].rearrange("p (g t q r) -> p g t q r", g=GROUPS, t=4, q=4),
+            in_=gam_raw[:].rearrange("p (g q t r) -> p g t q r", g=GROUPS, q=4, t=4),
         )
-        vec_t = psum.tile([P, 4, P], BF16, name="vec_t", tag="m", bufs=4)
-        for t in range(4):
-            nc.tensor.transpose(vec_t[:, t, :], vec_rows[:, t, :], id_bf[:])
-        nc.vector.tensor_copy(out=gam[:], in_=vec_t[:, :, 0:JG])
-        bits = gam[:].bitcast(I32)
+        nc.vector.transpose(out=gam_t[:], in_=gam_rows[:])
+        arrange_b(0)
+        bits = gam_t[:].bitcast(I32)[:, 0:512:32]
         nc.vector.tensor_scalar(
             out=mant[:], in0=bits, scalar1=0x007FFFFF, scalar2=0x3F800000, op0=ALU.bitwise_and, op1=ALU.bitwise_or
         )
@@ -390,46 +252,104 @@ def tile_balanced_nonlocal_means_s12_kernel(
             out=expo[:], in0=bits, scalar1=23, scalar2=0xFF, op0=ALU.logical_shift_right, op1=ALU.bitwise_and
         )
         nc.scalar.activation(out=mant_ln[:], in_=mant[:].bitcast(F32), func=ACT.Ln)
-        nc.scalar.activation(out=dummy[:], in_=dummy[:], func=ACT.Exp)
         nc.vector.tensor_scalar(
             out=expo_ln[:], in0=expo[:], scalar1=-127.0, scalar2=math.log(2.0), op0=ALU.add, op1=ALU.mult
         )
-        nc.vector.tensor_scalar(
-            out=sgn2[:], in0=gam[:].rearrange("p t g -> p g t"), scalar1=0.0, scalar2=2.0, op0=ALU.is_ge, op1=ALU.mult
-        )
         nc.vector.tensor_tensor(out=ln_gam[:], in0=mant_ln[:], in1=expo_ln[:], op=ALU.add)
-        nc.vector.tensor_scalar_add(out=sgn[:], in0=sgn2[:], scalar1=-1.0)
 
+        def e_jobs(s):
+            return [
+                lambda: interleave(e_grp[s], e_bf[s], 0, 256),
+                lambda: interleave(e_grp[s], e_bf[s], 256, 512),
+                lambda: quantize(e_codes[s], e_plane[s], e_grp[s]),
+            ]
 
-        def weights_w():
-            nc.vector.tensor_copy(
-                out=w_grp[:].rearrange("p (c i) j -> p c j i", i=4), in_=w_raw[:].rearrange("p j (c i) -> p c j i", i=4)
+        def q_x(g):
+            return lambda: quantize(x_codes[g], x_plane[g], x_grp[g])
+
+        def q_v(g):
+            return lambda: quantize(v_codes[g], v_plane[g], v_grp[g])
+
+        def arr(g):
+            return lambda: arrange_b(g)
+
+        def srt(g):
+            return lambda: sort_x(g)
+
+        def signs():
+            nc.vector.tensor_scalar(
+                out=twice_pos[:], in0=gam_x[:].rearrange("m g b -> m (g b)"), scalar1=0.0, scalar2=2.0, op0=ALU.is_ge, op1=ALU.mult
             )
+            arrange_b(1)
+            nc.vector.tensor_scalar_add(out=sign[:], in0=twice_pos[:], scalar1=-1.0)
 
-        def quant_w():
-            nc.vector.quantize_mx(
-                out=w_codes[:].bitcast(E4M3), scales=w_plane[:], in_=w_grp[:].rearrange("p c j -> p (c j)")
-            )
+        def turn_rho():
+            nc.vector.transpose(out=rho_t[:], in_=rho_raw[:])
 
-        def rho_turn():
-            rho_t = psum.tile([P, P], BF16, name="rho_t", tag="m", bufs=4)
-            nc.tensor.transpose(rho_t[:], rho_rows[:], id_bf[:])
-            nc.vector.tensor_copy(out=rho_col[:], in_=rho_t[:, 0:8])
+        def take_rho():
+            nc.vector.tensor_copy(out=rho_col[:], in_=rho_t[:, 0:256:32])
 
-        do = {
-            "G": weigh,
-            "T": turn_x,
-            "V": project,
-            "O": average,
-            "F": finish,
-            "arr": arrange_b,
-            "il": interleave,
-            "qe": quant_e,
-            "qx": quant_x,
-            "qv": quant_v,
-            "wi": weights_w,
-            "wq": quant_w,
-            "rho": rho_turn,
+        e = [e_jobs(s) for s in range(STEPS)]
+        vector_after = {
+            3: [lambda: interleave(w_grp, w_raw), signs, lambda: quantize(w_codes, w_plane, w_grp), srt(0), srt(1)],
+            5: [e[0][0], arr(2), e[0][1]],
+            6: [q_x(0)],
+            7: [e[0][2]],
+            8: [arr(3)],
+            9: [q_x(1)],
+            10: [e[1][0]],
+            11: [srt(2)],
+            12: [e[1][1]],
+            13: [srt(3)],
+            14: [e[1][2]],
+            15: [q_v(0)],
+            16: [e[2][0], e[2][1], q_v(1)],
+            17: [q_x(2)],
+            18: [e[2][2]],
+            19: [e[3][0]],
+            20: [e[3][1]],
+            21: [q_x(3)],
+            22: [e[3][2]],
+            23: [e[4][0]],
+            24: [q_v(2)],
+            25: [e[4][1]],
+            26: [turn_rho, e[4][2]],
+            27: [q_v(3), take_rho, e[5][0]],
+            28: [e[5][1], e[6][0]],
+            29: [e[5][2], e[6][1]],
+            30: [e[6][2]],
         }
-        for step in PLAN:
-            do[step[0]](*step[1:])
+        early = [(k, g) for k in range(TILES) for g in range(GROUPS)]
+        for slot in range(4 * STEPS):
+            weigh(*divmod(slot, 4))
+            for job in vector_after.get(slot, []):
+                job()
+            if 8 <= slot < 16:
+                project(*divmod(slot - 8, 4))
+            if 19 <= slot < 27:
+                project(*divmod(slot - 11, 4))
+            if slot >= 28:
+                for k, g in early[2 * (slot - 28) : 2 * (slot - 27)]:
+                    average(k, g)
+                    if g == GROUPS - 1:
+                        finish(k, False)
+            if slot in (5, 16):
+                pair = (0, 1) if slot == 5 else (2, 3)
+                for g in pair:
+                    turn_x(g)
+                for g in pair:
+                    take_x(g, nc.scalar.copy)
+
+        last = STEPS - 1
+        interleave(e_grp[last], e_bf[last], 0, 256)
+        interleave(e_grp[last], e_bf[last], 256, 512)
+        quantize(e_codes[last], e_plane[last], e_grp[last])
+        for k in range(2, 7):
+            for g in range(GROUPS):
+                average(k, g)
+            finish(k, k == 6)
+        for first in (0, 256):
+            for g in range(GROUPS):
+                average(7, g, first, first + 256)
+        finish(7, False, 0, 256)
+        finish(7, True, 256, 512)

@@ -23,6 +23,7 @@ HALF = 512
 DEPTH = D // 512
 TILES = HALF // P
 STEPS = 2 * GROUPS
+SCALAR_QUARTERS = [(1,), (0, 2), (1,), (0, 2)]
 
 
 def tile_balanced_nonlocal_means_s12_kernel(
@@ -40,11 +41,16 @@ def tile_balanced_nonlocal_means_s12_kernel(
 
         a_codes = [kept("a_codes%d" % h, [P, DEPTH, 2 * HALF], U8) for h in range(2)]
         a_plane = [kept("a_plane%d" % h, [P, DEPTH, HALF], U8) for h in range(2)]
-        b_raw = [kept("b_raw%d" % g, [P, DEPTH, 1024], U8) for g in range(GROUPS)]
+        b_raw = [kept("b_raw%d" % g, [P, DEPTH, 1024], U8) for g in range(2)]
+        b_raw_late = kept("b_raw_late", [P, DEPTH, 2048], U8)
         b_rows_first = kept("b_rows_first", [P, DEPTH, 512], U8)
         b_rows_rest = kept("b_rows_rest", [P, DEPTH, N - 512], U8)
-        b_codes = [kept("b_codes%d" % g, [P, DEPTH, 1024], U8) for g in range(GROUPS)]
-        b_plane = [kept("b_plane%d" % g, [P, DEPTH, 512], U8) for g in range(GROUPS)]
+        b_codes_early = [kept("b_codes%d" % g, [P, DEPTH, 1024], U8) for g in range(2)]
+        b_codes_late = kept("b_codes_late", [P, DEPTH, 2048], U8)
+        b_codes = [b_codes_early[0][:], b_codes_early[1][:], b_codes_late[:, :, 0:1024], b_codes_late[:, :, 1024:2048]]
+        b_plane_first = kept("b_plane_first", [P, DEPTH, 512], U8)
+        b_plane_rest = kept("b_plane_rest", [P, DEPTH, N - 512], U8)
+        b_plane = [b_plane_first[:]] + [b_plane_rest[:, :, 512 * g : 512 * (g + 1)] for g in range(GROUPS - 1)]
         x_raw = [kept("x_raw%d" % g, [P, 4, F], BF16) for g in range(GROUPS)]
         x_sorted = [kept("x_sorted%d" % g, [P, 4, F], BF16) for g in range(GROUPS)]
         x_grp = [kept("x_grp%d" % g, [P, 512, 4], BF16) for g in range(GROUPS)]
@@ -62,25 +68,23 @@ def tile_balanced_nonlocal_means_s12_kernel(
         e_codes = [kept("e_codes%d" % s, [P, HALF], U32) for s in range(STEPS)]
         e_plane = [kept("e_plane%d" % s, [P, HALF], U8) for s in range(STEPS)]
         gam_raw = kept("gam_raw", [P, 512], BF16)
-        rho_raw = kept("rho_raw", [P, 256], BF16)
+        rho_raw = kept("rho_raw", [P, M // P, 2], BF16)
         gam_x = kept("gam_x", [P, GROUPS, 4], BF16)
         gam_rows = kept("gam_rows", [P, 512], F32)
         gam_t = kept("gam_t", [P, 512], F32)
-        rho_t = kept("rho_t", [P, 256], BF16)
         rho_col = kept("rho_col", [P, M // P], F32)
         mant = kept("mant", [P, 16], I32)
         expo = kept("expo", [P, 16], I32)
         expo_ln = kept("expo_ln", [P, 16], F32)
         mant_ln = kept("mant_ln", [P, 16], F32)
         ln_gam = kept("ln_gam", [P, 16], F32)
-        twice_pos = kept("twice_pos", [P, 16], F32)
-        sign = kept("sign", [P, 16], F32)
+        half_sign = kept("half_sign", [P, 16], F32)
         ident = kept("ident", [P, P], F32)
 
         def load_codes(queue, tile, words, first):
             queue.dma_start(
                 out=tile[:].bitcast(I32),
-                in_=words.rearrange("d p n -> p d n")[:, :, first : first + 1024].bitcast(I32),
+                in_=words.rearrange("d p n -> p d n")[:, :, first : first + tile.shape[2]].bitcast(I32),
             )
 
         def load_rows(plane, rows, first, last):
@@ -98,7 +102,6 @@ def tile_balanced_nonlocal_means_s12_kernel(
         nc.vector.memset(a_plane[0][:].bitcast(I32), 0)
         nc.vector.memset(b_rows_rest[:].bitcast(I32), 0)
         nc.vector.memset(a_plane[1][:].bitcast(I32), 0)
-        nc.vector.memset(rho_raw[:], 0.0)
 
         load_codes(nc.gpsimd, a_codes[0], a_words, 0)
         make_identity(nc, ident[:])
@@ -116,34 +119,29 @@ def tile_balanced_nonlocal_means_s12_kernel(
         nc.sync.dma_start(out=gam_x[:], in_=gamma.rearrange("(g m b) -> m g b", g=GROUPS, b=4))
         load_x(0)
         load_x(1)
-        load_codes(nc.sync, b_raw[2], b_words, 2048)
-        load_codes(nc.sync, b_raw[3], b_words, 3072)
+        load_codes(nc.sync, b_raw_late, b_words, 2048)
         load_x(2)
         load_x(3)
         load_codes(nc.sync, a_codes[1], a_words, 1024)
         load_rows(a_plane[1], a_scales, HALF, M)
-        nc.sync.dma_start(
-            out=rho_raw[0:P:32, :].rearrange("q (k c) -> q k c", c=32),
-            in_=rho.rearrange("(k q c) -> q k c", q=4, c=32),
-        )
+        with nc.allow_non_contiguous_dma(reason="one rho value a pixel, onto the partition of its output row"):
+            nc.sync.dma_start(out=rho_raw[:, :, 0], in_=rho.rearrange("(k p) -> p k", p=P))
 
-        def arrange_b(g):
+        def arrange(dst, src, words):
             nc.vector.tensor_copy(
-                out=b_codes[g][:].bitcast(I32).rearrange("p d (t q w) -> p d t q w", t=4, w=4),
-                in_=b_raw[g][:].bitcast(I32).rearrange("p d (q t w) -> p d t q w", t=4, w=4),
-            )
-            rows = b_rows_first[:] if g == 0 else b_rows_rest[:, :, (g - 1) * 512 : g * 512]
-            nc.vector.tensor_copy(
-                out=b_plane[g][:].bitcast(I32).rearrange("p d (t q w) -> p d t q w", t=4, w=2),
-                in_=rows.bitcast(I32).rearrange("p d (q t w) -> p d t q w", t=4, w=2),
+                out=dst[:].bitcast(I32).rearrange("p d (g t q w) -> p (d g) t q w", t=4, q=16, w=words),
+                in_=src[:].bitcast(I32).rearrange("p d (g q t w) -> p (d g) t q w", t=4, q=16, w=words),
             )
 
         def sort_x(g):
             for row in range(4):
-                nc.vector.tensor_scalar_mul(
+                nc.vector.tensor_scalar(
                     out=x_sorted[g][:, row, :].rearrange("m (u p e) -> m u p e", u=2, e=2),
                     in0=x_raw[g][:, row, :].rearrange("m (p u e) -> m u p e", u=2, e=2),
-                    scalar1=sign[:, 4 * g + row : 4 * g + row + 1],
+                    scalar1=half_sign[:, 4 * g + row : 4 * g + row + 1],
+                    scalar2=2.0,
+                    op0=ALU.mult,
+                    op1=ALU.mult,
                 )
 
         x_banks = {}
@@ -173,8 +171,8 @@ def tile_balanced_nonlocal_means_s12_kernel(
                 in_=grouped[:, first:last, :].rearrange("p c t -> p (c t)"),
             )
 
-        def interleave(grouped, rows, first=0, last=512):
-            nc.vector.tensor_copy(
+        def interleave(grouped, rows, first=0, last=512, copy=nc.vector.tensor_copy):
+            copy(
                 out=grouped[:, first:last, :].rearrange("p (c i) t -> p c t i", i=4),
                 in_=rows[:, :, first:last].rearrange("p t (c i) -> p c t i", i=4),
             )
@@ -209,7 +207,7 @@ def tile_balanced_nonlocal_means_s12_kernel(
                     start=True,
                     stop=True,
                 )
-            copy = nc.scalar.copy if quarter % 2 == 0 else nc.vector.tensor_copy
+            copy = nc.scalar.copy if quarter in SCALAR_QUARTERS[g] else nc.vector.tensor_copy
             copy(out=v_grp[g][:, cols, :], in_=bank[:].rearrange("p t c -> p c t"))
 
         o_bank = {}
@@ -242,8 +240,9 @@ def tile_balanced_nonlocal_means_s12_kernel(
             out=gam_rows[:].rearrange("p (g t q r) -> p g t q r", g=GROUPS, t=4, q=4),
             in_=gam_raw[:].rearrange("p (g q t r) -> p g t q r", g=GROUPS, q=4, t=4),
         )
+        arrange(b_codes_early[0], b_raw[0], 4)
         nc.vector.transpose(out=gam_t[:], in_=gam_rows[:])
-        arrange_b(0)
+        arrange(b_plane_first, b_rows_first, 2)
         bits = gam_t[:].bitcast(I32)[:, 0:512:32]
         nc.vector.tensor_scalar(
             out=mant[:], in0=bits, scalar1=0x007FFFFF, scalar2=0x3F800000, op0=ALU.bitwise_and, op1=ALU.bitwise_or
@@ -259,10 +258,12 @@ def tile_balanced_nonlocal_means_s12_kernel(
 
         def e_jobs(s):
             return [
-                lambda: interleave(e_grp[s], e_bf[s], 0, 256),
-                lambda: interleave(e_grp[s], e_bf[s], 256, 512),
+                lambda: interleave(e_grp[s], e_bf[s]),
                 lambda: quantize(e_codes[s], e_plane[s], e_grp[s]),
             ]
+
+        def half(s, h):
+            return lambda: interleave(e_grp[s], e_bf[s], 256 * h, 256 * (h + 1))
 
         def q_x(g):
             return lambda: quantize(x_codes[g], x_plane[g], x_grp[g])
@@ -270,54 +271,46 @@ def tile_balanced_nonlocal_means_s12_kernel(
         def q_v(g):
             return lambda: quantize(v_codes[g], v_plane[g], v_grp[g])
 
-        def arr(g):
-            return lambda: arrange_b(g)
-
         def srt(g):
             return lambda: sort_x(g)
 
         def signs():
             nc.vector.tensor_scalar(
-                out=twice_pos[:], in0=gam_x[:].rearrange("m g b -> m (g b)"), scalar1=0.0, scalar2=2.0, op0=ALU.is_ge, op1=ALU.mult
+                out=half_sign[:], in0=gam_x[:].rearrange("m g b -> m (g b)"), scalar1=0.0, scalar2=0.5, op0=ALU.is_ge, op1=ALU.subtract
             )
-            arrange_b(1)
-            nc.vector.tensor_scalar_add(out=sign[:], in0=twice_pos[:], scalar1=-1.0)
-
-        def turn_rho():
-            nc.vector.transpose(out=rho_t[:], in_=rho_raw[:])
+            arrange(b_codes_early[1], b_raw[1], 4)
+            quantize(w_codes, w_plane, w_grp)
 
         def take_rho():
-            nc.vector.tensor_copy(out=rho_col[:], in_=rho_t[:, 0:256:32])
+            nc.scalar.copy(out=rho_col[:], in_=rho_raw[:, :, 0])
 
         e = [e_jobs(s) for s in range(STEPS)]
         vector_after = {
-            3: [lambda: interleave(w_grp, w_raw), signs, lambda: quantize(w_codes, w_plane, w_grp), srt(0), srt(1)],
-            5: [e[0][0], arr(2), e[0][1]],
+            3: [
+                lambda: interleave(w_grp, w_raw),
+                lambda: arrange(b_plane_rest, b_rows_rest, 2),
+                signs,
+                srt(0),
+                srt(1),
+            ],
+            5: [half(0, 0), lambda: arrange(b_codes_late, b_raw_late, 4)],
             6: [q_x(0)],
-            7: [e[0][2]],
-            8: [arr(3)],
+            7: [half(0, 1)],
             9: [q_x(1)],
-            10: [e[1][0]],
-            11: [srt(2)],
-            12: [e[1][1]],
-            13: [srt(3)],
-            14: [e[1][2]],
-            15: [q_v(0)],
-            16: [e[2][0], e[2][1], q_v(1)],
-            17: [q_x(2)],
-            18: [e[2][2]],
-            19: [e[3][0]],
-            20: [e[3][1]],
-            21: [q_x(3)],
-            22: [e[3][2]],
-            23: [e[4][0]],
+            10: [e[0][1], srt(2)],
+            11: [e[1][0]],
+            12: [srt(3)],
+            16: [q_v(0), e[1][1], q_v(1)],
+            17: [q_x(2), e[2][0]],
+            19: [e[2][1]],
+            20: [q_x(3)],
+            21: [e[3][0]],
+            23: [e[3][1]],
             24: [q_v(2)],
-            25: [e[4][1]],
-            26: [turn_rho, e[4][2]],
-            27: [q_v(3), take_rho, e[5][0]],
-            28: [e[5][1], e[6][0]],
-            29: [e[5][2], e[6][1]],
-            30: [e[6][2]],
+            27: [take_rho, q_v(3), e[4][0]],
+            28: [e[5][0], e[4][1]],
+            29: [e[6][0], e[5][1]],
+            30: [e[6][1]],
         }
         early = [(k, g) for k in range(TILES) for g in range(GROUPS)]
         for slot in range(4 * STEPS):
@@ -329,7 +322,7 @@ def tile_balanced_nonlocal_means_s12_kernel(
             if 19 <= slot < 27:
                 project(*divmod(slot - 11, 4))
             if slot >= 28:
-                for k, g in early[2 * (slot - 28) : 2 * (slot - 27)]:
+                for k, g in early[3 * (slot - 28) : 3 * (slot - 27)]:
                     average(k, g)
                     if g == GROUPS - 1:
                         finish(k, False)
@@ -342,12 +335,22 @@ def tile_balanced_nonlocal_means_s12_kernel(
 
         last = STEPS - 1
         interleave(e_grp[last], e_bf[last], 0, 256)
-        interleave(e_grp[last], e_bf[last], 256, 512)
-        quantize(e_codes[last], e_plane[last], e_grp[last])
-        for k in range(2, 7):
-            for g in range(GROUPS):
+        for g in range(GROUPS):
+            average(3, g)
+        finish(3, False)
+        for k in (4, 5):
+            for g in range(GROUPS - 1):
                 average(k, g)
-            finish(k, k == 6)
+        quantize(e_codes[last], e_plane[last], e_grp[last], 0, 256)
+        interleave(e_grp[last], e_bf[last], 256, 512)
+        for k in (4, 5):
+            average(k, GROUPS - 1)
+        quantize(e_codes[last], e_plane[last], e_grp[last], 256, 512)
+        finish(4, False)
+        finish(5, False)
+        for g in range(GROUPS):
+            average(6, g)
+        finish(6, True)
         for first in (0, 256):
             for g in range(GROUPS):
                 average(7, g, first, first + 256)

@@ -105,7 +105,6 @@ def tile_balanced_nonlocal_means_s12_kernel(
 
         load_codes(nc.gpsimd, a_codes[0], a_words, 0)
         make_identity(nc, ident[:])
-        nc.gpsimd.dma_start(out=w_raw[:], in_=w.rearrange("(p j) c -> p j c", j=4))
 
         load_codes(nc.sync, b_raw[0], b_words, 0)
         nc.sync.dma_start(
@@ -114,6 +113,7 @@ def tile_balanced_nonlocal_means_s12_kernel(
         )
         load_rows(b_rows_first, b_scales, 0, 512)
         load_rows(a_plane[0], a_scales, 0, HALF)
+        nc.sync.dma_start(out=w_raw[:], in_=w.rearrange("(p j) c -> p j c", j=4))
         load_rows(b_rows_rest, b_scales, 512, N)
         load_codes(nc.sync, b_raw[1], b_words, 1024)
         nc.sync.dma_start(out=gam_x[:], in_=gamma.rearrange("(g m b) -> m g b", g=GROUPS, b=4))

@@ -40,7 +40,7 @@ def tile_balanced_nonlocal_means_s12_kernel(
             return keep.tile(shape, dtype, name=name, tag=name, align_bytes=64)
 
         a_codes = [kept("a_codes%d" % h, [P, DEPTH, 2 * HALF], U8) for h in range(2)]
-        a_plane = [kept("a_plane%d" % h, [P, DEPTH, HALF], U8) for h in range(2)]
+        a_plane = kept("a_plane", [P, DEPTH, M], U8)
         b_raw = [kept("b_raw%d" % g, [P, DEPTH, 1024], U8) for g in range(2)]
         b_raw_late = kept("b_raw_late", [P, DEPTH, 2048], U8)
         b_rows_first = kept("b_rows_first", [P, DEPTH, 512], U8)
@@ -99,9 +99,8 @@ def tile_balanced_nonlocal_means_s12_kernel(
 
         nc.vector.memset(gam_raw[:], 0.0)
         nc.vector.memset(b_rows_first[:].bitcast(I32), 0)
-        nc.vector.memset(a_plane[0][:].bitcast(I32), 0)
+        nc.vector.memset(a_plane[:].bitcast(I32), 0)
         nc.vector.memset(b_rows_rest[:].bitcast(I32), 0)
-        nc.vector.memset(a_plane[1][:].bitcast(I32), 0)
 
         load_codes(nc.gpsimd, a_codes[0], a_words, 0)
         make_identity(nc, ident[:])
@@ -112,18 +111,17 @@ def tile_balanced_nonlocal_means_s12_kernel(
             in_=gamma.rearrange("(g q n) -> q g n", g=GROUPS, q=4),
         )
         load_rows(b_rows_first, b_scales, 0, 512)
-        load_rows(a_plane[0], a_scales, 0, HALF)
+        load_rows(a_plane, a_scales, 0, M)
+        load_codes(nc.sync, a_codes[1], a_words, 1024)
         nc.sync.dma_start(out=w_raw[:], in_=w.rearrange("(p j) c -> p j c", j=4))
-        load_rows(b_rows_rest, b_scales, 512, N)
-        load_codes(nc.sync, b_raw[1], b_words, 1024)
         nc.sync.dma_start(out=gam_x[:], in_=gamma.rearrange("(g m b) -> m g b", g=GROUPS, b=4))
         load_x(0)
         load_x(1)
+        load_rows(b_rows_rest, b_scales, 512, N)
+        load_codes(nc.sync, b_raw[1], b_words, 1024)
         load_codes(nc.sync, b_raw_late, b_words, 2048)
         load_x(2)
         load_x(3)
-        load_codes(nc.sync, a_codes[1], a_words, 1024)
-        load_rows(a_plane[1], a_scales, HALF, M)
         with nc.allow_non_contiguous_dma(reason="one rho value a pixel, onto the partition of its output row"):
             nc.sync.dma_start(out=rho_raw[:, :, 0], in_=rho.rearrange("(k p) -> p k", p=P))
 
@@ -186,7 +184,7 @@ def tile_balanced_nonlocal_means_s12_kernel(
                     lhsT=b_codes[g][:, d, 256 * t : 256 * (t + 1)].bitcast(E2M1),
                     lhsT_scale=b_plane[g][:, d, P * t : P * (t + 1)],
                     rhs=a_codes[h][:, d, :].bitcast(E2M1),
-                    rhs_scale=a_plane[h][:, d, :],
+                    rhs_scale=a_plane[:, d, HALF * h : HALF * (h + 1)],
                     start=(d == 0),
                     stop=(d == DEPTH - 1),
                 )
@@ -262,8 +260,8 @@ def tile_balanced_nonlocal_means_s12_kernel(
                 lambda: quantize(e_codes[s], e_plane[s], e_grp[s]),
             ]
 
-        def half(s, h):
-            return lambda: interleave(e_grp[s], e_bf[s], 256 * h, 256 * (h + 1))
+        def half(s, h, copy=nc.vector.tensor_copy):
+            return lambda: interleave(e_grp[s], e_bf[s], 256 * h, 256 * (h + 1), copy)
 
         def q_x(g):
             return lambda: quantize(x_codes[g], x_plane[g], x_grp[g])
@@ -278,7 +276,6 @@ def tile_balanced_nonlocal_means_s12_kernel(
             nc.vector.tensor_scalar(
                 out=half_sign[:], in0=gam_x[:].rearrange("m g b -> m (g b)"), scalar1=0.0, scalar2=0.5, op0=ALU.is_ge, op1=ALU.subtract
             )
-            arrange(b_codes_early[1], b_raw[1], 4)
             quantize(w_codes, w_plane, w_grp)
 
         def take_rho():
@@ -288,46 +285,48 @@ def tile_balanced_nonlocal_means_s12_kernel(
         vector_after = {
             3: [
                 lambda: interleave(w_grp, w_raw),
-                lambda: arrange(b_plane_rest, b_rows_rest, 2),
                 signs,
                 srt(0),
                 srt(1),
+                half(0, 0),
             ],
-            5: [half(0, 0), lambda: arrange(b_codes_late, b_raw_late, 4)],
-            6: [q_x(0)],
-            7: [half(0, 1)],
-            9: [q_x(1)],
-            10: [e[0][1], srt(2)],
-            11: [e[1][0]],
-            12: [srt(3)],
-            16: [q_v(0), e[1][1], q_v(1)],
-            17: [q_x(2), e[2][0]],
-            19: [e[2][1]],
-            20: [q_x(3)],
-            21: [e[3][0]],
-            23: [e[3][1]],
-            24: [q_v(2)],
-            27: [take_rho, q_v(3), e[4][0]],
-            28: [e[5][0], e[4][1]],
-            29: [e[6][0], e[5][1]],
-            30: [e[6][1]],
+            7: [lambda: arrange(b_plane_rest, b_rows_rest, 2), lambda: arrange(b_codes_early[1], b_raw[1], 4), half(0, 1)],
+            8: [q_x(0), lambda: arrange(b_codes_late, b_raw_late, 4)],
+            9: [e[0][1]],
+            11: [q_x(1)],
+            12: [srt(2)],
+            13: [e[1][0]],
+            14: [srt(3)],
+            16: [e[1][1]],
+            18: [q_v(0), q_v(1), half(4, 0)],
+            19: [q_x(2), e[2][0]],
+            21: [q_x(3)],
+            22: [e[2][1]],
+            23: [e[3][0]],
+            25: [e[3][1]],
+            26: [q_v(2)],
+            27: [half(4, 1)],
+            29: [take_rho, q_v(3), e[5][0], e[4][1]],
+            30: [half(6, 1, nc.scalar.copy), half(6, 0), e[5][1]],
+            31: [e[6][1]],
         }
-        early = [(k, g) for k in range(TILES) for g in range(GROUPS)]
+        order = [0, 4, 1, 2, 3, 5, 6, 7]
+        early = [(k, g) for k in range(3) for g in range(3)] + [(k, 3) for k in range(3)] + [(3, g) for g in range(GROUPS)]
         for slot in range(4 * STEPS):
-            weigh(*divmod(slot, 4))
+            weigh(order[slot // 4], slot % 4)
             for job in vector_after.get(slot, []):
                 job()
-            if 8 <= slot < 16:
-                project(*divmod(slot - 8, 4))
-            if 19 <= slot < 27:
-                project(*divmod(slot - 11, 4))
-            if slot >= 28:
-                for k, g in early[3 * (slot - 28) : 3 * (slot - 27)]:
+            if 10 <= slot < 18:
+                project(*divmod(slot - 10, 4))
+            if 21 <= slot < 29:
+                project(*divmod(slot - 13, 4))
+            if slot >= 29:
+                for k, g in early[3 * (slot - 29) : 3 * (slot - 28)]:
                     average(k, g)
                     if g == GROUPS - 1:
                         finish(k, False)
-            if slot in (5, 16):
-                pair = (0, 1) if slot == 5 else (2, 3)
+            if slot in (7, 18):
+                pair = (0, 1) if slot == 7 else (2, 3)
                 for g in pair:
                     turn_x(g)
                 for g in pair:
@@ -335,9 +334,10 @@ def tile_balanced_nonlocal_means_s12_kernel(
 
         last = STEPS - 1
         interleave(e_grp[last], e_bf[last], 0, 256)
-        for g in range(GROUPS):
-            average(3, g)
-        finish(3, False)
+        for k, g in early[9:]:
+            average(k, g)
+            if g == GROUPS - 1:
+                finish(k, False)
         for k in (4, 5):
             for g in range(GROUPS - 1):
                 average(k, g)

@@ -23,7 +23,8 @@ HALF = 512
 DEPTH = D // 512
 TILES = HALF // P
 STEPS = 2 * GROUPS
-SCALAR_QUARTERS = [(1,), (0, 2), (1,), (0, 2)]
+SORTED = (0, 1, 3)
+SCALAR_QUARTERS = [(1,), (0, 2), (), (0, 1, 2, 3)]
 
 
 def tile_balanced_nonlocal_means_s12_kernel(
@@ -52,7 +53,7 @@ def tile_balanced_nonlocal_means_s12_kernel(
         b_plane_rest = kept("b_plane_rest", [P, DEPTH, N - 512], U8)
         b_plane = [b_plane_first[:]] + [b_plane_rest[:, :, 512 * g : 512 * (g + 1)] for g in range(GROUPS - 1)]
         x_raw = [kept("x_raw%d" % g, [P, 4, F], BF16) for g in range(GROUPS)]
-        x_sorted = [kept("x_sorted%d" % g, [P, 4, F], BF16) for g in range(GROUPS)]
+        x_sorted = {g: kept("x_sorted%d" % g, [P, 4, F], BF16) for g in SORTED}
         x_grp = [kept("x_grp%d" % g, [P, 512, 4], BF16) for g in range(GROUPS)]
         x_codes = [kept("x_codes%d" % g, [P, 512], U32) for g in range(GROUPS)]
         x_plane = [kept("x_plane%d" % g, [P, 512], U8) for g in range(GROUPS)]
@@ -79,6 +80,8 @@ def tile_balanced_nonlocal_means_s12_kernel(
         mant_ln = kept("mant_ln", [P, 16], F32)
         ln_gam = kept("ln_gam", [P, 16], F32)
         half_sign = kept("half_sign", [P, 16], F32)
+        twice_pos = kept("twice_pos", [P, 16], F32)
+        sign = kept("sign", [P, GROUPS, 4], F32)
         ident = kept("ident", [P, P], F32)
 
         def load_codes(queue, tile, words, first):
@@ -102,8 +105,6 @@ def tile_balanced_nonlocal_means_s12_kernel(
         nc.vector.memset(a_plane[:].bitcast(I32), 0)
         nc.vector.memset(b_rows_rest[:].bitcast(I32), 0)
 
-        load_codes(nc.gpsimd, a_codes[0], a_words, 0)
-        make_identity(nc, ident[:])
 
         load_codes(nc.sync, b_raw[0], b_words, 0)
         nc.sync.dma_start(
@@ -112,8 +113,10 @@ def tile_balanced_nonlocal_means_s12_kernel(
         )
         load_rows(b_rows_first, b_scales, 0, 512)
         load_rows(a_plane, a_scales, 0, M)
-        load_codes(nc.sync, a_codes[1], a_words, 1024)
+        load_codes(nc.gpsimd, a_codes[0], a_words, 0)
+        make_identity(nc, ident[:])
         nc.sync.dma_start(out=w_raw[:], in_=w.rearrange("(p j) c -> p j c", j=4))
+        load_codes(nc.sync, a_codes[1], a_words, 1024)
         nc.sync.dma_start(out=gam_x[:], in_=gamma.rearrange("(g m b) -> m g b", g=GROUPS, b=4))
         load_x(0)
         load_x(1)
@@ -150,9 +153,11 @@ def tile_balanced_nonlocal_means_s12_kernel(
                 x_banks[g, k] = bank
                 for row in range(2):
                     for u in range(2):
-                        nc.tensor.transpose(
-                            bank[:, 2 * row + u, :], x_sorted[g][:, 2 * k + row, :].bitcast(F32)[:, P * u : P * (u + 1)], ident[:]
-                        )
+                        if g in SORTED:
+                            words = x_sorted[g][:, 2 * k + row, :].bitcast(F32)[:, P * u : P * (u + 1)]
+                        else:
+                            words = x_raw[g][:, 2 * k + row, :].bitcast(F32)[:, u::2]
+                        nc.tensor.transpose(bank[:, 2 * row + u, :], words, ident[:])
 
         def take_x(g, copy):
             words = x_grp[g][:].rearrange("p c j -> p (c j)").bitcast(F32)
@@ -205,8 +210,16 @@ def tile_balanced_nonlocal_means_s12_kernel(
                     start=True,
                     stop=True,
                 )
-            copy = nc.scalar.copy if quarter in SCALAR_QUARTERS[g] else nc.vector.tensor_copy
-            copy(out=v_grp[g][:, cols, :], in_=bank[:].rearrange("p t c -> p c t"))
+            if g in SORTED:
+                copy = nc.scalar.copy if quarter in SCALAR_QUARTERS[g] else nc.vector.tensor_copy
+                copy(out=v_grp[g][:, cols, :], in_=bank[:].rearrange("p t c -> p c t"))
+            else:
+                nc.vector.tensor_tensor(
+                    out=v_grp[g][:, cols, :],
+                    in0=bank[:].rearrange("p t c -> p c t"),
+                    in1=sign[:, g : g + 1, :].to_broadcast([P, P, 4]),
+                    op=ALU.mult,
+                )
 
         o_bank = {}
 
@@ -250,8 +263,12 @@ def tile_balanced_nonlocal_means_s12_kernel(
         )
         nc.scalar.activation(out=mant_ln[:], in_=mant[:].bitcast(F32), func=ACT.Ln)
         nc.vector.tensor_scalar(
+            out=twice_pos[:], in0=gam_t[:, 0:512:32], scalar1=0.0, scalar2=2.0, op0=ALU.is_ge, op1=ALU.mult
+        )
+        nc.vector.tensor_scalar(
             out=expo_ln[:], in0=expo[:], scalar1=-127.0, scalar2=math.log(2.0), op0=ALU.add, op1=ALU.mult
         )
+        nc.vector.tensor_scalar_add(out=sign[:].rearrange("p g t -> p (g t)"), in0=twice_pos[:], scalar1=-1.0)
         nc.vector.tensor_tensor(out=ln_gam[:], in0=mant_ln[:], in1=expo_ln[:], op=ALU.add)
 
         def e_jobs(s):
@@ -290,24 +307,22 @@ def tile_balanced_nonlocal_means_s12_kernel(
                 srt(1),
                 half(0, 0),
             ],
-            7: [lambda: arrange(b_plane_rest, b_rows_rest, 2), lambda: arrange(b_codes_early[1], b_raw[1], 4), half(0, 1)],
+            7: [lambda: arrange(b_plane_rest, b_rows_rest, 2), lambda: arrange(b_codes_early[1], b_raw[1], 4), half(0, 1), half(4, 0)],
             8: [q_x(0), lambda: arrange(b_codes_late, b_raw_late, 4)],
             9: [e[0][1]],
             11: [q_x(1)],
-            12: [srt(2)],
+            12: [half(4, 1)],
             13: [e[1][0]],
             14: [srt(3)],
-            16: [e[1][1]],
-            18: [q_v(0), q_v(1), half(4, 0)],
-            19: [q_x(2), e[2][0]],
-            21: [q_x(3)],
-            22: [e[2][1]],
-            23: [e[3][0]],
-            25: [e[3][1]],
-            26: [q_v(2)],
-            27: [half(4, 1)],
-            29: [take_rho, q_v(3), e[5][0], e[4][1]],
-            30: [half(6, 1, nc.scalar.copy), half(6, 0), e[5][1]],
+            16: [e[4][1]],
+            19: [q_v(0), q_x(2), e[1][1]],
+            20: [e[2][0]],
+            22: [q_x(3)],
+            23: [q_v(1)],
+            24: [half(5, 0, nc.scalar.copy)],
+            25: [e[2][1], q_v(2), e[3][0]],
+            27: [half(5, 1), e[3][1]],
+            29: [take_rho, q_v(3), e[6][0], e[5][1]],
             31: [e[6][1]],
         }
         order = [0, 4, 1, 2, 3, 5, 6, 7]
@@ -330,7 +345,7 @@ def tile_balanced_nonlocal_means_s12_kernel(
                 for g in pair:
                     turn_x(g)
                 for g in pair:
-                    take_x(g, nc.scalar.copy)
+                    take_x(g, nc.vector.tensor_copy if g == 2 else nc.scalar.copy)
 
         last = STEPS - 1
         interleave(e_grp[last], e_bf[last], 0, 256)

@@ -240,7 +240,7 @@ def tile_balanced_nonlocal_means_s12_kernel(
             )
 
         def finish(k, on_vector, first=0, last=C):
-            res = work.tile([P, last - first], F32, name="res", tag="res", bufs=9)
+            res = work.tile([P, last - first], F32, name="res", tag="res", bufs=11)
             if on_vector:
                 nc.vector.tensor_scalar_mul(out=res[:], in0=o_bank[k, first][:], scalar1=rho_col[:, k : k + 1])
             else:
@@ -322,8 +322,7 @@ def tile_balanced_nonlocal_means_s12_kernel(
             24: [half(5, 0, nc.scalar.copy)],
             25: [e[2][1], q_v(2), e[3][0]],
             27: [half(5, 1), e[3][1]],
-            29: [take_rho, q_v(3), e[6][0], e[5][1]],
-            31: [e[6][1]],
+            29: [take_rho, q_v(3), half(6, 0), e[5][1]],
         }
         order = [0, 4, 1, 2, 3, 5, 6, 7]
         early = [(k, g) for k in range(3) for g in range(3)] + [(k, 3) for k in range(3)] + [(3, g) for g in range(GROUPS)]
@@ -348,26 +347,19 @@ def tile_balanced_nonlocal_means_s12_kernel(
                     take_x(g, nc.vector.tensor_copy if g == 2 else nc.scalar.copy)
 
         last = STEPS - 1
-        interleave(e_grp[last], e_bf[last], 0, 256)
+        half(last, 0)()
+        for s in (last - 1, last):
+            quantize(e_codes[s], e_plane[s], e_grp[s], 0, 256)
+        for s in (last - 1, last):
+            half(s, 1)()
+        for s in (last - 1, last):
+            quantize(e_codes[s], e_plane[s], e_grp[s], 256, 512)
         for k, g in early[9:]:
             average(k, g)
             if g == GROUPS - 1:
                 finish(k, False)
-        for k in (4, 5):
-            for g in range(GROUPS - 1):
-                average(k, g)
-        quantize(e_codes[last], e_plane[last], e_grp[last], 0, 256)
-        interleave(e_grp[last], e_bf[last], 256, 512)
-        for k in (4, 5):
-            average(k, GROUPS - 1)
-        quantize(e_codes[last], e_plane[last], e_grp[last], 256, 512)
-        finish(4, False)
-        finish(5, False)
-        for g in range(GROUPS):
-            average(6, g)
-        finish(6, True)
-        for first in (0, 256):
+        pieces = [(4, 0, C), (5, 0, C), (6, 0, 256), (6, 256, C), (7, 0, 256), (7, 256, 384), (7, 384, C)]
+        for n, (k, first, end) in enumerate(pieces):
             for g in range(GROUPS):
-                average(7, g, first, first + 256)
-        finish(7, False, 0, 256)
-        finish(7, True, 256, 512)
+                average(k, g, first, end)
+            finish(k, n >= 2 and n % 2 == 0, first, end)

@@ -90,8 +90,8 @@ def tile_balanced_nonlocal_means_s12_kernel(
                 in_=words.rearrange("d p n -> p d n")[:, :, first : first + tile.shape[2]].bitcast(I32),
             )
 
-        def load_rows(plane, rows, first, last):
-            for q in range(4):
+        def load_rows(plane, rows, first, last, quadrants=range(4)):
+            for q in quadrants:
                 nc.sync.dma_start(
                     out=plane[32 * q : 32 * q + 4, :, :].bitcast(I32),
                     in_=rows[:, 4 * q : 4 * q + 4, first:last].rearrange("d r n -> r d n").bitcast(I32),
@@ -100,20 +100,22 @@ def tile_balanced_nonlocal_means_s12_kernel(
         def load_x(g):
             nc.sync.dma_start(out=x_raw[g][:], in_=x.rearrange("(g m b) f -> g m b f", g=GROUPS, b=4)[g])
 
-        nc.vector.memset(gam_raw[:], 0.0)
-        nc.vector.memset(b_rows_first[:].bitcast(I32), 0)
+        nc.gpsimd.memset(gam_raw[:].bitcast(I32), 0)
+        nc.gpsimd.memset(b_rows_first[:].bitcast(I32), 0)
         nc.vector.memset(a_plane[:].bitcast(I32), 0)
         nc.vector.memset(b_rows_rest[:].bitcast(I32), 0)
 
 
-        load_codes(nc.sync, b_raw[0], b_words, 0)
         nc.sync.dma_start(
             out=gam_raw[0:P:32, :].rearrange("q (g n) -> q g n", g=GROUPS),
             in_=gamma.rearrange("(g q n) -> q g n", g=GROUPS, q=4),
         )
-        load_rows(b_rows_first, b_scales, 0, 512)
-        load_rows(a_plane, a_scales, 0, M)
-        load_codes(nc.gpsimd, a_codes[0], a_words, 0)
+        load_rows(b_rows_first, b_scales, 0, 512, (0, 1, 2))
+        load_codes(nc.sync, b_raw[0], b_words, 0)
+        load_rows(b_rows_first, b_scales, 0, 512, (3,))
+        load_rows(a_plane, a_scales, 0, M, (0,))
+        load_codes(nc.sync, a_codes[0], a_words, 0)
+        load_rows(a_plane, a_scales, 0, M, (1, 2, 3))
         make_identity(nc, ident[:])
         nc.sync.dma_start(out=w_raw[:], in_=w.rearrange("(p j) c -> p j c", j=4))
         load_codes(nc.sync, a_codes[1], a_words, 1024)
@@ -251,9 +253,8 @@ def tile_balanced_nonlocal_means_s12_kernel(
             out=gam_rows[:].rearrange("p (g t q r) -> p g t q r", g=GROUPS, t=4, q=4),
             in_=gam_raw[:].rearrange("p (g q t r) -> p g t q r", g=GROUPS, q=4, t=4),
         )
-        arrange(b_codes_early[0], b_raw[0], 4)
         nc.vector.transpose(out=gam_t[:], in_=gam_rows[:])
-        arrange(b_plane_first, b_rows_first, 2)
+        arrange(b_codes_early[0], b_raw[0], 4)
         bits = gam_t[:].bitcast(I32)[:, 0:512:32]
         nc.vector.tensor_scalar(
             out=mant[:], in0=bits, scalar1=0x007FFFFF, scalar2=0x3F800000, op0=ALU.bitwise_and, op1=ALU.bitwise_or
@@ -261,6 +262,7 @@ def tile_balanced_nonlocal_means_s12_kernel(
         nc.vector.tensor_scalar(
             out=expo[:], in0=bits, scalar1=23, scalar2=0xFF, op0=ALU.logical_shift_right, op1=ALU.bitwise_and
         )
+        arrange(b_plane_first, b_rows_first, 2)
         nc.scalar.activation(out=mant_ln[:], in_=mant[:].bitcast(F32), func=ACT.Ln)
         nc.vector.tensor_scalar(
             out=twice_pos[:], in0=gam_t[:, 0:512:32], scalar1=0.0, scalar2=2.0, op0=ALU.is_ge, op1=ALU.mult

@@ -45,13 +45,15 @@ def tile_balanced_nonlocal_means_s12_kernel(
         b_raw = [kept("b_raw%d" % g, [P, DEPTH, 1024], U8) for g in range(2)]
         b_raw_late = kept("b_raw_late", [P, DEPTH, 2048], U8)
         b_rows_first = kept("b_rows_first", [P, DEPTH, 512], U8)
-        b_rows_rest = kept("b_rows_rest", [P, DEPTH, N - 512], U8)
+        b_rows_second = kept("b_rows_second", [P, DEPTH, 512], U8)
+        b_rows_late = kept("b_rows_late", [P, DEPTH, 1024], U8)
         b_codes_early = [kept("b_codes%d" % g, [P, DEPTH, 1024], U8) for g in range(2)]
         b_codes_late = kept("b_codes_late", [P, DEPTH, 2048], U8)
         b_codes = [b_codes_early[0][:], b_codes_early[1][:], b_codes_late[:, :, 0:1024], b_codes_late[:, :, 1024:2048]]
         b_plane_first = kept("b_plane_first", [P, DEPTH, 512], U8)
-        b_plane_rest = kept("b_plane_rest", [P, DEPTH, N - 512], U8)
-        b_plane = [b_plane_first[:]] + [b_plane_rest[:, :, 512 * g : 512 * (g + 1)] for g in range(GROUPS - 1)]
+        b_plane_second = kept("b_plane_second", [P, DEPTH, 512], U8)
+        b_plane_late = kept("b_plane_late", [P, DEPTH, 1024], U8)
+        b_plane = [b_plane_first[:], b_plane_second[:], b_plane_late[:, :, 0:512], b_plane_late[:, :, 512:1024]]
         x_raw = [kept("x_raw%d" % g, [P, 4, F], BF16) for g in range(GROUPS)]
         x_sorted = {g: kept("x_sorted%d" % g, [P, 4, F], BF16) for g in SORTED}
         x_grp = [kept("x_grp%d" % g, [P, 512, 4], BF16) for g in range(GROUPS)]
@@ -70,7 +72,8 @@ def tile_balanced_nonlocal_means_s12_kernel(
         e_plane = [kept("e_plane%d" % s, [P, HALF], U8) for s in range(STEPS)]
         gam_raw = kept("gam_raw", [P, 512], BF16)
         rho_raw = kept("rho_raw", [P, M // P, 2], BF16)
-        gam_x = kept("gam_x", [P, GROUPS, 4], BF16)
+        gam_by_row = kept("gam_by_row", [P, 512], BF16)
+        gam_x = kept("gam_x", [P, 512], BF16)
         gam_rows = kept("gam_rows", [P, 512], F32)
         gam_t = kept("gam_t", [P, 512], F32)
         rho_col = kept("rho_col", [P, M // P], F32)
@@ -103,27 +106,27 @@ def tile_balanced_nonlocal_means_s12_kernel(
         nc.gpsimd.memset(gam_raw[:].bitcast(I32), 0)
         nc.gpsimd.memset(b_rows_first[:].bitcast(I32), 0)
         nc.vector.memset(a_plane[:].bitcast(I32), 0)
-        nc.vector.memset(b_rows_rest[:].bitcast(I32), 0)
+        nc.vector.memset(b_rows_second[:].bitcast(I32), 0)
+        nc.vector.memset(b_rows_late[:].bitcast(I32), 0)
 
 
+        load_codes(nc.sync, b_raw[0], b_words, 0)
         nc.sync.dma_start(
             out=gam_raw[0:P:32, :].rearrange("q (g n) -> q g n", g=GROUPS),
             in_=gamma.rearrange("(g q n) -> q g n", g=GROUPS, q=4),
         )
-        load_rows(b_rows_first, b_scales, 0, 512, (0, 1, 2))
-        load_codes(nc.sync, b_raw[0], b_words, 0)
-        load_rows(b_rows_first, b_scales, 0, 512, (3,))
+        load_rows(b_rows_first, b_scales, 0, 512)
         load_rows(a_plane, a_scales, 0, M, (0,))
         load_codes(nc.sync, a_codes[0], a_words, 0)
         load_rows(a_plane, a_scales, 0, M, (1, 2, 3))
         make_identity(nc, ident[:])
         nc.sync.dma_start(out=w_raw[:], in_=w.rearrange("(p j) c -> p j c", j=4))
         load_codes(nc.sync, a_codes[1], a_words, 1024)
-        nc.sync.dma_start(out=gam_x[:], in_=gamma.rearrange("(g m b) -> m g b", g=GROUPS, b=4))
         load_x(0)
         load_x(1)
-        load_rows(b_rows_rest, b_scales, 512, N)
+        load_rows(b_rows_second, b_scales, 512, 1024)
         load_codes(nc.sync, b_raw[1], b_words, 1024)
+        load_rows(b_rows_late, b_scales, 1024, N)
         load_codes(nc.sync, b_raw_late, b_words, 2048)
         load_x(2)
         load_x(3)
@@ -253,8 +256,9 @@ def tile_balanced_nonlocal_means_s12_kernel(
             out=gam_rows[:].rearrange("p (g t q r) -> p g t q r", g=GROUPS, t=4, q=4),
             in_=gam_raw[:].rearrange("p (g q t r) -> p g t q r", g=GROUPS, q=4, t=4),
         )
-        nc.vector.transpose(out=gam_t[:], in_=gam_rows[:])
         arrange(b_codes_early[0], b_raw[0], 4)
+        nc.vector.transpose(out=gam_t[:], in_=gam_rows[:])
+        arrange(b_plane_first, b_rows_first, 2)
         bits = gam_t[:].bitcast(I32)[:, 0:512:32]
         nc.vector.tensor_scalar(
             out=mant[:], in0=bits, scalar1=0x007FFFFF, scalar2=0x3F800000, op0=ALU.bitwise_and, op1=ALU.bitwise_or
@@ -262,7 +266,6 @@ def tile_balanced_nonlocal_means_s12_kernel(
         nc.vector.tensor_scalar(
             out=expo[:], in0=bits, scalar1=23, scalar2=0xFF, op0=ALU.logical_shift_right, op1=ALU.bitwise_and
         )
-        arrange(b_plane_first, b_rows_first, 2)
         nc.scalar.activation(out=mant_ln[:], in_=mant[:].bitcast(F32), func=ACT.Ln)
         nc.vector.tensor_scalar(
             out=twice_pos[:], in0=gam_t[:, 0:512:32], scalar1=0.0, scalar2=2.0, op0=ALU.is_ge, op1=ALU.mult
@@ -271,7 +274,13 @@ def tile_balanced_nonlocal_means_s12_kernel(
             out=expo_ln[:], in0=expo[:], scalar1=-127.0, scalar2=math.log(2.0), op0=ALU.add, op1=ALU.mult
         )
         nc.vector.tensor_scalar_add(out=sign[:].rearrange("p g t -> p (g t)"), in0=twice_pos[:], scalar1=-1.0)
+        nc.vector.tensor_copy(
+            out=gam_by_row[:].rearrange("p (g b m) -> p g b m", g=GROUPS, b=4),
+            in_=gam_raw[:].rearrange("p (g m b) -> p g b m", g=GROUPS, b=4),
+        )
         nc.vector.tensor_tensor(out=ln_gam[:], in0=mant_ln[:], in1=expo_ln[:], op=ALU.add)
+
+        nc.vector.transpose(out=gam_x[:], in_=gam_by_row[:])
 
         def e_jobs(s):
             return [
@@ -293,7 +302,7 @@ def tile_balanced_nonlocal_means_s12_kernel(
 
         def signs():
             nc.vector.tensor_scalar(
-                out=half_sign[:], in0=gam_x[:].rearrange("m g b -> m (g b)"), scalar1=0.0, scalar2=0.5, op0=ALU.is_ge, op1=ALU.subtract
+                out=half_sign[:], in0=gam_x[:, 0:512:32], scalar1=0.0, scalar2=0.5, op0=ALU.is_ge, op1=ALU.subtract
             )
             quantize(w_codes, w_plane, w_grp)
 
@@ -306,18 +315,18 @@ def tile_balanced_nonlocal_means_s12_kernel(
                 lambda: interleave(w_grp, w_raw),
                 signs,
                 srt(0),
-                srt(1),
                 half(0, 0),
+                srt(1),
             ],
-            7: [lambda: arrange(b_plane_rest, b_rows_rest, 2), lambda: arrange(b_codes_early[1], b_raw[1], 4), half(0, 1), half(4, 0)],
-            8: [q_x(0), lambda: arrange(b_codes_late, b_raw_late, 4)],
+            7: [lambda: arrange(b_plane_second, b_rows_second, 2), lambda: arrange(b_codes_early[1], b_raw[1], 4), half(0, 1), half(4, 0)],
+            8: [q_x(0), lambda: arrange(b_plane_late, b_rows_late, 2), lambda: arrange(b_codes_late, b_raw_late, 4)],
             9: [e[0][1]],
             11: [q_x(1)],
             12: [half(4, 1)],
             13: [e[1][0]],
             14: [srt(3)],
             16: [e[4][1]],
-            19: [q_v(0), q_x(2), e[1][1]],
+            19: [q_x(2), q_v(0), e[1][1]],
             20: [e[2][0]],
             22: [q_x(3)],
             23: [q_v(1)],

@@ -18,13 +18,20 @@ ALU = mybir.AluOpType
 ACT = mybir.ActivationFunctionType
 
 P = 128
-GROUPS = N // 512
-HALF = 512
-DEPTH = D // 512
+PASS = 512
+GROUPS = N // PASS
+HALF = M // 2
+DEPTH = D // PASS
 TILES = HALF // P
 STEPS = 2 * GROUPS
+SLOTS = 4 * STEPS
+
+FIRST_TURN, SECOND_TURN = 7, 18
+V_LAG = 3
 SORTED = (0, 1, 3)
-SCALAR_QUARTERS = [(1,), (0, 2), (), (0, 1, 2, 3)]
+LAST_SORT = 14
+SCALAR_QUARTERS = ((1, 3), (0, 2), (), (0, 1, 2, 3))
+OUT_PASSES = 3
 
 
 def tile_balanced_nonlocal_means_s12_kernel(
@@ -42,23 +49,23 @@ def tile_balanced_nonlocal_means_s12_kernel(
 
         a_codes = [kept("a_codes%d" % h, [P, DEPTH, 2 * HALF], U8) for h in range(2)]
         a_plane = kept("a_plane", [P, DEPTH, M], U8)
-        b_raw = [kept("b_raw%d" % g, [P, DEPTH, 1024], U8) for g in range(2)]
-        b_raw_late = kept("b_raw_late", [P, DEPTH, 2048], U8)
-        b_rows_first = kept("b_rows_first", [P, DEPTH, 512], U8)
-        b_rows_second = kept("b_rows_second", [P, DEPTH, 512], U8)
-        b_rows_late = kept("b_rows_late", [P, DEPTH, 1024], U8)
-        b_codes_early = [kept("b_codes%d" % g, [P, DEPTH, 1024], U8) for g in range(2)]
-        b_codes_late = kept("b_codes_late", [P, DEPTH, 2048], U8)
-        b_codes = [b_codes_early[0][:], b_codes_early[1][:], b_codes_late[:, :, 0:1024], b_codes_late[:, :, 1024:2048]]
-        b_plane_first = kept("b_plane_first", [P, DEPTH, 512], U8)
-        b_plane_second = kept("b_plane_second", [P, DEPTH, 512], U8)
-        b_plane_late = kept("b_plane_late", [P, DEPTH, 1024], U8)
-        b_plane = [b_plane_first[:], b_plane_second[:], b_plane_late[:, :, 0:512], b_plane_late[:, :, 512:1024]]
+        b_raw = [kept("b_raw%d" % g, [P, DEPTH, 2 * PASS], U8) for g in range(2)]
+        b_raw_late = kept("b_raw_late", [P, DEPTH, 4 * PASS], U8)
+        b_rows_first = kept("b_rows_first", [P, DEPTH, PASS], U8)
+        b_rows_second = kept("b_rows_second", [P, DEPTH, PASS], U8)
+        b_rows_late = kept("b_rows_late", [P, DEPTH, 2 * PASS], U8)
+        b_codes_early = [kept("b_codes%d" % g, [P, DEPTH, 2 * PASS], U8) for g in range(2)]
+        b_codes_late = kept("b_codes_late", [P, DEPTH, 4 * PASS], U8)
+        b_codes = [tile[:] for tile in b_codes_early] + [b_codes_late[:, :, 2 * PASS * g : 2 * PASS * (g + 1)] for g in range(2)]
+        b_plane_first = kept("b_plane_first", [P, DEPTH, PASS], U8)
+        b_plane_second = kept("b_plane_second", [P, DEPTH, PASS], U8)
+        b_plane_late = kept("b_plane_late", [P, DEPTH, 2 * PASS], U8)
+        b_plane = [b_plane_first[:], b_plane_second[:]] + [b_plane_late[:, :, PASS * g : PASS * (g + 1)] for g in range(2)]
         x_raw = [kept("x_raw%d" % g, [P, 4, F], BF16) for g in range(GROUPS)]
         x_sorted = {g: kept("x_sorted%d" % g, [P, 4, F], BF16) for g in SORTED}
-        x_grp = [kept("x_grp%d" % g, [P, 512, 4], BF16) for g in range(GROUPS)]
-        x_codes = [kept("x_codes%d" % g, [P, 512], U32) for g in range(GROUPS)]
-        x_plane = [kept("x_plane%d" % g, [P, 512], U8) for g in range(GROUPS)]
+        x_grp = [kept("x_grp%d" % g, [P, PASS, 4], BF16) for g in range(GROUPS)]
+        x_codes = [kept("x_codes%d" % g, [P, PASS], U32) for g in range(GROUPS)]
+        x_plane = [kept("x_plane%d" % g, [P, PASS], U8) for g in range(GROUPS)]
         w_raw = kept("w_raw", [P, 4, C], BF16)
         w_grp = kept("w_grp", [P, C, 4], BF16)
         w_codes = kept("w_codes", [P, C], U32)
@@ -70,25 +77,25 @@ def tile_balanced_nonlocal_means_s12_kernel(
         e_grp = [kept("e_grp%d" % s, [P, HALF, 4], BF16) for s in range(STEPS)]
         e_codes = [kept("e_codes%d" % s, [P, HALF], U32) for s in range(STEPS)]
         e_plane = [kept("e_plane%d" % s, [P, HALF], U8) for s in range(STEPS)]
-        gam_raw = kept("gam_raw", [P, 512], BF16)
+        gam_raw = kept("gam_raw", [P, PASS], BF16)
         rho_raw = kept("rho_raw", [P, M // P, 2], BF16)
-        gam_by_row = kept("gam_by_row", [P, 512], BF16)
-        gam_x = kept("gam_x", [P, 512], BF16)
-        gam_rows = kept("gam_rows", [P, 512], F32)
-        gam_t = kept("gam_t", [P, 512], F32)
+        gam_by_row = kept("gam_by_row", [P, PASS], BF16)
+        gam_x = kept("gam_x", [P, PASS], BF16)
+        gam_by_place = kept("gam_by_place", [P, PASS], F32)
+        gam_t = kept("gam_t", [P, PASS], F32)
         rho_col = kept("rho_col", [P, M // P], F32)
-        mant = kept("mant", [P, 16], I32)
-        expo = kept("expo", [P, 16], I32)
-        expo_ln = kept("expo_ln", [P, 16], F32)
-        mant_ln = kept("mant_ln", [P, 16], F32)
-        ln_gam = kept("ln_gam", [P, 16], F32)
-        half_sign = kept("half_sign", [P, 16], F32)
-        twice_pos = kept("twice_pos", [P, 16], F32)
+        mant = kept("mant", [P, 4 * GROUPS], I32)
+        expo = kept("expo", [P, 4 * GROUPS], I32)
+        expo_ln = kept("expo_ln", [P, 4 * GROUPS], F32)
+        mant_ln = kept("mant_ln", [P, 4 * GROUPS], F32)
+        ln_gam = kept("ln_gam", [P, 4 * GROUPS], F32)
+        half_sign = kept("half_sign", [P, 4 * GROUPS], F32)
+        twice_pos = kept("twice_pos", [P, 4 * GROUPS], F32)
         sign = kept("sign", [P, GROUPS, 4], F32)
         ident = kept("ident", [P, P], F32)
 
-        def load_codes(queue, tile, words, first):
-            queue.dma_start(
+        def load_codes(tile, words, first):
+            nc.sync.dma_start(
                 out=tile[:].bitcast(I32),
                 in_=words.rearrange("d p n -> p d n")[:, :, first : first + tile.shape[2]].bitcast(I32),
             )
@@ -109,25 +116,24 @@ def tile_balanced_nonlocal_means_s12_kernel(
         nc.vector.memset(b_rows_second[:].bitcast(I32), 0)
         nc.vector.memset(b_rows_late[:].bitcast(I32), 0)
 
-
-        load_codes(nc.sync, b_raw[0], b_words, 0)
+        load_codes(b_raw[0], b_words, 0)
         nc.sync.dma_start(
             out=gam_raw[0:P:32, :].rearrange("q (g n) -> q g n", g=GROUPS),
             in_=gamma.rearrange("(g q n) -> q g n", g=GROUPS, q=4),
         )
-        load_rows(b_rows_first, b_scales, 0, 512)
+        load_rows(b_rows_first, b_scales, 0, PASS)
         load_rows(a_plane, a_scales, 0, M, (0,))
-        load_codes(nc.sync, a_codes[0], a_words, 0)
+        load_codes(a_codes[0], a_words, 0)
         load_rows(a_plane, a_scales, 0, M, (1, 2, 3))
         make_identity(nc, ident[:])
         nc.sync.dma_start(out=w_raw[:], in_=w.rearrange("(p j) c -> p j c", j=4))
-        load_codes(nc.sync, a_codes[1], a_words, 1024)
+        load_codes(a_codes[1], a_words, 2 * HALF)
         load_x(0)
         load_x(1)
-        load_rows(b_rows_second, b_scales, 512, 1024)
-        load_codes(nc.sync, b_raw[1], b_words, 1024)
-        load_rows(b_rows_late, b_scales, 1024, N)
-        load_codes(nc.sync, b_raw_late, b_words, 2048)
+        load_rows(b_rows_second, b_scales, PASS, 2 * PASS)
+        load_codes(b_raw[1], b_words, 2 * PASS)
+        load_codes(b_raw_late, b_words, 4 * PASS)
+        load_rows(b_rows_late, b_scales, 2 * PASS, N)
         load_x(2)
         load_x(3)
         with nc.allow_non_contiguous_dma(reason="one rho value a pixel, onto the partition of its output row"):
@@ -159,28 +165,28 @@ def tile_balanced_nonlocal_means_s12_kernel(
                 for row in range(2):
                     for u in range(2):
                         if g in SORTED:
-                            words = x_sorted[g][:, 2 * k + row, :].bitcast(F32)[:, P * u : P * (u + 1)]
+                            pairs = x_sorted[g][:, 2 * k + row, :].bitcast(F32)[:, P * u : P * (u + 1)]
                         else:
-                            words = x_raw[g][:, 2 * k + row, :].bitcast(F32)[:, u::2]
-                        nc.tensor.transpose(bank[:, 2 * row + u, :], words, ident[:])
+                            pairs = x_raw[g][:, 2 * k + row, :].bitcast(F32)[:, u::2]
+                        nc.tensor.transpose(bank[:, 2 * row + u, :], pairs, ident[:])
 
         def take_x(g, copy):
-            words = x_grp[g][:].rearrange("p c j -> p (c j)").bitcast(F32)
+            pairs = x_grp[g][:].rearrange("p c j -> p (c j)").bitcast(F32)
             for k in range(2):
                 copy(
-                    out=words.rearrange("p (t q r e) -> p t q r e", t=4, r=2, e=8)[:, :, :, :, 4 * k : 4 * k + 4],
+                    out=pairs.rearrange("p (t q r e) -> p t q r e", t=4, r=2, e=8)[:, :, :, :, 4 * k : 4 * k + 4],
                     in_=x_banks[g, k][:].rearrange("p e (q t r) -> p t q r e", t=4, r=2),
                 )
 
-        def quantize(codes, plane, grouped, first=0, last=512):
+        def quantize(codes, plane, grouped, first=0, last=PASS):
             nc.vector.quantize_mx(
                 out=codes[:, first:last].bitcast(E4M3),
                 scales=plane[:, first:last],
                 in_=grouped[:, first:last, :].rearrange("p c t -> p (c t)"),
             )
 
-        def interleave(grouped, rows, first=0, last=512, copy=nc.vector.tensor_copy):
-            copy(
+        def interleave(grouped, rows, first=0, last=PASS):
+            nc.vector.tensor_copy(
                 out=grouped[:, first:last, :].rearrange("p (c i) t -> p c t i", i=4),
                 in_=rows[:, :, first:last].rearrange("p t (c i) -> p c t i", i=4),
             )
@@ -191,7 +197,7 @@ def tile_balanced_nonlocal_means_s12_kernel(
             for d in range(DEPTH):
                 nc.tensor.matmul_mx(
                     out=bank[:],
-                    lhsT=b_codes[g][:, d, 256 * t : 256 * (t + 1)].bitcast(E2M1),
+                    lhsT=b_codes[g][:, d, 2 * P * t : 2 * P * (t + 1)].bitcast(E2M1),
                     lhsT_scale=b_plane[g][:, d, P * t : P * (t + 1)],
                     rhs=a_codes[h][:, d, :].bitcast(E2M1),
                     rhs_scale=a_plane[:, d, HALF * h : HALF * (h + 1)],
@@ -244,8 +250,10 @@ def tile_balanced_nonlocal_means_s12_kernel(
                 stop=(g == GROUPS - 1),
             )
 
+        pieces = [(4, 0, C), (5, 0, C), (6, 0, 256), (6, 256, C), (7, 0, 256), (7, 256, 384), (7, 384, C)]
+
         def finish(k, on_vector, first=0, last=C):
-            res = work.tile([P, last - first], F32, name="res", tag="res", bufs=11)
+            res = work.tile([P, last - first], F32, name="res", tag="res", bufs=TILES + len(pieces))
             if on_vector:
                 nc.vector.tensor_scalar_mul(out=res[:], in0=o_bank[k, first][:], scalar1=rho_col[:, k : k + 1])
             else:
@@ -253,13 +261,13 @@ def tile_balanced_nonlocal_means_s12_kernel(
             nc.sync.dma_start(out=out[P * k : P * (k + 1), first:last], in_=res[:])
 
         nc.vector.tensor_copy(
-            out=gam_rows[:].rearrange("p (g t q r) -> p g t q r", g=GROUPS, t=4, q=4),
+            out=gam_by_place[:].rearrange("p (g t q r) -> p g t q r", g=GROUPS, t=4, q=4),
             in_=gam_raw[:].rearrange("p (g q t r) -> p g t q r", g=GROUPS, q=4, t=4),
         )
         arrange(b_codes_early[0], b_raw[0], 4)
-        nc.vector.transpose(out=gam_t[:], in_=gam_rows[:])
+        nc.vector.transpose(out=gam_t[:], in_=gam_by_place[:])
         arrange(b_plane_first, b_rows_first, 2)
-        bits = gam_t[:].bitcast(I32)[:, 0:512:32]
+        bits = gam_t[:].bitcast(I32)[:, 0:PASS:32]
         nc.vector.tensor_scalar(
             out=mant[:], in0=bits, scalar1=0x007FFFFF, scalar2=0x3F800000, op0=ALU.bitwise_and, op1=ALU.bitwise_or
         )
@@ -268,7 +276,7 @@ def tile_balanced_nonlocal_means_s12_kernel(
         )
         nc.scalar.activation(out=mant_ln[:], in_=mant[:].bitcast(F32), func=ACT.Ln)
         nc.vector.tensor_scalar(
-            out=twice_pos[:], in0=gam_t[:, 0:512:32], scalar1=0.0, scalar2=2.0, op0=ALU.is_ge, op1=ALU.mult
+            out=twice_pos[:], in0=gam_t[:, 0:PASS:32], scalar1=0.0, scalar2=2.0, op0=ALU.is_ge, op1=ALU.mult
         )
         nc.vector.tensor_scalar(
             out=expo_ln[:], in0=expo[:], scalar1=-127.0, scalar2=math.log(2.0), op0=ALU.add, op1=ALU.mult
@@ -279,98 +287,102 @@ def tile_balanced_nonlocal_means_s12_kernel(
             in_=gam_raw[:].rearrange("p (g m b) -> p g b m", g=GROUPS, b=4),
         )
         nc.vector.tensor_tensor(out=ln_gam[:], in0=mant_ln[:], in1=expo_ln[:], op=ALU.add)
-
         nc.vector.transpose(out=gam_x[:], in_=gam_by_row[:])
 
-        def e_jobs(s):
-            return [
-                lambda: interleave(e_grp[s], e_bf[s]),
-                lambda: quantize(e_codes[s], e_plane[s], e_grp[s]),
-            ]
+        order = [0, GROUPS] + list(range(1, GROUPS)) + list(range(GROUPS + 1, STEPS))
+        turns = {FIRST_TURN: (0, 1), SECOND_TURN: (2, 3)}
+        v_slot = [(FIRST_TURN, SECOND_TURN)[g // 2] + V_LAG + 4 * (g % 2) for g in range(GROUPS)]
+        out_slot = v_slot[-1] + 4
 
-        def half(s, h, copy=nc.vector.tensor_copy):
-            return lambda: interleave(e_grp[s], e_bf[s], 256 * h, 256 * (h + 1), copy)
+        def job(call, *args):
+            return lambda: call(*args)
 
-        def q_x(g):
-            return lambda: quantize(x_codes[g], x_plane[g], x_grp[g])
+        needed = {slot: [] for slot in range(SLOTS)}
+        needed[FIRST_TURN] += [
+            job(arrange, b_plane_second, b_rows_second, 2),
+            job(arrange, b_codes_early[1], b_raw[1], 4),
+        ]
+        for g in range(GROUPS):
+            needed[v_slot[g] - 2 - g % 2].append(job(quantize, x_codes[g], x_plane[g], x_grp[g]))
+        for g in range(GROUPS):
+            slot = v_slot[g] + 4 if g >= 2 else SECOND_TURN + 1 + 4 * g
+            needed[slot].append(job(quantize, v_codes[g], v_plane[g], v_grp[g]))
+        needed[FIRST_TURN + 1] += [
+            job(arrange, b_codes_late, b_raw_late, 4),
+            job(arrange, b_plane_late, b_rows_late, 2),
+        ]
+        needed[LAST_SORT].append(job(sort_x, GROUPS - 1))
 
-        def q_v(g):
-            return lambda: quantize(v_codes[g], v_plane[g], v_grp[g])
+        backlog = []
+        for n, s in enumerate(order[:-1]):
+            backlog.append((4 * n + 3, job(interleave, e_grp[s], e_bf[s], 0, HALF // 2)))
+            if n > 0:
+                before = order[n - 1]
+                backlog.append((0, job(quantize, e_codes[before], e_plane[before], e_grp[before])))
+            if n < STEPS - 2:
+                backlog.append((0, job(interleave, e_grp[s], e_bf[s], HALF // 2, HALF)))
 
-        def srt(g):
-            return lambda: sort_x(g)
+        room = {slot: 1 for slot in range(SLOTS)}
+        for slot in range(FIRST_TURN):
+            room[slot] = 0
+        room[4] = 1
+        room[FIRST_TURN] = 4
+        room[v_slot[1] + 3] = 0
+        room[SECOND_TURN] = 0
+        room[SECOND_TURN + 1] = 3
+        room[SECOND_TURN + 2] = 2
+        for quarter in range(4):
+            room[v_slot[2] + quarter] = 0
+            room[v_slot[3] + quarter] = 2 if quarter < 3 else 0
+        for slot in range(out_slot, SLOTS):
+            room[slot] = 3
 
-        def signs():
-            nc.vector.tensor_scalar(
-                out=half_sign[:], in0=gam_x[:, 0:512:32], scalar1=0.0, scalar2=0.5, op0=ALU.is_ge, op1=ALU.subtract
-            )
-            quantize(w_codes, w_plane, w_grp)
+        early = [(k, g) for k in range(TILES - 1) for g in range(GROUPS - 1)]
+        early += [(k, GROUPS - 1) for k in range(TILES - 1)] + [(TILES - 1, g) for g in range(GROUPS)]
 
-        def take_rho():
-            nc.scalar.copy(out=rho_col[:], in_=rho_raw[:, :, 0])
-
-        e = [e_jobs(s) for s in range(STEPS)]
-        vector_after = {
-            3: [
-                lambda: interleave(w_grp, w_raw),
-                signs,
-                srt(0),
-                half(0, 0),
-                srt(1),
-            ],
-            7: [lambda: arrange(b_plane_second, b_rows_second, 2), lambda: arrange(b_codes_early[1], b_raw[1], 4), half(0, 1), half(4, 0)],
-            8: [q_x(0), lambda: arrange(b_plane_late, b_rows_late, 2), lambda: arrange(b_codes_late, b_raw_late, 4)],
-            9: [e[0][1]],
-            11: [q_x(1)],
-            12: [half(4, 1)],
-            13: [e[1][0]],
-            14: [srt(3)],
-            16: [e[4][1]],
-            19: [q_x(2), q_v(0), e[1][1]],
-            20: [e[2][0]],
-            22: [q_x(3)],
-            23: [q_v(1)],
-            24: [half(5, 0, nc.scalar.copy)],
-            25: [e[2][1], q_v(2), e[3][0]],
-            27: [half(5, 1), e[3][1]],
-            29: [take_rho, q_v(3), half(6, 0), e[5][1]],
-        }
-        order = [0, 4, 1, 2, 3, 5, 6, 7]
-        early = [(k, g) for k in range(3) for g in range(3)] + [(k, 3) for k in range(3)] + [(3, g) for g in range(GROUPS)]
-        for slot in range(4 * STEPS):
+        for slot in range(SLOTS):
             weigh(order[slot // 4], slot % 4)
-            for job in vector_after.get(slot, []):
-                job()
-            if 10 <= slot < 18:
-                project(*divmod(slot - 10, 4))
-            if 21 <= slot < 29:
-                project(*divmod(slot - 13, 4))
-            if slot >= 29:
-                for k, g in early[3 * (slot - 29) : 3 * (slot - 28)]:
+            if slot == 3:
+                interleave(w_grp, w_raw)
+                nc.vector.tensor_scalar(
+                    out=half_sign[:], in0=gam_x[:, 0:PASS:32], scalar1=0.0, scalar2=0.5, op0=ALU.is_ge, op1=ALU.subtract
+                )
+                quantize(w_codes, w_plane, w_grp)
+                sort_x(0)
+            if slot == 5:
+                sort_x(1)
+            for call in needed[slot]:
+                call()
+            for n in range(room[slot] - len(needed[slot])):
+                if backlog and backlog[0][0] <= slot:
+                    backlog[0][1]()
+                    backlog = backlog[1:]
+            for g in range(GROUPS):
+                if 0 <= slot - v_slot[g] < 4:
+                    project(g, slot - v_slot[g])
+            if slot == out_slot:
+                nc.scalar.copy(out=rho_col[:], in_=rho_raw[:, :, 0])
+            if slot >= out_slot:
+                for k, g in early[OUT_PASSES * (slot - out_slot) : OUT_PASSES * (slot - out_slot + 1)]:
                     average(k, g)
-                    if g == GROUPS - 1:
-                        finish(k, False)
-            if slot in (7, 18):
-                pair = (0, 1) if slot == 7 else (2, 3)
-                for g in pair:
-                    turn_x(g)
-                for g in pair:
-                    take_x(g, nc.vector.tensor_copy if g == 2 else nc.scalar.copy)
+            for g in turns.get(slot, ()):
+                turn_x(g)
+            for g in turns.get(slot, ()):
+                take_x(g, nc.vector.tensor_copy if g == turns[SECOND_TURN][0] else nc.scalar.copy)
 
-        last = STEPS - 1
-        half(last, 0)()
-        for s in (last - 1, last):
-            quantize(e_codes[s], e_plane[s], e_grp[s], 0, 256)
-        for s in (last - 1, last):
-            half(s, 1)()
-        for s in (last - 1, last):
-            quantize(e_codes[s], e_plane[s], e_grp[s], 256, 512)
-        for k, g in early[9:]:
+        last_two = (STEPS - 2, STEPS - 1)
+        interleave(e_grp[STEPS - 1], e_bf[STEPS - 1], 0, HALF // 2)
+        for s in last_two:
+            quantize(e_codes[s], e_plane[s], e_grp[s], 0, HALF // 2)
+        for s in last_two:
+            interleave(e_grp[s], e_bf[s], HALF // 2, HALF)
+        for s in last_two:
+            quantize(e_codes[s], e_plane[s], e_grp[s], HALF // 2, HALF)
+        for k, g in early[OUT_PASSES * (SLOTS - out_slot) :]:
             average(k, g)
             if g == GROUPS - 1:
                 finish(k, False)
-        pieces = [(4, 0, C), (5, 0, C), (6, 0, 256), (6, 256, C), (7, 0, 256), (7, 256, 384), (7, 384, C)]
-        for n, (k, first, end) in enumerate(pieces):
+        for n, (k, first, last) in enumerate(pieces):
             for g in range(GROUPS):
-                average(k, g, first, end)
-            finish(k, n >= 2 and n % 2 == 0, first, end)
+                average(k, g, first, last)
+            finish(k, n >= 2 and n % 2 == 0, first, last)

@@ -77,17 +77,14 @@ def tile_balanced_nonlocal_means_s12_kernel(
         e_grp = [kept("e_grp%d" % s, [P, HALF, 4], BF16) for s in range(STEPS)]
         e_codes = [kept("e_codes%d" % s, [P, HALF], U32) for s in range(STEPS)]
         e_plane = [kept("e_plane%d" % s, [P, HALF], U8) for s in range(STEPS)]
-        gam_raw = kept("gam_raw", [P, PASS], BF16)
+        gam_raw = kept("gam_raw", [GROUPS, PASS], BF16)
+        mant = kept("mant", [GROUPS, PASS], BF16)
+        gam_rows = kept("gam_rows", [P, 2, 4, P], F32)
         rho_raw = kept("rho_raw", [P, M // P, 2], BF16)
-        gam_by_row = kept("gam_by_row", [P, PASS], BF16)
-        gam_x = kept("gam_x", [P, PASS], BF16)
-        gam_by_place = kept("gam_by_place", [P, PASS], F32)
-        gam_t = kept("gam_t", [P, PASS], F32)
+        gam_col = kept("gam_col", [P, 4 * GROUPS], F32)
         rho_col = kept("rho_col", [P, M // P], F32)
-        mant = kept("mant", [P, 4 * GROUPS], I32)
         expo = kept("expo", [P, 4 * GROUPS], I32)
         expo_ln = kept("expo_ln", [P, 4 * GROUPS], F32)
-        mant_ln = kept("mant_ln", [P, 4 * GROUPS], F32)
         ln_gam = kept("ln_gam", [P, 4 * GROUPS], F32)
         half_sign = kept("half_sign", [P, 4 * GROUPS], F32)
         twice_pos = kept("twice_pos", [P, 4 * GROUPS], F32)
@@ -110,22 +107,19 @@ def tile_balanced_nonlocal_means_s12_kernel(
         def load_x(g):
             nc.sync.dma_start(out=x_raw[g][:], in_=x.rearrange("(g m b) f -> g m b f", g=GROUPS, b=4)[g])
 
-        nc.gpsimd.memset(gam_raw[:].bitcast(I32), 0)
         nc.gpsimd.memset(b_rows_first[:].bitcast(I32), 0)
         nc.vector.memset(a_plane[:].bitcast(I32), 0)
-        nc.vector.memset(b_rows_second[:].bitcast(I32), 0)
-        nc.vector.memset(b_rows_late[:].bitcast(I32), 0)
+        nc.vector.memset(gam_rows[:], 0.0)
 
+        nc.sync.dma_start(out=gam_raw[:], in_=gamma.rearrange("(g n) -> g n", g=GROUPS))
         load_codes(b_raw[0], b_words, 0)
-        nc.sync.dma_start(
-            out=gam_raw[0:P:32, :].rearrange("q (g n) -> q g n", g=GROUPS),
-            in_=gamma.rearrange("(g q n) -> q g n", g=GROUPS, q=4),
-        )
         load_rows(b_rows_first, b_scales, 0, PASS)
         load_rows(a_plane, a_scales, 0, M, (0,))
         load_codes(a_codes[0], a_words, 0)
         load_rows(a_plane, a_scales, 0, M, (1, 2, 3))
         make_identity(nc, ident[:])
+        nc.gpsimd.memset(b_rows_second[:].bitcast(I32), 0)
+        nc.gpsimd.memset(b_rows_late[:].bitcast(I32), 0)
         nc.sync.dma_start(out=w_raw[:], in_=w.rearrange("(p j) c -> p j c", j=4))
         load_codes(a_codes[1], a_words, 2 * HALF)
         load_x(0)
@@ -260,34 +254,59 @@ def tile_balanced_nonlocal_means_s12_kernel(
                 nc.scalar.activation(out=res[:], in_=o_bank[k, first][:], func=ACT.Copy, scale=rho_col[:, k : k + 1])
             nc.sync.dma_start(out=out[P * k : P * (k + 1), first:last], in_=res[:])
 
+        nc.vector.tensor_scalar(
+            out=mant[:].bitcast(I32),
+            in0=gam_raw[:].bitcast(I32),
+            scalar1=0x007F007F,
+            scalar2=0x3F803F80,
+            op0=ALU.bitwise_and,
+            op1=ALU.bitwise_or,
+        )
+        by_place = "g (q t r) -> g t q r"
+        nc.scalar.activation(
+            out=gam_rows[0:GROUPS, 1].rearrange("g t (q r) -> g t q r", r=8),
+            in_=mant[:].rearrange(by_place, t=4, r=8),
+            func=ACT.Ln,
+        )
+        gam_pairs = gam_rows[0:GROUPS, 0].bitcast(BF16).rearrange("g t (c e) -> g t c e", e=2)
         nc.vector.tensor_copy(
-            out=gam_by_place[:].rearrange("p (g t q r) -> p g t q r", g=GROUPS, t=4, q=4),
-            in_=gam_raw[:].rearrange("p (g q t r) -> p g t q r", g=GROUPS, q=4, t=4),
+            out=gam_pairs[:, :, :, 0].rearrange("g t (q r) -> g t q r", r=8), in_=gam_raw[:].rearrange(by_place, t=4, r=8)
         )
+        nc.vector.tensor_copy(out=gam_pairs[:, :, :, 1], in_=gam_raw[:].rearrange("g (m b) -> g b m", b=4))
+        gam_banks = []
+        for k in range(2):
+            bank = psum.tile([P, 4, P], F32, name="gam_t", tag="side")
+            for t in range(4):
+                nc.tensor.transpose(bank[:, t, :], gam_rows[:, k, t, :], ident[:])
+            gam_banks.append(bank[:, :, 0:GROUPS])
+        pair_cols = gam_banks[0].bitcast(BF16).rearrange("p t (g e) -> p g t e", e=2)
+        gam_cols = [pair_cols[:, :, :, 0], pair_cols[:, :, :, 1], gam_banks[1].rearrange("p t g -> p g t")]
+
+        def by_group(tile):
+            return tile[:].rearrange("p (g t) -> p g t", t=4)
+
         arrange(b_codes_early[0], b_raw[0], 4)
-        nc.vector.transpose(out=gam_t[:], in_=gam_by_place[:])
+        nc.vector.tensor_copy(out=by_group(gam_col), in_=gam_cols[0])
         arrange(b_plane_first, b_rows_first, 2)
-        bits = gam_t[:].bitcast(I32)[:, 0:PASS:32]
         nc.vector.tensor_scalar(
-            out=mant[:], in0=bits, scalar1=0x007FFFFF, scalar2=0x3F800000, op0=ALU.bitwise_and, op1=ALU.bitwise_or
+            out=expo[:],
+            in0=gam_col[:].bitcast(I32),
+            scalar1=23,
+            scalar2=0xFF,
+            op0=ALU.logical_shift_right,
+            op1=ALU.bitwise_and,
         )
         nc.vector.tensor_scalar(
-            out=expo[:], in0=bits, scalar1=23, scalar2=0xFF, op0=ALU.logical_shift_right, op1=ALU.bitwise_and
-        )
-        nc.scalar.activation(out=mant_ln[:], in_=mant[:].bitcast(F32), func=ACT.Ln)
-        nc.vector.tensor_scalar(
-            out=twice_pos[:], in0=gam_t[:, 0:PASS:32], scalar1=0.0, scalar2=2.0, op0=ALU.is_ge, op1=ALU.mult
+            out=twice_pos[:], in0=gam_col[:], scalar1=0.0, scalar2=2.0, op0=ALU.is_ge, op1=ALU.mult
         )
         nc.vector.tensor_scalar(
             out=expo_ln[:], in0=expo[:], scalar1=-127.0, scalar2=math.log(2.0), op0=ALU.add, op1=ALU.mult
         )
-        nc.vector.tensor_scalar_add(out=sign[:].rearrange("p g t -> p (g t)"), in0=twice_pos[:], scalar1=-1.0)
-        nc.vector.tensor_copy(
-            out=gam_by_row[:].rearrange("p (g b m) -> p g b m", g=GROUPS, b=4),
-            in_=gam_raw[:].rearrange("p (g m b) -> p g b m", g=GROUPS, b=4),
+        nc.vector.tensor_scalar(
+            out=by_group(half_sign), in0=gam_cols[1], scalar1=0.0, scalar2=0.5, op0=ALU.is_ge, op1=ALU.subtract
         )
-        nc.vector.tensor_tensor(out=ln_gam[:], in0=mant_ln[:], in1=expo_ln[:], op=ALU.add)
-        nc.vector.transpose(out=gam_x[:], in_=gam_by_row[:])
+        nc.vector.tensor_tensor(out=by_group(ln_gam), in0=gam_cols[2], in1=by_group(expo_ln), op=ALU.add)
+        nc.vector.tensor_scalar_add(out=sign[:].rearrange("p g t -> p (g t)"), in0=twice_pos[:], scalar1=-1.0)
 
         order = [0, GROUPS] + list(range(1, GROUPS)) + list(range(GROUPS + 1, STEPS))
         turns = {FIRST_TURN: (0, 1), SECOND_TURN: (2, 3)}
@@ -344,9 +363,6 @@ def tile_balanced_nonlocal_means_s12_kernel(
             weigh(order[slot // 4], slot % 4)
             if slot == 3:
                 interleave(w_grp, w_raw)
-                nc.vector.tensor_scalar(
-                    out=half_sign[:], in0=gam_x[:, 0:PASS:32], scalar1=0.0, scalar2=0.5, op0=ALU.is_ge, op1=ALU.subtract
-                )
                 quantize(w_codes, w_plane, w_grp)
                 sort_x(0)
             if slot == 5:

@@ -26,12 +26,9 @@ TILES = HALF // P
 STEPS = 2 * GROUPS
 SLOTS = 4 * STEPS
 
-FIRST_TURN, SECOND_TURN = 7, 18
-V_LAG = 3
-SORTED = (0, 1, 3)
-LAST_SORT = 14
-SCALAR_QUARTERS = ((1, 3), (0, 2), (), (0, 1, 2, 3))
-OUT_PASSES = 3
+FIRST_TURN, SECOND_TURN = 9, 20
+V_LAG = 4
+OUT_SLOT = 29
 
 
 def tile_balanced_nonlocal_means_s12_kernel(
@@ -62,7 +59,7 @@ def tile_balanced_nonlocal_means_s12_kernel(
         b_plane_late = kept("b_plane_late", [P, DEPTH, 2 * PASS], U8)
         b_plane = [b_plane_first[:], b_plane_second[:]] + [b_plane_late[:, :, PASS * g : PASS * (g + 1)] for g in range(2)]
         x_raw = [kept("x_raw%d" % g, [P, 4, F], BF16) for g in range(GROUPS)]
-        x_sorted = {g: kept("x_sorted%d" % g, [P, 4, F], BF16) for g in SORTED}
+        x_sorted = [kept("x_sorted%d" % g, [P, 4, F], BF16) for g in range(GROUPS)]
         x_grp = [kept("x_grp%d" % g, [P, PASS, 4], BF16) for g in range(GROUPS)]
         x_codes = [kept("x_codes%d" % g, [P, PASS], U32) for g in range(GROUPS)]
         x_plane = [kept("x_plane%d" % g, [P, PASS], U8) for g in range(GROUPS)]
@@ -87,8 +84,6 @@ def tile_balanced_nonlocal_means_s12_kernel(
         expo_ln = kept("expo_ln", [P, 4 * GROUPS], F32)
         ln_gam = kept("ln_gam", [P, 4 * GROUPS], F32)
         half_sign = kept("half_sign", [P, 4 * GROUPS], F32)
-        twice_pos = kept("twice_pos", [P, 4 * GROUPS], F32)
-        sign = kept("sign", [P, GROUPS, 4], F32)
         ident = kept("ident", [P, P], F32)
 
         def load_codes(tile, words, first):
@@ -122,10 +117,10 @@ def tile_balanced_nonlocal_means_s12_kernel(
         nc.gpsimd.memset(b_rows_late[:].bitcast(I32), 0)
         nc.sync.dma_start(out=w_raw[:], in_=w.rearrange("(p j) c -> p j c", j=4))
         load_codes(a_codes[1], a_words, 2 * HALF)
-        load_x(0)
-        load_x(1)
         load_rows(b_rows_second, b_scales, PASS, 2 * PASS)
         load_codes(b_raw[1], b_words, 2 * PASS)
+        load_x(0)
+        load_x(1)
         load_codes(b_raw_late, b_words, 4 * PASS)
         load_rows(b_rows_late, b_scales, 2 * PASS, N)
         load_x(2)
@@ -158,10 +153,7 @@ def tile_balanced_nonlocal_means_s12_kernel(
                 x_banks[g, k] = bank
                 for row in range(2):
                     for u in range(2):
-                        if g in SORTED:
-                            pairs = x_sorted[g][:, 2 * k + row, :].bitcast(F32)[:, P * u : P * (u + 1)]
-                        else:
-                            pairs = x_raw[g][:, 2 * k + row, :].bitcast(F32)[:, u::2]
+                        pairs = x_sorted[g][:, 2 * k + row, :].bitcast(F32)[:, P * u : P * (u + 1)]
                         nc.tensor.transpose(bank[:, 2 * row + u, :], pairs, ident[:])
 
         def take_x(g, copy):
@@ -202,7 +194,7 @@ def tile_balanced_nonlocal_means_s12_kernel(
                 out=e_bf[s][:, t, :], in_=bank[:], func=ACT.Exp, bias=ln_gam[:, 4 * g + t : 4 * g + t + 1]
             )
 
-        def project(g, quarter):
+        def project(g, quarter, copy):
             bank = psum.tile([P, 4, P], F32, name="val", tag="side")
             cols = slice(P * quarter, P * (quarter + 1))
             for t in range(4):
@@ -215,23 +207,14 @@ def tile_balanced_nonlocal_means_s12_kernel(
                     start=True,
                     stop=True,
                 )
-            if g in SORTED:
-                copy = nc.scalar.copy if quarter in SCALAR_QUARTERS[g] else nc.vector.tensor_copy
-                copy(out=v_grp[g][:, cols, :], in_=bank[:].rearrange("p t c -> p c t"))
-            else:
-                nc.vector.tensor_tensor(
-                    out=v_grp[g][:, cols, :],
-                    in0=bank[:].rearrange("p t c -> p c t"),
-                    in1=sign[:, g : g + 1, :].to_broadcast([P, P, 4]),
-                    op=ALU.mult,
-                )
+            copy(out=v_grp[g][:, cols, :], in_=bank[:].rearrange("p t c -> p c t"))
 
         o_bank = {}
 
         def average(k, g, first=0, last=C):
             h, i = divmod(k, TILES)
             if g == 0:
-                tag = "gram" if h == 1 and first == 0 else "side"
+                tag = "gram" if k in (TILES, TILES + 1) else "side"
                 o_bank[k, first] = psum.tile([P, last - first], F32, name="avg", tag=tag)
             s = h * GROUPS + g
             nc.tensor.matmul_mx(
@@ -247,7 +230,7 @@ def tile_balanced_nonlocal_means_s12_kernel(
         pieces = [(4, 0, C), (5, 0, C), (6, 0, 256), (6, 256, C), (7, 0, 256), (7, 256, 384), (7, 384, C)]
 
         def finish(k, on_vector, first=0, last=C):
-            res = work.tile([P, last - first], F32, name="res", tag="res", bufs=TILES + len(pieces))
+            res = work.tile([P, last - first], F32, name="res", tag="res", bufs=2 * TILES)
             if on_vector:
                 nc.vector.tensor_scalar_mul(out=res[:], in0=o_bank[k, first][:], scalar1=rho_col[:, k : k + 1])
             else:
@@ -286,8 +269,8 @@ def tile_balanced_nonlocal_means_s12_kernel(
             return tile[:].rearrange("p (g t) -> p g t", t=4)
 
         arrange(b_codes_early[0], b_raw[0], 4)
-        nc.vector.tensor_copy(out=by_group(gam_col), in_=gam_cols[0])
         arrange(b_plane_first, b_rows_first, 2)
+        nc.vector.tensor_copy(out=by_group(gam_col), in_=gam_cols[0])
         nc.vector.tensor_scalar(
             out=expo[:],
             in0=gam_col[:].bitcast(I32),
@@ -297,107 +280,114 @@ def tile_balanced_nonlocal_means_s12_kernel(
             op1=ALU.bitwise_and,
         )
         nc.vector.tensor_scalar(
-            out=twice_pos[:], in0=gam_col[:], scalar1=0.0, scalar2=2.0, op0=ALU.is_ge, op1=ALU.mult
-        )
-        nc.vector.tensor_scalar(
             out=expo_ln[:], in0=expo[:], scalar1=-127.0, scalar2=math.log(2.0), op0=ALU.add, op1=ALU.mult
         )
         nc.vector.tensor_scalar(
             out=by_group(half_sign), in0=gam_cols[1], scalar1=0.0, scalar2=0.5, op0=ALU.is_ge, op1=ALU.subtract
         )
         nc.vector.tensor_tensor(out=by_group(ln_gam), in0=gam_cols[2], in1=by_group(expo_ln), op=ALU.add)
-        nc.vector.tensor_scalar_add(out=sign[:].rearrange("p g t -> p (g t)"), in0=twice_pos[:], scalar1=-1.0)
 
-        order = [0, GROUPS] + list(range(1, GROUPS)) + list(range(GROUPS + 1, STEPS))
-        turns = {FIRST_TURN: (0, 1), SECOND_TURN: (2, 3)}
-        v_slot = [(FIRST_TURN, SECOND_TURN)[g // 2] + V_LAG + 4 * (g % 2) for g in range(GROUPS)]
-        out_slot = v_slot[-1] + 4
+        order = [0, GROUPS, 1, GROUPS + 1, 2, 3, GROUPS + 2, GROUPS + 3]
+        tile_passes = [(k, g) for k in range(TILES) for g in range(GROUPS)]
 
-        def job(call, *args):
-            return lambda: call(*args)
+        def weigh_slots(first, last):
+            for slot in range(first, last + 1):
+                weigh(order[slot // 4], slot % 4)
 
-        needed = {slot: [] for slot in range(SLOTS)}
-        needed[FIRST_TURN] += [
-            job(arrange, b_plane_second, b_rows_second, 2),
-            job(arrange, b_codes_early[1], b_raw[1], 4),
-        ]
-        for g in range(GROUPS):
-            needed[v_slot[g] - 2 - g % 2].append(job(quantize, x_codes[g], x_plane[g], x_grp[g]))
-        for g in range(GROUPS):
-            slot = v_slot[g] + 4 if g >= 2 else SECOND_TURN + 1 + 4 * g
-            needed[slot].append(job(quantize, v_codes[g], v_plane[g], v_grp[g]))
-        needed[FIRST_TURN + 1] += [
-            job(arrange, b_codes_late, b_raw_late, 4),
-            job(arrange, b_plane_late, b_rows_late, 2),
-        ]
-        needed[LAST_SORT].append(job(sort_x, GROUPS - 1))
+        def spread(s, half):
+            interleave(e_grp[s], e_bf[s], half * HALF // 2, (half + 1) * HALF // 2)
 
-        backlog = []
-        for n, s in enumerate(order[:-1]):
-            backlog.append((4 * n + 3, job(interleave, e_grp[s], e_bf[s], 0, HALF // 2)))
-            if n > 0:
-                before = order[n - 1]
-                backlog.append((0, job(quantize, e_codes[before], e_plane[before], e_grp[before])))
-            if n < STEPS - 2:
-                backlog.append((0, job(interleave, e_grp[s], e_bf[s], HALF // 2, HALF)))
+        def quantize_e(s, first=0, last=HALF):
+            quantize(e_codes[s], e_plane[s], e_grp[s], first, last)
 
-        room = {slot: 1 for slot in range(SLOTS)}
-        for slot in range(FIRST_TURN):
-            room[slot] = 0
-        room[4] = 1
-        room[FIRST_TURN] = 4
-        room[v_slot[1] + 3] = 0
-        room[SECOND_TURN] = 0
-        room[SECOND_TURN + 1] = 3
-        room[SECOND_TURN + 2] = 2
-        for quarter in range(4):
-            room[v_slot[2] + quarter] = 0
-            room[v_slot[3] + quarter] = 2 if quarter < 3 else 0
-        for slot in range(out_slot, SLOTS):
-            room[slot] = 3
+        def quantize_x(g):
+            quantize(x_codes[g], x_plane[g], x_grp[g])
 
-        early = [(k, g) for k in range(TILES - 1) for g in range(GROUPS - 1)]
-        early += [(k, GROUPS - 1) for k in range(TILES - 1)] + [(TILES - 1, g) for g in range(GROUPS)]
+        def quantize_v(g):
+            quantize(v_codes[g], v_plane[g], v_grp[g])
 
-        for slot in range(SLOTS):
-            weigh(order[slot // 4], slot % 4)
-            if slot == 3:
-                interleave(w_grp, w_raw)
-                quantize(w_codes, w_plane, w_grp)
-                sort_x(0)
-            if slot == 5:
-                sort_x(1)
-            for call in needed[slot]:
-                call()
-            for n in range(room[slot] - len(needed[slot])):
-                if backlog and backlog[0][0] <= slot:
-                    backlog[0][1]()
-                    backlog = backlog[1:]
-            for g in range(GROUPS):
-                if 0 <= slot - v_slot[g] < 4:
-                    project(g, slot - v_slot[g])
-            if slot == out_slot:
-                nc.scalar.copy(out=rho_col[:], in_=rho_raw[:, :, 0])
-            if slot >= out_slot:
-                for k, g in early[OUT_PASSES * (slot - out_slot) : OUT_PASSES * (slot - out_slot + 1)]:
-                    average(k, g)
-            for g in turns.get(slot, ()):
-                turn_x(g)
-            for g in turns.get(slot, ()):
-                take_x(g, nc.vector.tensor_copy if g == turns[SECOND_TURN][0] else nc.scalar.copy)
+        def project_group(g, on_vector):
+            for quarter in range(4):
+                project(g, quarter, nc.vector.tensor_copy if quarter in on_vector else nc.scalar.copy)
 
-        last_two = (STEPS - 2, STEPS - 1)
-        interleave(e_grp[STEPS - 1], e_bf[STEPS - 1], 0, HALF // 2)
-        for s in last_two:
-            quantize(e_codes[s], e_plane[s], e_grp[s], 0, HALF // 2)
-        for s in last_two:
-            interleave(e_grp[s], e_bf[s], HALF // 2, HALF)
-        for s in last_two:
-            quantize(e_codes[s], e_plane[s], e_grp[s], HALF // 2, HALF)
-        for k, g in early[OUT_PASSES * (SLOTS - out_slot) :]:
-            average(k, g)
-            if g == GROUPS - 1:
-                finish(k, False)
+        def average_and_finish(passes):
+            for k, g in passes:
+                average(k, g)
+                if g == GROUPS - 1:
+                    finish(k, False)
+
+        weigh_slots(0, 3)
+        interleave(w_grp, w_raw)
+        arrange(b_plane_second, b_rows_second, 2)
+        quantize(w_codes, w_plane, w_grp)
+        arrange(b_codes_early[1], b_raw[1], 4)
+        spread(0, 0)
+        spread(0, 1)
+        sort_x(0)
+        sort_x(1)
+        weigh_slots(4, FIRST_TURN)
+        spread(GROUPS, 0)
+        quantize_e(0)
+        for g in (0, 1):
+            turn_x(g)
+        for g in (0, 1):
+            take_x(g, nc.scalar.copy)
+
+        spread(GROUPS, 1)
+        quantize_x(0)
+        arrange(b_codes_late, b_raw_late, 4)
+        quantize_x(1)
+        arrange(b_plane_late, b_rows_late, 2)
+        weigh_slots(FIRST_TURN + 1, FIRST_TURN + V_LAG)
+        project_group(0, (0, 2))
+
+        spread(1, 0)
+        sort_x(2)
+        spread(1, 1)
+        quantize_v(0)
+        sort_x(3)
+        weigh_slots(FIRST_TURN + V_LAG + 1, FIRST_TURN + 2 * V_LAG)
+        project_group(1, (0, 2))
+        quantize_e(1)
+        quantize_v(1)
+        weigh_slots(FIRST_TURN + 2 * V_LAG + 1, SECOND_TURN)
+
+        for g in (2, 3):
+            turn_x(g)
+        take_x(2, nc.vector.tensor_copy)
+        take_x(3, nc.scalar.copy)
+        nc.scalar.copy(out=rho_col[:], in_=rho_raw[:, :, 0])
+        spread(2, 0)
+        quantize_x(2)
+        spread(2, 1)
+        quantize_x(3)
+        weigh_slots(SECOND_TURN + 1, SECOND_TURN + V_LAG)
+        project_group(2, (0, 2))
+        spread(3, 0)
+        quantize_e(2)
+        weigh_slots(SECOND_TURN + V_LAG + 1, SECOND_TURN + V_LAG + 1)
+        project_group(3, (2,))
+
+        quantize_v(2)
+        spread(3, 1)
+        quantize_v(3)
+        quantize_e(3)
+        spread(GROUPS + 1, 0)
+        quantize_e(GROUPS)
+        spread(GROUPS + 1, 1)
+        weigh_slots(SECOND_TURN + V_LAG + 2, OUT_SLOT - 1)
+        spread(GROUPS + 2, 0)
+        quantize_e(GROUPS + 1)
+        spread(GROUPS + 2, 1)
+        for slot in range(OUT_SLOT, SLOTS):
+            weigh_slots(slot, slot)
+            average_and_finish(tile_passes[2 * (slot - OUT_SLOT) : 2 * (slot - OUT_SLOT + 1)])
+
+        for half in range(2):
+            spread(STEPS - 1, half)
+            for s in (STEPS - 2, STEPS - 1):
+                quantize_e(s, half * HALF // 2, (half + 1) * HALF // 2)
+        average_and_finish(tile_passes[2 * (SLOTS - OUT_SLOT) :])
         for n, (k, first, last) in enumerate(pieces):
             for g in range(GROUPS):
                 average(k, g, first, last)

@@ -92,11 +92,11 @@ def tile_balanced_nonlocal_means_s12_kernel(
                 in_=words.rearrange("d p n -> p d n")[:, :, first : first + tile.shape[2]].bitcast(I32),
             )
 
-        def load_rows(plane, rows, first, last, quadrants=range(4)):
-            for q in quadrants:
+        def load_rows(plane, rows, first, last, which=range(4)):
+            for r in which:
                 nc.sync.dma_start(
-                    out=plane[32 * q : 32 * q + 4, :, :].bitcast(I32),
-                    in_=rows[:, 4 * q : 4 * q + 4, first:last].rearrange("d r n -> r d n").bitcast(I32),
+                    out=plane[r:P:32, :, :].bitcast(I32),
+                    in_=rows[:, r:16:4, first:last].rearrange("d q n -> q d n").bitcast(I32),
                 )
 
         def load_x(g):

@@ -44,8 +44,11 @@ def tile_balanced_nonlocal_means_s12_kernel(
         def kept(name, shape, dtype):
             return keep.tile(shape, dtype, name=name, tag=name, align_bytes=64)
 
+        def kept_plane(name, columns):
+            return kept(name, [P, columns + 256], U8)[:, 128 : 128 + columns]
+
         a_codes = [kept("a_codes%d" % h, [P, DEPTH, 2 * HALF], U8) for h in range(2)]
-        a_plane = kept("a_plane", [P, DEPTH, M], U8)
+        a_plane = kept_plane("a_plane", DEPTH * M).rearrange("p (d n) -> p d n", d=DEPTH)
         b_raw = [kept("b_raw%d" % g, [P, DEPTH, 2 * PASS], U8) for g in range(2)]
         b_raw_late = kept("b_raw_late", [P, DEPTH, 4 * PASS], U8)
         b_rows_first = kept("b_rows_first", [P, DEPTH, PASS], U8)
@@ -66,10 +69,10 @@ def tile_balanced_nonlocal_means_s12_kernel(
         w_raw = kept("w_raw", [P, 4, C], BF16)
         w_grp = kept("w_grp", [P, C, 4], BF16)
         w_codes = kept("w_codes", [P, C], U32)
-        w_plane = kept("w_plane", [P, C], U8)
+        w_plane = kept_plane("w_plane", C)
         v_grp = [kept("v_grp%d" % g, [P, C, 4], BF16) for g in range(GROUPS)]
         v_codes = [kept("v_codes%d" % g, [P, C], U32) for g in range(GROUPS)]
-        v_plane = [kept("v_plane%d" % g, [P, C], U8) for g in range(GROUPS)]
+        v_plane = [kept_plane("v_plane%d" % g, C) for g in range(GROUPS)]
         e_bf = [kept("e_bf%d" % s, [P, 4, HALF], BF16) for s in range(STEPS)]
         e_grp = [kept("e_grp%d" % s, [P, HALF, 4], BF16) for s in range(STEPS)]
         e_codes = [kept("e_codes%d" % s, [P, HALF], U32) for s in range(STEPS)]
@@ -103,7 +106,7 @@ def tile_balanced_nonlocal_means_s12_kernel(
             nc.sync.dma_start(out=x_raw[g][:], in_=x.rearrange("(g m b) f -> g m b f", g=GROUPS, b=4)[g])
 
         nc.gpsimd.memset(b_rows_first[:].bitcast(I32), 0)
-        nc.vector.memset(a_plane[:].bitcast(I32), 0)
+        nc.vector.memset(a_plane.bitcast(I32), 0)
         nc.vector.memset(gam_rows[:], 0.0)
 
         nc.sync.dma_start(out=gam_raw[:], in_=gamma.rearrange("(g n) -> g n", g=GROUPS))

@@ -38,8 +38,11 @@ def tile_balanced_nonlocal_means_s12_kernel(
     with ExitStack() as ctx:
         keep = ctx.enter_context(tc.tile_pool(name="keep", bufs=1))
         work = ctx.enter_context(tc.tile_pool(name="work", bufs=4))
-        psum = ctx.enter_context(tc.psum_pool(name="psum", bufs=4))
+        psum = ctx.enter_context(tc.psum_pool(name="psum", bufs=1))
         ctx.enter_context(tc.manual_schedule())
+
+        def bank_tile(name, shape, bank):
+            return psum.tile(shape, F32, name=name, tag="bank%d" % bank)
 
         def kept(name, shape, dtype):
             return keep.tile(shape, dtype, name=name, tag=name, align_bytes=64)
@@ -73,8 +76,6 @@ def tile_balanced_nonlocal_means_s12_kernel(
         v_grp = [kept("v_grp%d" % g, [P, C, 4], BF16) for g in range(GROUPS)]
         v_codes = [kept("v_codes%d" % g, [P, C], U32) for g in range(GROUPS)]
         v_plane = [kept_plane("v_plane%d" % g, C) for g in range(GROUPS)]
-        e_bf = [kept("e_bf%d" % s, [P, 4, HALF], BF16) for s in range(STEPS)]
-        e_grp = [kept("e_grp%d" % s, [P, HALF, 4], BF16) for s in range(STEPS)]
         e_codes = [kept("e_codes%d" % s, [P, HALF], U32) for s in range(STEPS)]
         e_plane = [kept("e_plane%d" % s, [P, HALF], U8) for s in range(STEPS)]
         gam_raw = kept("gam_raw", [GROUPS, PASS], BF16)
@@ -150,22 +151,21 @@ def tile_balanced_nonlocal_means_s12_kernel(
 
         x_banks = {}
 
-        def turn_x(g):
+        def turn_x(g, banks):
             for k in range(2):
-                bank = psum.tile([P, 4, P], F32, name="x_t", tag="side")
+                bank = bank_tile("x_t", [P, 4, P], banks[k])
                 x_banks[g, k] = bank
                 for row in range(2):
                     for u in range(2):
                         pairs = x_sorted[g][:, 2 * k + row, :].bitcast(F32)[:, P * u : P * (u + 1)]
                         nc.tensor.transpose(bank[:, 2 * row + u, :], pairs, ident[:])
 
-        def take_x(g, copy):
+        def take_x(g, k, copy):
             pairs = x_grp[g][:].rearrange("p c j -> p (c j)").bitcast(F32)
-            for k in range(2):
-                copy(
-                    out=pairs.rearrange("p (t q r e) -> p t q r e", t=4, r=2, e=8)[:, :, :, :, 4 * k : 4 * k + 4],
-                    in_=x_banks[g, k][:].rearrange("p e (q t r) -> p t q r e", t=4, r=2),
-                )
+            copy(
+                out=pairs.rearrange("p (t q r e) -> p t q r e", t=4, r=2, e=8)[:, :, :, :, 4 * k : 4 * k + 4],
+                in_=x_banks[g, k][:].rearrange("p e (q t r) -> p t q r e", t=4, r=2),
+            )
 
         def quantize(codes, plane, grouped, first=0, last=PASS):
             nc.vector.quantize_mx(
@@ -180,12 +180,17 @@ def tile_balanced_nonlocal_means_s12_kernel(
                 in_=rows[:, :, first:last].rearrange("p t (c i) -> p c t i", i=4),
             )
 
-        def weigh(s, t):
+        e_bf = {}
+        e_grp = {}
+
+        def weigh(s, t, bank):
             h, g = divmod(s, GROUPS)
-            bank = psum.tile([P, HALF], F32, name="gram", tag="gram")
+            gram = bank_tile("gram", [P, HALF], bank)
+            if t == 0:
+                e_bf[s] = work.tile([P, 4, HALF], BF16, name="e_bf", tag="e_bf", bufs=6, align_bytes=64)
             for d in range(DEPTH):
                 nc.tensor.matmul_mx(
-                    out=bank[:],
+                    out=gram[:],
                     lhsT=b_codes[g][:, d, 2 * P * t : 2 * P * (t + 1)].bitcast(E2M1),
                     lhsT_scale=b_plane[g][:, d, P * t : P * (t + 1)],
                     rhs=a_codes[h][:, d, :].bitcast(E2M1),
@@ -194,15 +199,18 @@ def tile_balanced_nonlocal_means_s12_kernel(
                     stop=(d == DEPTH - 1),
                 )
             nc.scalar.activation(
-                out=e_bf[s][:, t, :], in_=bank[:], func=ACT.Exp, bias=ln_gam[:, 4 * g + t : 4 * g + t + 1]
+                out=e_bf[s][:, t, :], in_=gram[:], func=ACT.Exp, bias=ln_gam[:, 4 * g + t : 4 * g + t + 1]
             )
 
-        def project(g, quarter, copy):
-            bank = psum.tile([P, 4, P], F32, name="val", tag="side")
+        v_banks = {}
+
+        def project(g, quarter, bank):
+            val = bank_tile("val", [P, 4, P], bank)
+            v_banks[g, quarter] = val
             cols = slice(P * quarter, P * (quarter + 1))
             for t in range(4):
                 nc.tensor.matmul_mx(
-                    out=bank[:, t, :],
+                    out=val[:, t, :],
                     lhsT=x_codes[g][:, P * t : P * (t + 1)].bitcast(E4M3),
                     lhsT_scale=x_plane[g][:, P * t : P * (t + 1)],
                     rhs=w_codes[:, cols].bitcast(E4M3),
@@ -210,15 +218,17 @@ def tile_balanced_nonlocal_means_s12_kernel(
                     start=True,
                     stop=True,
                 )
-            copy(out=v_grp[g][:, cols, :], in_=bank[:].rearrange("p t c -> p c t"))
+
+        def take_v(g, quarter, copy):
+            cols = slice(P * quarter, P * (quarter + 1))
+            copy(out=v_grp[g][:, cols, :], in_=v_banks[g, quarter][:].rearrange("p t c -> p c t"))
 
         o_bank = {}
 
-        def average(k, g, first=0, last=C):
+        def average(k, g, bank=None, first=0, last=C):
             h, i = divmod(k, TILES)
             if g == 0:
-                tag = "gram" if k in (TILES, TILES + 1) else "side"
-                o_bank[k, first] = psum.tile([P, last - first], F32, name="avg", tag=tag)
+                o_bank[k, first] = bank_tile("avg", [P, last - first], bank)
             s = h * GROUPS + g
             nc.tensor.matmul_mx(
                 out=o_bank[k, first][:],
@@ -229,8 +239,6 @@ def tile_balanced_nonlocal_means_s12_kernel(
                 start=(g == 0),
                 stop=(g == GROUPS - 1),
             )
-
-        pieces = [(4, 0, C), (5, 0, C), (6, 0, 256), (6, 256, C), (7, 0, 256), (7, 256, 384), (7, 384, C)]
 
         def finish(k, on_vector, first=0, last=C):
             res = work.tile([P, last - first], F32, name="res", tag="res", bufs=2 * TILES)
@@ -261,7 +269,7 @@ def tile_balanced_nonlocal_means_s12_kernel(
         nc.vector.tensor_copy(out=gam_pairs[:, :, :, 1], in_=gam_raw[:].rearrange("g (m b) -> g b m", b=4))
         gam_banks = []
         for k in range(2):
-            bank = psum.tile([P, 4, P], F32, name="gam_t", tag="side")
+            bank = bank_tile("gam_t", [P, 4, P], 4 + k)
             for t in range(4):
                 nc.tensor.transpose(bank[:, t, :], gam_rows[:, k, t, :], ident[:])
             gam_banks.append(bank[:, :, 0:GROUPS])
@@ -290,15 +298,26 @@ def tile_balanced_nonlocal_means_s12_kernel(
         )
         nc.vector.tensor_tensor(out=by_group(ln_gam), in0=gam_cols[2], in1=by_group(expo_ln), op=ALU.add)
 
+        on_scalar, on_vector = nc.scalar.copy, nc.vector.tensor_copy
         order = [0, GROUPS, 1, GROUPS + 1, 2, 3, GROUPS + 2, GROUPS + 3]
-        tile_passes = [(k, g) for k in range(TILES) for g in range(GROUPS)]
+        handed_out = []
+        early_passes = [(k, g) for g in range(2) for k in range(TILES)]
+
+        def next_bank():
+            handed_out.append(len(handed_out) % 4)
+            return handed_out[-1]
 
         def weigh_slots(first, last):
             for slot in range(first, last + 1):
-                weigh(order[slot // 4], slot % 4)
+                weigh(order[slot // 4], slot % 4, next_bank())
 
-        def spread(s, half):
-            interleave(e_grp[s], e_bf[s], half * HALF // 2, (half + 1) * HALF // 2)
+        def spread(s, first, last):
+            if first == 0:
+                e_grp[s] = work.tile([P, HALF, 4], BF16, name="e_grp", tag="e_grp", align_bytes=64)
+            interleave(e_grp[s], e_bf[s], first, last)
+
+        def spread_half(s, half):
+            spread(s, half * HALF // 2, (half + 1) * HALF // 2)
 
         def quantize_e(s, first=0, last=HALF):
             quantize(e_codes[s], e_plane[s], e_grp[s], first, last)
@@ -309,89 +328,119 @@ def tile_balanced_nonlocal_means_s12_kernel(
         def quantize_v(g):
             quantize(v_codes[g], v_plane[g], v_grp[g])
 
-        def project_group(g, on_vector):
-            for quarter in range(4):
-                project(g, quarter, nc.vector.tensor_copy if quarter in on_vector else nc.scalar.copy)
+        def early_pass():
+            k, g = early_passes.pop(0)
+            average(k, g, 4 + k)
 
-        def average_and_finish(passes):
-            for k, g in passes:
-                average(k, g)
-                if g == GROUPS - 1:
-                    finish(k, False)
+        def project_early(g):
+            for quarter in range(4):
+                project(g, quarter, 4 + quarter)
+                take_v(g, quarter, on_scalar if quarter % 2 else on_vector)
+
+        def project_late(g, vector_quarter, followed):
+            for quarter in range(4):
+                project(g, quarter, next_bank())
+                take_v(g, quarter, on_vector if quarter == vector_quarter else on_scalar)
+                if quarter in followed:
+                    early_pass()
 
         weigh_slots(0, 3)
         interleave(w_grp, w_raw)
         arrange(b_plane_second, b_rows_second, 2)
         quantize(w_codes, w_plane, w_grp)
         arrange(b_codes_early[1], b_raw[1], 4)
-        spread(0, 0)
-        spread(0, 1)
+        spread_half(0, 0)
+        spread_half(0, 1)
         sort_x(0)
         sort_x(1)
         weigh_slots(4, FIRST_TURN)
-        spread(GROUPS, 0)
+        spread_half(GROUPS, 0)
         quantize_e(0)
+        turn_x(0, (6, 7))
+        turn_x(1, (4, 5))
         for g in (0, 1):
-            turn_x(g)
-        for g in (0, 1):
-            take_x(g, nc.scalar.copy)
+            for k in (0, 1):
+                take_x(g, k, on_scalar)
 
-        spread(GROUPS, 1)
+        spread_half(GROUPS, 1)
         quantize_x(0)
         arrange(b_codes_late, b_raw_late, 4)
         quantize_x(1)
         arrange(b_plane_late, b_rows_late, 2)
         weigh_slots(FIRST_TURN + 1, FIRST_TURN + V_LAG)
-        project_group(0, (0, 2))
+        project_early(0)
 
-        spread(1, 0)
+        spread_half(1, 0)
         sort_x(2)
-        spread(1, 1)
+        spread_half(1, 1)
         quantize_v(0)
         sort_x(3)
         weigh_slots(FIRST_TURN + V_LAG + 1, FIRST_TURN + 2 * V_LAG)
-        project_group(1, (0, 2))
+        project_early(1)
         quantize_e(1)
         quantize_v(1)
         weigh_slots(FIRST_TURN + 2 * V_LAG + 1, SECOND_TURN)
 
-        for g in (2, 3):
-            turn_x(g)
-        take_x(2, nc.vector.tensor_copy)
-        take_x(3, nc.scalar.copy)
+        turn_x(2, (4, 5))
+        turn_x(3, (6, 7))
+        for k in (0, 1):
+            take_x(2, k, on_vector)
+        for k in (0, 1):
+            take_x(3, k, on_scalar)
         nc.scalar.copy(out=rho_col[:], in_=rho_raw[:, :, 0])
-        spread(2, 0)
+        spread_half(2, 0)
         quantize_x(2)
-        spread(2, 1)
+        spread_half(2, 1)
         quantize_x(3)
-        weigh_slots(SECOND_TURN + 1, SECOND_TURN + V_LAG)
-        project_group(2, (0, 2))
-        spread(3, 0)
-        quantize_e(2)
-        weigh_slots(SECOND_TURN + V_LAG + 1, SECOND_TURN + V_LAG + 1)
-        project_group(3, (2,))
 
-        quantize_v(2)
-        spread(3, 1)
-        quantize_v(3)
-        quantize_e(3)
-        spread(GROUPS + 1, 0)
-        quantize_e(GROUPS)
-        spread(GROUPS + 1, 1)
-        weigh_slots(SECOND_TURN + V_LAG + 2, OUT_SLOT - 1)
-        spread(GROUPS + 2, 0)
-        quantize_e(GROUPS + 1)
-        spread(GROUPS + 2, 1)
-        for slot in range(OUT_SLOT, SLOTS):
+        weigh_slots(SECOND_TURN + 1, SECOND_TURN + 1)
+        for slot in range(SECOND_TURN + 2, SECOND_TURN + V_LAG + 1):
             weigh_slots(slot, slot)
-            average_and_finish(tile_passes[2 * (slot - OUT_SLOT) : 2 * (slot - OUT_SLOT + 1)])
+            early_pass()
+        quantize_e(2)
+        project_late(2, 0, (0, 1, 3))
+        spread_half(3, 0)
+        quantize_e(GROUPS)
+        spread_half(3, 1)
+        project_late(3, 1, (0, 2))
+        quantize_v(2)
+        quantize_e(3)
+        quantize_v(3)
+        spread_half(GROUPS + 1, 0)
+        spread_half(GROUPS + 1, 1)
+        weigh_slots(SECOND_TURN + V_LAG + 1, OUT_SLOT - 1)
+        quantize_e(GROUPS + 1)
+        spread_half(GROUPS + 2, 0)
+        spread_half(GROUPS + 2, 1)
 
-        for half in range(2):
-            spread(STEPS - 1, half)
-            for s in (STEPS - 2, STEPS - 1):
-                quantize_e(s, half * HALF // 2, (half + 1) * HALF // 2)
-        average_and_finish(tile_passes[2 * (SLOTS - OUT_SLOT) :])
-        for n, (k, first, last) in enumerate(pieces):
+        for k in range(SLOTS - OUT_SLOT):
+            weigh_slots(OUT_SLOT + k, OUT_SLOT + k)
+            average(k, 2)
+            average(k, 3)
+            if k < 2:
+                finish(k, k == 1)
+        quantize_e(GROUPS + 2)
+        average(3, 2)
+        average(3, 3)
+
+        last = STEPS - 1
+        spread(last, 0, P)
+        spread(last, P, 2 * P)
+        quantize_e(last, 0, P)
+        finish(2, False)
+        spread(last, 2 * P, HALF)
+        quantize_e(last, P, 2 * P)
+        finish(3, False)
+        quantize_e(last, 2 * P, HALF)
+        free = [next_bank() for k in range(4)]
+        for k, g in ((4, 0), (4, 1), (4, 2), (5, 0), (5, 1), (4, 3)):
+            average(k, g, free[k - TILES])
+        finish(4, True)
+        average(5, 2)
+        average(5, 3)
+        finish(5, False)
+        pieces = [(6, 0, 256, free[2]), (6, 256, C, free[3]), (7, 0, 256, 4), (7, 256, 384, 5), (7, 384, C, 6)]
+        for n, (k, first, end, bank) in enumerate(pieces):
             for g in range(GROUPS):
-                average(k, g, first, last)
-            finish(k, n >= 2 and n % 2 == 0, first, last)
+                average(k, g, bank, first, end)
+            finish(k, n % 2 == 0, first, end)

@@ -174,8 +174,8 @@ def tile_balanced_nonlocal_means_s12_kernel(
                 in_=grouped[:, first:last, :].rearrange("p c t -> p (c t)"),
             )
 
-        def interleave(grouped, rows, first=0, last=PASS):
-            nc.vector.tensor_copy(
+        def interleave(grouped, rows, first=0, last=PASS, copy=nc.vector.tensor_copy):
+            copy(
                 out=grouped[:, first:last, :].rearrange("p (c i) t -> p c t i", i=4),
                 in_=rows[:, :, first:last].rearrange("p t (c i) -> p c t i", i=4),
             )
@@ -332,10 +332,10 @@ def tile_balanced_nonlocal_means_s12_kernel(
             k, g = early_passes.pop(0)
             average(k, g, 4 + k)
 
-        def project_early(g):
+        def project_early(g, vector_quarters=(0, 2)):
             for quarter in range(4):
                 project(g, quarter, 4 + quarter)
-                take_v(g, quarter, on_scalar if quarter % 2 else on_vector)
+                take_v(g, quarter, on_vector if quarter in vector_quarters else on_scalar)
 
         def project_late(g, vector_quarter, followed):
             for quarter in range(4):
@@ -368,7 +368,7 @@ def tile_balanced_nonlocal_means_s12_kernel(
         quantize_x(1)
         arrange(b_plane_late, b_rows_late, 2)
         weigh_slots(FIRST_TURN + 1, FIRST_TURN + V_LAG)
-        project_early(0)
+        project_early(0, (0,))
 
         spread_half(1, 0)
         sort_x(2)
@@ -398,19 +398,19 @@ def tile_balanced_nonlocal_means_s12_kernel(
             weigh_slots(slot, slot)
             early_pass()
         quantize_e(2)
-        project_late(2, 0, (0, 1, 3))
+        project_late(2, None, (0, 1, 3))
         spread_half(3, 0)
         quantize_e(GROUPS)
         spread_half(3, 1)
         project_late(3, 1, (0, 2))
         quantize_v(2)
         quantize_e(3)
-        quantize_v(3)
         spread_half(GROUPS + 1, 0)
+        quantize_v(3)
         spread_half(GROUPS + 1, 1)
         weigh_slots(SECOND_TURN + V_LAG + 1, OUT_SLOT - 1)
-        quantize_e(GROUPS + 1)
         spread_half(GROUPS + 2, 0)
+        quantize_e(GROUPS + 1)
         spread_half(GROUPS + 2, 1)
 
         for k in range(SLOTS - OUT_SLOT):
@@ -427,15 +427,16 @@ def tile_balanced_nonlocal_means_s12_kernel(
         spread(last, 0, P)
         spread(last, P, 2 * P)
         quantize_e(last, 0, P)
+        interleave(e_grp[last], e_bf[last], 3 * P, HALF, on_scalar)
         finish(2, False)
-        spread(last, 2 * P, HALF)
+        spread(last, 2 * P, 3 * P)
         quantize_e(last, P, 2 * P)
         finish(3, False)
         quantize_e(last, 2 * P, HALF)
         free = [next_bank() for k in range(4)]
         for k, g in ((4, 0), (4, 1), (4, 2), (5, 0), (5, 1), (4, 3)):
             average(k, g, free[k - TILES])
-        finish(4, True)
+        finish(4, False)
         average(5, 2)
         average(5, 3)
         finish(5, False)

@@ -107,6 +107,7 @@ def tile_balanced_nonlocal_means_s12_kernel(
             nc.sync.dma_start(out=x_raw[g][:], in_=x.rearrange("(g m b) f -> g m b f", g=GROUPS, b=4)[g])
 
         nc.gpsimd.memset(b_rows_first[:].bitcast(I32), 0)
+        nc.gpsimd.memset(b_rows_second[:].bitcast(I32), 0)
         nc.vector.memset(a_plane.bitcast(I32), 0)
         nc.vector.memset(gam_rows[:], 0.0)
 
@@ -117,8 +118,6 @@ def tile_balanced_nonlocal_means_s12_kernel(
         load_codes(a_codes[0], a_words, 0)
         load_rows(a_plane, a_scales, 0, M, (1, 2, 3))
         make_identity(nc, ident[:])
-        nc.gpsimd.memset(b_rows_second[:].bitcast(I32), 0)
-        nc.gpsimd.memset(b_rows_late[:].bitcast(I32), 0)
         nc.sync.dma_start(out=w_raw[:], in_=w.rearrange("(p j) c -> p j c", j=4))
         load_codes(a_codes[1], a_words, 2 * HALF)
         load_rows(b_rows_second, b_scales, PASS, 2 * PASS)
@@ -126,11 +125,6 @@ def tile_balanced_nonlocal_means_s12_kernel(
         load_x(0)
         load_x(1)
         load_codes(b_raw_late, b_words, 4 * PASS)
-        load_rows(b_rows_late, b_scales, 2 * PASS, N)
-        load_x(2)
-        load_x(3)
-        with nc.allow_non_contiguous_dma(reason="one rho value a pixel, onto the partition of its output row"):
-            nc.sync.dma_start(out=rho_raw[:, :, 0], in_=rho.rearrange("(k p) -> p k", p=P))
 
         def arrange(dst, src, words):
             nc.vector.tensor_copy(
@@ -263,10 +257,15 @@ def tile_balanced_nonlocal_means_s12_kernel(
             func=ACT.Ln,
         )
         gam_pairs = gam_rows[0:GROUPS, 0].bitcast(BF16).rearrange("g t (c e) -> g t c e", e=2)
-        nc.vector.tensor_copy(
-            out=gam_pairs[:, :, :, 0].rearrange("g t (q r) -> g t q r", r=8), in_=gam_raw[:].rearrange(by_place, t=4, r=8)
-        )
-        nc.vector.tensor_copy(out=gam_pairs[:, :, :, 1], in_=gam_raw[:].rearrange("g (m b) -> g b m", b=4))
+        for first in (0, 2):
+            quarters = slice(first, first + 2)
+            nc.vector.tensor_copy(
+                out=gam_pairs[:, quarters, :, 0].rearrange("g t (q r) -> g t q r", r=8),
+                in_=gam_raw[:].rearrange(by_place, t=4, r=8)[:, quarters],
+            )
+            nc.vector.tensor_copy(
+                out=gam_pairs[:, quarters, :, 1], in_=gam_raw[:].rearrange("g (m b) -> g b m", b=4)[:, quarters]
+            )
         gam_banks = []
         for k in range(2):
             bank = bank_tile("gam_t", [P, 4, P], 4 + k)
@@ -346,6 +345,12 @@ def tile_balanced_nonlocal_means_s12_kernel(
 
         weigh_slots(0, 3)
         interleave(w_grp, w_raw)
+        nc.vector.memset(b_rows_late[:].bitcast(I32), 0)
+        load_rows(b_rows_late, b_scales, 2 * PASS, N)
+        load_x(2)
+        load_x(3)
+        with nc.allow_non_contiguous_dma(reason="one rho value a pixel, onto the partition of its output row"):
+            nc.sync.dma_start(out=rho_raw[:, :, 0], in_=rho.rearrange("(k p) -> p k", p=P))
         arrange(b_plane_second, b_rows_second, 2)
         quantize(w_codes, w_plane, w_grp)
         arrange(b_codes_early[1], b_raw[1], 4)
@@ -427,8 +432,8 @@ def tile_balanced_nonlocal_means_s12_kernel(
         spread(last, 0, P)
         spread(last, P, 2 * P)
         quantize_e(last, 0, P)
-        interleave(e_grp[last], e_bf[last], 3 * P, HALF, on_scalar)
         finish(2, False)
+        interleave(e_grp[last], e_bf[last], 3 * P, HALF, on_scalar)
         spread(last, 2 * P, 3 * P)
         quantize_e(last, P, 2 * P)
         finish(3, False)
@@ -439,7 +444,7 @@ def tile_balanced_nonlocal_means_s12_kernel(
         finish(4, False)
         average(5, 2)
         average(5, 3)
-        finish(5, False)
+        finish(5, True)
         pieces = [(6, 0, 256, free[2]), (6, 256, C, free[3]), (7, 0, 256, 4), (7, 256, 384, 5), (7, 384, C, 6)]
         for n, (k, first, end, bank) in enumerate(pieces):
             for g in range(GROUPS):

import math
from contextlib import ExitStack

import concourse.mybir as mybir
from concourse.masks import make_identity

M, N, D, F, C = 1024, 2048, 1024, 512, 512
FLOPS = 2 * (M * N * D + N * F * C + M * N * C)

F32 = mybir.dt.float32
BF16 = mybir.dt.bfloat16
I32 = mybir.dt.int32
U32 = mybir.dt.uint32
U8 = mybir.dt.uint8
E4M3 = mybir.dt.float8_e4m3fn_x4
E2M1 = mybir.dt.float4_e2m1fn_x4
ALU = mybir.AluOpType
ACT = mybir.ActivationFunctionType

P = 128
PASS = 512
GROUPS = N // PASS
HALF = M // 2
DEPTH = D // PASS
TILES = HALF // P
STEPS = 2 * GROUPS
SLOTS = 4 * STEPS

FIRST_TURN, SECOND_TURN = 9, 20
V_LAG = 4
OUT_SLOT = 29


def tile_balanced_nonlocal_means_s12_kernel(
    tc, a_words, a_scales, b_words, b_scales, gamma, rho, x, w, out
):
    nc = tc.nc
    with ExitStack() as ctx:
        keep = ctx.enter_context(tc.tile_pool(name="keep", bufs=1))
        work = ctx.enter_context(tc.tile_pool(name="work", bufs=4))
        psum = ctx.enter_context(tc.psum_pool(name="psum", bufs=1))
        ctx.enter_context(tc.manual_schedule())

        def bank_tile(name, shape, bank):
            return psum.tile(shape, F32, name=name, tag="bank%d" % bank)

        def kept(name, shape, dtype):
            return keep.tile(shape, dtype, name=name, tag=name, align_bytes=64)

        def kept_plane(name, columns):
            return kept(name, [P, columns + 256], U8)[:, 128 : 128 + columns]

        a_codes = [kept("a_codes%d" % h, [P, DEPTH, 2 * HALF], U8) for h in range(2)]
        a_plane = kept_plane("a_plane", DEPTH * M).rearrange("p (d n) -> p d n", d=DEPTH)
        b_raw = [kept("b_raw%d" % g, [P, DEPTH, 2 * PASS], U8) for g in range(2)]
        b_raw_late = kept("b_raw_late", [P, DEPTH, 4 * PASS], U8)
        b_rows_first = kept("b_rows_first", [P, DEPTH, PASS], U8)
        b_rows_second = kept("b_rows_second", [P, DEPTH, PASS], U8)
        b_rows_late = kept("b_rows_late", [P, DEPTH, 2 * PASS], U8)
        b_codes_early = [kept("b_codes%d" % g, [P, DEPTH, 2 * PASS], U8) for g in range(2)]
        b_codes_late = kept("b_codes_late", [P, DEPTH, 4 * PASS], U8)
        b_codes = [tile[:] for tile in b_codes_early] + [b_codes_late[:, :, 2 * PASS * g : 2 * PASS * (g + 1)] for g in range(2)]
        b_plane_first = kept("b_plane_first", [P, DEPTH, PASS], U8)
        b_plane_second = kept("b_plane_second", [P, DEPTH, PASS], U8)
        b_plane_late = kept("b_plane_late", [P, DEPTH, 2 * PASS], U8)
        b_plane = [b_plane_first[:], b_plane_second[:]] + [b_plane_late[:, :, PASS * g : PASS * (g + 1)] for g in range(2)]
        x_raw = [kept("x_raw%d" % g, [P, 4, F], BF16) for g in range(GROUPS)]
        x_sorted = [kept("x_sorted%d" % g, [P, 4, F], BF16) for g in range(GROUPS)]
        x_grp = [kept("x_grp%d" % g, [P, PASS, 4], BF16) for g in range(GROUPS)]
        x_codes = [kept("x_codes%d" % g, [P, PASS], U32) for g in range(GROUPS)]
        x_plane = [kept("x_plane%d" % g, [P, PASS], U8) for g in range(GROUPS)]
        w_raw = kept("w_raw", [P, 4, C], BF16)
        w_grp = kept("w_grp", [P, C, 4], BF16)
        w_codes = kept("w_codes", [P, C], U32)
        w_plane = kept_plane("w_plane", C)
        v_grp = [kept("v_grp%d" % g, [P, C, 4], BF16) for g in range(GROUPS)]
        v_codes = [kept("v_codes%d" % g, [P, C], U32) for g in range(GROUPS)]
        v_plane = [kept_plane("v_plane%d" % g, C) for g in range(GROUPS)]
        e_codes = [kept("e_codes%d" % s, [P, HALF], U32) for s in range(STEPS)]
        e_plane = [kept("e_plane%d" % s, [P, HALF], U8) for s in range(STEPS)]
        gam_raw = kept("gam_raw", [GROUPS, PASS], BF16)
        mant = kept("mant", [GROUPS, PASS], BF16)
        gam_rows = kept("gam_rows", [P, 2, 4, P], F32)
        rho_raw = kept("rho_raw", [P, M // P, 2], BF16)
        gam_col = kept("gam_col", [P, 4 * GROUPS], F32)
        rho_col = kept("rho_col", [P, M // P], F32)
        expo = kept("expo", [P, 4 * GROUPS], I32)
        expo_ln = kept("expo_ln", [P, 4 * GROUPS], F32)
        ln_gam = kept("ln_gam", [P, 4 * GROUPS], F32)
        half_sign = kept("half_sign", [P, 4 * GROUPS], F32)
        ident = kept("ident", [P, P], F32)

        def load_codes(tile, words, first):
            nc.sync.dma_start(
                out=tile[:].bitcast(I32),
                in_=words.rearrange("d p n -> p d n")[:, :, first : first + tile.shape[2]].bitcast(I32),
            )

        def load_rows(plane, rows, first, last, which=range(4)):
            for r in which:
                nc.sync.dma_start(
                    out=plane[r:P:32, :, :].bitcast(I32),
                    in_=rows[:, r:16:4, first:last].rearrange("d q n -> q d n").bitcast(I32),
                )

        def load_x(g):
            nc.sync.dma_start(out=x_raw[g][:], in_=x.rearrange("(g m b) f -> g m b f", g=GROUPS, b=4)[g])

        nc.gpsimd.memset(b_rows_first[:].bitcast(I32), 0)
        nc.gpsimd.memset(b_rows_second[:].bitcast(I32), 0)
        nc.vector.memset(a_plane.bitcast(I32), 0)
        nc.vector.memset(gam_rows[:], 0.0)

        nc.sync.dma_start(out=gam_raw[:], in_=gamma.rearrange("(g n) -> g n", g=GROUPS))
        load_codes(b_raw[0], b_words, 0)
        load_rows(b_rows_first, b_scales, 0, PASS)
        load_rows(a_plane, a_scales, 0, M, (0,))
        load_codes(a_codes[0], a_words, 0)
        load_rows(a_plane, a_scales, 0, M, (1, 2, 3))
        make_identity(nc, ident[:])
        nc.sync.dma_start(out=w_raw[:], in_=w.rearrange("(p j) c -> p j c", j=4))
        load_codes(a_codes[1], a_words, 2 * HALF)
        load_rows(b_rows_second, b_scales, PASS, 2 * PASS)
        load_codes(b_raw[1], b_words, 2 * PASS)
        load_x(0)
        load_x(1)
        load_codes(b_raw_late, b_words, 4 * PASS)

        def arrange(dst, src, words):
            nc.vector.tensor_copy(
                out=dst[:].bitcast(I32).rearrange("p d (g t q w) -> p (d g) t q w", t=4, q=16, w=words),
                in_=src[:].bitcast(I32).rearrange("p d (g q t w) -> p (d g) t q w", t=4, q=16, w=words),
            )

        def sort_x(g):
            for row in range(4):
                nc.vector.tensor_scalar(
                    out=x_sorted[g][:, row, :].rearrange("m (u p e) -> m u p e", u=2, e=2),
                    in0=x_raw[g][:, row, :].rearrange("m (p u e) -> m u p e", u=2, e=2),
                    scalar1=half_sign[:, 4 * g + row : 4 * g + row + 1],
                    scalar2=2.0,
                    op0=ALU.mult,
                    op1=ALU.mult,
                )

        x_banks = {}

        def turn_x(g, banks):
            for k in range(2):
                bank = bank_tile("x_t", [P, 4, P], banks[k])
                x_banks[g, k] = bank
                for row in range(2):
                    for u in range(2):
                        pairs = x_sorted[g][:, 2 * k + row, :].bitcast(F32)[:, P * u : P * (u + 1)]
                        nc.tensor.transpose(bank[:, 2 * row + u, :], pairs, ident[:])

        def take_x(g, k, copy):
            pairs = x_grp[g][:].rearrange("p c j -> p (c j)").bitcast(F32)
            copy(
                out=pairs.rearrange("p (t q r e) -> p t q r e", t=4, r=2, e=8)[:, :, :, :, 4 * k : 4 * k + 4],
                in_=x_banks[g, k][:].rearrange("p e (q t r) -> p t q r e", t=4, r=2),
            )

        def quantize(codes, plane, grouped, first=0, last=PASS):
            nc.vector.quantize_mx(
                out=codes[:, first:last].bitcast(E4M3),
                scales=plane[:, first:last],
                in_=grouped[:, first:last, :].rearrange("p c t -> p (c t)"),
            )

        def interleave(grouped, rows, first=0, last=PASS, copy=nc.vector.tensor_copy):
            copy(
                out=grouped[:, first:last, :].rearrange("p (c i) t -> p c t i", i=4),
                in_=rows[:, :, first:last].rearrange("p t (c i) -> p c t i", i=4),
            )

        e_bf = {}
        e_grp = {}

        def weigh(s, t, bank):
            h, g = divmod(s, GROUPS)
            gram = bank_tile("gram", [P, HALF], bank)
            if t == 0:
                e_bf[s] = work.tile([P, 4, HALF], BF16, name="e_bf", tag="e_bf", bufs=6, align_bytes=64)
            for d in range(DEPTH):
                nc.tensor.matmul_mx(
                    out=gram[:],
                    lhsT=b_codes[g][:, d, 2 * P * t : 2 * P * (t + 1)].bitcast(E2M1),
                    lhsT_scale=b_plane[g][:, d, P * t : P * (t + 1)],
                    rhs=a_codes[h][:, d, :].bitcast(E2M1),
                    rhs_scale=a_plane[:, d, HALF * h : HALF * (h + 1)],
                    start=(d == 0),
                    stop=(d == DEPTH - 1),
                )
            nc.scalar.activation(
                out=e_bf[s][:, t, :], in_=gram[:], func=ACT.Exp, bias=ln_gam[:, 4 * g + t : 4 * g + t + 1]
            )

        v_banks = {}

        def project(g, quarter, bank):
            val = bank_tile("val", [P, 4, P], bank)
            v_banks[g, quarter] = val
            cols = slice(P * quarter, P * (quarter + 1))
            for t in range(4):
                nc.tensor.matmul_mx(
                    out=val[:, t, :],
                    lhsT=x_codes[g][:, P * t : P * (t + 1)].bitcast(E4M3),
                    lhsT_scale=x_plane[g][:, P * t : P * (t + 1)],
                    rhs=w_codes[:, cols].bitcast(E4M3),
                    rhs_scale=w_plane[:, cols],
                    start=True,
                    stop=True,
                )

        def take_v(g, quarter, copy):
            cols = slice(P * quarter, P * (quarter + 1))
            copy(out=v_grp[g][:, cols, :], in_=v_banks[g, quarter][:].rearrange("p t c -> p c t"))

        o_bank = {}

        def average(k, g, bank=None, first=0, last=C):
            h, i = divmod(k, TILES)
            if g == 0:
                o_bank[k, first] = bank_tile("avg", [P, last - first], bank)
            s = h * GROUPS + g
            nc.tensor.matmul_mx(
                out=o_bank[k, first][:],
                lhsT=e_codes[s][:, P * i : P * (i + 1)].bitcast(E4M3),
                lhsT_scale=e_plane[s][:, P * i : P * (i + 1)],
                rhs=v_codes[g][:, first:last].bitcast(E4M3),
                rhs_scale=v_plane[g][:, first:last],
                start=(g == 0),
                stop=(g == GROUPS - 1),
            )

        def finish(k, on_vector, first=0, last=C):
            res = work.tile([P, last - first], F32, name="res", tag="res", bufs=2 * TILES)
            if on_vector:
                nc.vector.tensor_scalar_mul(out=res[:], in0=o_bank[k, first][:], scalar1=rho_col[:, k : k + 1])
            else:
                nc.scalar.activation(out=res[:], in_=o_bank[k, first][:], func=ACT.Copy, scale=rho_col[:, k : k + 1])
            nc.sync.dma_start(out=out[P * k : P * (k + 1), first:last], in_=res[:])

        nc.vector.tensor_scalar(
            out=mant[:].bitcast(I32),
            in0=gam_raw[:].bitcast(I32),
            scalar1=0x007F007F,
            scalar2=0x3F803F80,
            op0=ALU.bitwise_and,
            op1=ALU.bitwise_or,
        )
        by_place = "g (q t r) -> g t q r"
        nc.scalar.activation(
            out=gam_rows[0:GROUPS, 1].rearrange("g t (q r) -> g t q r", r=8),
            in_=mant[:].rearrange(by_place, t=4, r=8),
            func=ACT.Ln,
        )
        gam_pairs = gam_rows[0:GROUPS, 0].bitcast(BF16).rearrange("g t (c e) -> g t c e", e=2)
        for first in (0, 2):
            quarters = slice(first, first + 2)
            nc.vector.tensor_copy(
                out=gam_pairs[:, quarters, :, 0].rearrange("g t (q r) -> g t q r", r=8),
                in_=gam_raw[:].rearrange(by_place, t=4, r=8)[:, quarters],
            )
            nc.vector.tensor_copy(
                out=gam_pairs[:, quarters, :, 1], in_=gam_raw[:].rearrange("g (m b) -> g b m", b=4)[:, quarters]
            )
        gam_banks = []
        for k in range(2):
            bank = bank_tile("gam_t", [P, 4, P], 4 + k)
            for t in range(4):
                nc.tensor.transpose(bank[:, t, :], gam_rows[:, k, t, :], ident[:])
            gam_banks.append(bank[:, :, 0:GROUPS])
        pair_cols = gam_banks[0].bitcast(BF16).rearrange("p t (g e) -> p g t e", e=2)
        gam_cols = [pair_cols[:, :, :, 0], pair_cols[:, :, :, 1], gam_banks[1].rearrange("p t g -> p g t")]

        def by_group(tile):
            return tile[:].rearrange("p (g t) -> p g t", t=4)

        arrange(b_codes_early[0], b_raw[0], 4)
        arrange(b_plane_first, b_rows_first, 2)
        nc.vector.tensor_copy(out=by_group(gam_col), in_=gam_cols[0])
        nc.vector.tensor_scalar(
            out=expo[:],
            in0=gam_col[:].bitcast(I32),
            scalar1=23,
            scalar2=0xFF,
            op0=ALU.logical_shift_right,
            op1=ALU.bitwise_and,
        )
        nc.vector.tensor_scalar(
            out=expo_ln[:], in0=expo[:], scalar1=-127.0, scalar2=math.log(2.0), op0=ALU.add, op1=ALU.mult
        )
        nc.vector.tensor_scalar(
            out=by_group(half_sign), in0=gam_cols[1], scalar1=0.0, scalar2=0.5, op0=ALU.is_ge, op1=ALU.subtract
        )
        nc.vector.tensor_tensor(out=by_group(ln_gam), in0=gam_cols[2], in1=by_group(expo_ln), op=ALU.add)

        on_scalar, on_vector = nc.scalar.copy, nc.vector.tensor_copy
        order = [0, GROUPS, 1, GROUPS + 1, 2, 3, GROUPS + 2, GROUPS + 3]
        handed_out = []
        early_passes = [(k, g) for g in range(2) for k in range(TILES)]

        def next_bank():
            handed_out.append(len(handed_out) % 4)
            return handed_out[-1]

        def weigh_slots(first, last):
            for slot in range(first, last + 1):
                weigh(order[slot // 4], slot % 4, next_bank())

        def spread(s, first, last):
            if first == 0:
                e_grp[s] = work.tile([P, HALF, 4], BF16, name="e_grp", tag="e_grp", align_bytes=64)
            interleave(e_grp[s], e_bf[s], first, last)

        def spread_half(s, half):
            spread(s, half * HALF // 2, (half + 1) * HALF // 2)

        def quantize_e(s, first=0, last=HALF):
            quantize(e_codes[s], e_plane[s], e_grp[s], first, last)

        def quantize_x(g):
            quantize(x_codes[g], x_plane[g], x_grp[g])

        def quantize_v(g):
            quantize(v_codes[g], v_plane[g], v_grp[g])

        def early_pass():
            k, g = early_passes.pop(0)
            average(k, g, 4 + k)

        def project_early(g, vector_quarters=(0, 2)):
            for quarter in range(4):
                project(g, quarter, 4 + quarter)
                take_v(g, quarter, on_vector if quarter in vector_quarters else on_scalar)

        def project_late(g, vector_quarter, followed):
            for quarter in range(4):
                project(g, quarter, next_bank())
                take_v(g, quarter, on_vector if quarter == vector_quarter else on_scalar)
                if quarter in followed:
                    early_pass()

        weigh_slots(0, 3)
        interleave(w_grp, w_raw)
        nc.vector.memset(b_rows_late[:].bitcast(I32), 0)
        load_rows(b_rows_late, b_scales, 2 * PASS, N)
        load_x(2)
        load_x(3)
        with nc.allow_non_contiguous_dma(reason="one rho value a pixel, onto the partition of its output row"):
            nc.sync.dma_start(out=rho_raw[:, :, 0], in_=rho.rearrange("(k p) -> p k", p=P))
        arrange(b_plane_second, b_rows_second, 2)
        quantize(w_codes, w_plane, w_grp)
        arrange(b_codes_early[1], b_raw[1], 4)
        spread_half(0, 0)
        spread_half(0, 1)
        sort_x(0)
        sort_x(1)
        weigh_slots(4, FIRST_TURN)
        spread_half(GROUPS, 0)
        quantize_e(0)
        turn_x(0, (6, 7))
        turn_x(1, (4, 5))
        for g in (0, 1):
            for k in (0, 1):
                take_x(g, k, on_scalar)

        spread_half(GROUPS, 1)
        quantize_x(0)
        arrange(b_codes_late, b_raw_late, 4)
        quantize_x(1)
        arrange(b_plane_late, b_rows_late, 2)
        weigh_slots(FIRST_TURN + 1, FIRST_TURN + V_LAG)
        project_early(0, (0,))

        spread_half(1, 0)
        sort_x(2)
        spread_half(1, 1)
        quantize_v(0)
        sort_x(3)
        weigh_slots(FIRST_TURN + V_LAG + 1, FIRST_TURN + 2 * V_LAG)
        project_early(1)
        quantize_e(1)
        quantize_v(1)
        weigh_slots(FIRST_TURN + 2 * V_LAG + 1, SECOND_TURN)

        turn_x(2, (4, 5))
        turn_x(3, (6, 7))
        for k in (0, 1):
            take_x(2, k, on_vector)
        for k in (0, 1):
            take_x(3, k, on_scalar)
        nc.scalar.copy(out=rho_col[:], in_=rho_raw[:, :, 0])
        spread_half(2, 0)
        quantize_x(2)
        spread_half(2, 1)
        quantize_x(3)

        weigh_slots(SECOND_TURN + 1, SECOND_TURN + 1)
        for slot in range(SECOND_TURN + 2, SECOND_TURN + V_LAG + 1):
            weigh_slots(slot, slot)
            early_pass()
        quantize_e(2)
        project_late(2, None, (0, 1, 3))
        spread_half(3, 0)
        quantize_e(GROUPS)
        spread_half(3, 1)
        project_late(3, 1, (0, 2))
        quantize_v(2)
        quantize_e(3)
        spread_half(GROUPS + 1, 0)
        quantize_v(3)
        spread_half(GROUPS + 1, 1)
        weigh_slots(SECOND_TURN + V_LAG + 1, OUT_SLOT - 1)
        spread_half(GROUPS + 2, 0)
        quantize_e(GROUPS + 1)
        spread_half(GROUPS + 2, 1)

        for k in range(SLOTS - OUT_SLOT):
            weigh_slots(OUT_SLOT + k, OUT_SLOT + k)
            average(k, 2)
            average(k, 3)
            if k < 2:
                finish(k, k == 1)
        quantize_e(GROUPS + 2)
        average(3, 2)
        average(3, 3)

        last = STEPS - 1
        spread(last, 0, P)
        spread(last, P, 2 * P)
        quantize_e(last, 0, P)
        finish(2, False)
        interleave(e_grp[last], e_bf[last], 3 * P, HALF, on_scalar)
        spread(last, 2 * P, 3 * P)
        quantize_e(last, P, 2 * P)
        finish(3, False)
        quantize_e(last, 2 * P, HALF)
        free = [next_bank() for k in range(4)]
        for k, g in ((4, 0), (4, 1), (4, 2), (5, 0), (5, 1), (4, 3)):
            average(k, g, free[k - TILES])
        finish(4, False)
        average(5, 2)
        average(5, 3)
        finish(5, True)
        pieces = [(6, 0, 256, free[2]), (6, 256, C, free[3]), (7, 0, 256, 4), (7, 256, 384, 5), (7, 384, C, 6)]
        for n, (k, first, end, bank) in enumerate(pieces):
            for g in range(GROUPS):
                average(k, g, bank, first, end)
            finish(k, n % 2 == 0, first, end)
